import numpy as np, ml_dtypes
CORES = [40,41,42,43,44,45,46,47]
N = 8
import mx_ref
BF = ml_dtypes.bfloat16
def gentries(a):
    return np.ascontiguousarray(a.reshape(8, 16, -1).transpose(0, 2, 1)).reshape(8, -1)
def gtable(e):
    e = np.asarray(e); return np.ascontiguousarray(e.reshape(8, -1, 16).transpose(0, 2, 1)).reshape(128, -1).astype(np.int32)
def gcols(t, e):
    v = np.concatenate([t.reshape(8, 16, -1, 4), np.zeros((8, 16, 1, 4), BF)], axis=2)
    return np.ascontiguousarray(np.stack([v[g][:, e[g]] for g in range(8)])).reshape(128, -1)
def tile(rs):
    return np.stack(rs, axis=2).reshape(128, -1).astype(BF)
def pick(q, e):
    c = np.concatenate([q[0].reshape(128, -1, 4), np.zeros((128, 1, 4), np.uint8)], axis=1); s = np.concatenate([q[1], np.ones((16, 1), np.uint8)], axis=1)
    return (np.ascontiguousarray(c[:, e].reshape(128, -1)), np.ascontiguousarray(s[:, e]))
def join(*qs):
    return (np.concatenate([q[0] for q in qs], axis=1), np.concatenate([q[1] for q in qs], axis=1))
def put(q, e, v):
    c, s = q[0].reshape(128, -1, 4).copy(), q[1].copy(); c[:, e] = v[0].reshape(128, -1, 4); s[:, e] = v[1]
    return (c.reshape(128, -1), s)
def pk(c, s):
    return (np.ascontiguousarray(c), mx_ref.live(s))
def emit(q):
    return q[0], q[1]
def packed(v, rng):
    q = [mx_ref.quantize(np.ascontiguousarray(v[r])) for r in range(N)]
    return np.stack([a for a, b in q]), np.stack([mx_ref.plane(b, rng) for a, b in q])
def values_of_codes():
    e, c = np.zeros((128, 128, 4), np.float32), np.zeros((128, 2, 4), np.uint8)
    e[np.arange(128), np.arange(128), 0] = 1
    c[:127, :, 0] = np.arange(256).reshape(2, 128).T[:127]
    return mx_ref.matmul(mx_ref.quantize(e.reshape(128, 512).astype(BF)), (c.reshape(128, 8), np.full((16, 2), 127, np.uint8))).T.reshape(-1).astype(np.float64)
CODE_VALUE, SCALE_VALUE = values_of_codes(), 2.0 ** (np.arange(256) - 127.0)
def decode(q):
    return (CODE_VALUE[q[0]].reshape(16, 8, -1, 4) * SCALE_VALUE[q[1]][:, None, :, None] + 0.0).reshape(128, -1).astype(np.float32)
def f(rng, *shape):
    return mx_ref.flush((rng.standard_normal(shape, dtype=np.float32) * np.exp2(rng.integers(-2, 3, shape[:-1] + (1,)))).astype(BF))
def wide(rng, *shape, cols=0):
    v = rng.standard_normal(shape, dtype=np.float32) * np.exp2(rng.integers(-12, 13, shape)).astype(np.float32)
    if cols: v *= np.repeat(np.exp2(rng.integers(-cols, cols + 1, shape[:-2] + (1, shape[-1] // 4))) * (rng.random(shape[:-2] + (1, shape[-1] // 4)) > 0.0625), 4, axis=-1).astype(np.float32)
    return mx_ref.flush(v.astype(BF))
C, L, M, R = 384, 48, 192, 3
STEP = [1, 2, 4]
place = np.arange(C)
def at(a, e):
    return np.take_along_axis(a, e, axis=1)
def big(v):
    v = v.astype(np.float32)
    v[np.abs(v) < np.float32(2.0 ** -16)] = 0
    return v.astype(BF)
def numbers_of(rng):
    return {"x": big(f(rng, N, 128, 4 * C)), "u": np.array(f(rng, N, 128, 512)), "v": np.array(f(rng, N, 128, 512))}
def layers(rng):
    return big(f(rng, N, 128, 2048)).reshape(N, 8, 16, 4, 8, 16, 4)
def weights(rng, w):
    c, p = packed(np.ascontiguousarray(w).reshape(N, 128, 2048), rng)
    return {"wc": c, "ws": p}
def twins(rng):
    o = np.argsort(rng.random((N, 8, C)), axis=2)
    e = np.zeros((N, 8, C), int)
    np.put_along_axis(e, o[:, :, :M], o[:, :, M:], axis=2)
    np.put_along_axis(e, o[:, :, M:], o[:, :, :M], axis=2)
    return e
def listed(e):
    return {"tw": np.stack([gtable(e[r]) for r in range(N)])}
def signs(rng):
    return np.stack([rng.permutation(8) % 2 * 2.0 - 1.0 for r in range(N)])
def setup_inputs(rng):
    return {**numbers_of(rng), **weights(rng, layers(rng)), **listed(twins(rng))}
def setup_inputs_ties(rng):
    d = numbers_of(rng)
    e = rng.permutation(N)
    x = d["x"].reshape(N, 8, 16, C, 4)
    for r in range(N):
        k = np.zeros(C, int) if r == e[0] else rng.permutation(C) % 3
        a = x[r][:, :8, :3].copy()
        a[:, :, 2] = 0
        x[r][:, :8] = a[:, :, k]
    x[e[1]] = 0
    u = d["u"].reshape(N, 8, 16, 8, 16, 4)
    k = u.copy()
    u[:, :, :, :, 0] = 0
    for g in range(8): u[:, g, :8, g, 0] = k[:, g, :8, g, 0]
    w = layers(rng)
    w[:, :, :, :, :, :8] = 0
    return {"x": x.reshape(N, 128, 4 * C), "u": u.reshape(N, 128, 512), "v": d["v"], **weights(rng, w), **listed(twins(rng))}
def setup_inputs_near(rng):
    d = numbers_of(rng)
    x = np.zeros((N, 8, 16, C, 4), np.float32)
    u = d["u"].reshape(N, 128, 128, 4)
    u[:, :, ::16] = 0
    o, e = rng.permutation(N) % 4, twins(rng)
    n = np.arange(M)
    for r in range(N):
        size = 1.0 if o[r] < 2 else 2.0 ** -4
        k = 1.0 if o[r] == 0 else 2.0 ** -30
        kind = rng.permutation(8)
        for g in range(8):
            low = np.flatnonzero(place < e[r, g])
            high = e[r, g][low]
            h, c = 16 * g, 1.0 - 2.0 * (kind[g] % 2)
            u[r, h, h, 0] = k
            u[r, h + 8:h + 12, h] = k
            s, unit = np.zeros(C, int), 2.0 ** -23 * size
            if kind[g] < 4:
                i = (n + rng.integers(0, (M - L) // 2 + 1)) % M
                upper = i // (M // 2)
                more = (M - i) // 2 + 1 if o[r] < 2 else M // 2 - i % (M // 2) + 1 - upper
                s[low] = rng.integers(0, 255 - M // 2, M)
                s[high] = s[low] + more
                if o[r] < 2:
                    u[r, h, h, 0] = k * 2.0 ** 20
                    x[r, g, 0, :, 0] = c * 2.0 ** -20
                    j = int(np.argmax(more))
                    if kind[g] < 2: x[r, g, 0, high[j] if c > 0 else low[j], 0] *= np.float32(2.0 ** 50)
                else:
                    x[r, g, 0, :, 0] = 8 * 2.0 ** -30
                    x[r, g, 0, high[upper == 0], 0] = 9 * 2.0 ** -30
            elif o[r] < 2:
                great, small = (high, low) if c > 0 else (low, high)
                third = 3 * n // M
                s[small] = 512 * (2 * int(rng.integers(17, 32)) - (third == 0)) + 255 * (third != 1)
                x[r, g, 0, great, 0] = 512 * c
                x[r, g, 0, small, 0] = 0.5 * c
                unit = 2.0 ** -24 * c
            else:
                m = np.where(n < M // 2, 10, 9) * 2.0 ** -32
                x[r, g, :2, :, 0] = 8 * 2.0 ** -32
                x[r, g, 0, high, 0] = m
                x[r, g, 1, low, 0] = m
                u[r, h, h, 0] = 9 * 2.0 ** -33
                u[r, h + 1, h, 0] = 2.0 ** -30
            z = ((s[:, None] >> np.arange(16)) & 1) * np.exp2(np.arange(16.0)) * unit + 0.0
            for i in range(4): x[r, g, 8 + i] = z[:, 4 * i:4 * i + 4]
        x[r, :, 12:] = rng.integers(4, 8, (8, 4, C, 4)) * 2.0 ** -20 * size
    w = layers(rng)
    w[:, :, :12] = 0
    w[:, :, :, :, :, :12] = 0
    return {"x": x.reshape(N, 128, 4 * C).astype(BF), "u": u.reshape(N, 128, 512), "v": d["v"], **weights(rng, w), **listed(e)}
def setup_inputs_arcs(rng):
    d = numbers_of(rng)
    x = d["x"].astype(np.float32).reshape(N, 8, 16, C, 4)
    u = d["u"].reshape(N, 128, 128, 4)
    u[:, :, ::16] = 0
    size = np.where(rng.permutation(N) < N // 2, 2.0 ** -30, 1.0).astype(np.float32).astype(BF)
    e = np.zeros((N, 8, C), int)
    for r in range(N):
        k, m, n = rng.permutation(8), rng.permutation(8), rng.permutation(8)
        for g in range(8):
            ways = [place, place[::-1], np.argsort(place % 2, kind="stable"), np.argsort(-(place % 2), kind="stable"), np.roll(place, M // 2), np.roll(place, int(rng.integers(1, C))), rng.permutation(C), rng.permutation(C)]
            low = np.sort(ways[k[g]][:M])
            high = np.setdiff1d(place, low)
            if m[g] % 3 == 1: high = high[::-1]
            if m[g] % 3 == 2: high = rng.permutation(high)
            more = [np.arange(1, M + 1), np.arange(M, 0, -1), np.ones(M, int), rng.permutation(M) + 1][n[g] % 4]
            key = np.zeros(C, int)
            key[low] = rng.integers(0, 256, M)
            key[high] = key[low] + more
            z = ((key[:, None] >> np.arange(12)) & 1) * np.exp2(np.arange(12.0))
            for i in range(3): x[r, g, 8 + i] = z[:, 4 * i:4 * i + 4]
            e[r, g, low] = high
            e[r, g, high] = low
        for h in range(0, 128, 16): u[r, h + 8:h + 11, h] = size[r]
    w = layers(rng)
    w[:, :, 8:11] = 0
    w[:, :, :, :, :, 8:11] = 0
    return {"x": x.reshape(N, 128, 4 * C).astype(BF), "u": u.reshape(N, 128, 512), "v": d["v"], **weights(rng, w), **listed(e)}
def setup_inputs_huge(rng):
    d = numbers_of(rng)
    e = twins(rng)
    c = np.ones((N, C))
    x = 0.7 + 0.2 * rng.random((N, 128, C, 4))
    a = 1 - 0.1 * rng.random((N, 128, 8, 4))
    for r in rng.permutation(N)[:N // 2]:
        x[r] = 0.9375 - 0.1 * rng.random((128, C, 4)) ** 4
        a[r] = 1 - 0.025 * rng.random((128, 8, 4))
        a[r, :, :, 0] = 1
        c[r] = rng.permutation(C) % 2 * 2.0 - 1.0
        for g in range(8):
            i, j = rng.permutation(np.flatnonzero(c[r] > 0)), np.flatnonzero(c[r] < 0)
            e[r, g, i] = j
            e[r, g, j] = i
    x = 2.0 ** 30 * x * c[:, None, :, None]
    u = d["u"].reshape(N, 128, 128, 4)
    a = 2.0 ** 30 * a * signs(rng)[:, None, :, None]
    u[:, :, ::16] = a.astype(np.float32).astype(BF)
    w = np.zeros((N, 128, 4, 128, 4), np.float32)
    i = np.arange(128)
    for b in range(4): w[:, i, b, i, b] = -0.25
    return {"x": x.astype(np.float32).reshape(N, 128, 4 * C).astype(BF), "u": u.reshape(N, 128, 512), "v": d["v"], **weights(rng, w.astype(BF)), **listed(e)}
def setup_inputs_spread(rng):
    d = setup_inputs(rng)
    d["x"] = big(wide(rng, N, 128, 4 * C, cols=6))
    return d
def check_inputs(d):
    b = []
    for k in ("x", "u", "v"):
        a = np.abs(d[k].astype(np.float32))
        if not (np.isfinite(a).all() and ((a == 0) | (a >= 2.0 ** -30) & (a <= 2.0 ** 30)).all()): b.append("a value of " + k)
    none, least, most = [emit(mx_ref.quantize(np.full((128, 16), k, np.float32).astype(BF)))[1][0, 0] for k in (0.0, 2.0 ** -30, 2.0 ** 30)]
    for r in range(N):
        if ((d["wc"][r] == 0x7F) | (d["wc"][r] == 0xFF)).any(): b.append("wc: a code that is no number")
        s = mx_ref.live(d["ws"][r])
        if ((s != none) & ((s < least) | (s > most))).any(): b.append("ws: a scale out of range")
        e = gentries(d["tw"][r])
        if ((e < 0) | (e >= C)).any(): b.append("tw: a twin out of range")
        elif (e == place).any() or (at(e, e) != place).any(): b.append("tw: places that aren't each other's twins")
    return b
def reference(x, u, v, wc, ws, tw):
    qu = [mx_ref.quantize(u[r]) for r in range(N)]
    lay = [pk(wc[r], ws[r]) for r in range(N)]
    now = [x[r] for r in range(N)]
    twin = [gentries(tw[r]) for r in range(N)]
    for t in range(R):
        kept, sent, named = [], [], []
        for r in range(N):
            e = twin[r]
            s = mx_ref.matmul(qu[r], mx_ref.quantize(now[r]))[::16] + np.float32(0.0)
            o = np.argsort(~((s < at(s, e)) | (s == at(s, e)) & (place > e)), axis=1, kind="stable")[:, :M]
            a = (np.stack([np.searchsorted(o[g], place, "right") for g in range(8)]) - 1) % M
            over = at(e, o)
            z = ((gcols(now[r], np.roll(o, 1, axis=1)).astype(np.float32) + gcols(now[r], at(o, at(a, over))).astype(np.float32)) * np.float32(0.5)).astype(BF)
            q = mx_ref.quantize(z)
            h = tile([mx_ref.matmul(pick(lay[r], np.arange(128 * b, 128 * b + 128)), q) * np.float32(0.03125) for b in range(4)])
            new = (now[r].astype(np.float32) + gcols(h, a).astype(np.float32)).astype(BF)
            weak = np.argsort(at(s, over) - at(s, o), axis=1, kind="stable")[:, :L]
            gone = np.zeros((8, C), bool)
            np.put_along_axis(gone, np.concatenate([at(o, weak), at(over, weak)], axis=1), True, axis=1)
            i = np.argsort(gone, axis=1, kind="stable")
            named.append(at(np.argsort(i, axis=1), at(e, i)))
            kept.append(gcols(new, i[:, :C - 2 * L]))
            sent.append(gcols(decode(mx_ref.quantize(new)).astype(BF), i[:, C - 2 * L:]))
        for r in range(N):
            p = (r - STEP[t]) % N
            now[r] = np.concatenate([kept[r], sent[p]], axis=1)
            twin[r] = np.concatenate([named[r][:, :C - 2 * L], named[p][:, C - 2 * L:]], axis=1)
    y, ot = np.zeros((N, 128, C), np.float32), np.zeros((N, 8, C), np.float32)
    oc, osc = np.zeros((N, 128, 4 * C), np.uint8), np.zeros((N, 16, C), np.uint8)
    for r in range(N):
        q = mx_ref.quantize(now[r])
        y[r] = mx_ref.matmul(mx_ref.quantize(v[r]), q)
        ot[r] = twin[r]
        oc[r], osc[r] = emit(q)
    return {"y": y, "ot": ot, "oc": oc, "osc": osc}

@@ -1,0 +1,499 @@
+import numpy as np
+from concourse.bass import DstId, RemoteDMATransfer
+from concourse.mybir import dt, AluOpType, ActivationFunctionType
+
+C, M, NL, NS, R = 384, 192, 96, 288, 3
+STEP = [1, 2, 4]
+PL = 208
+BIG = 2.0 ** 80
+EPS = 2.0 ** -110
+OPT = {"cy": 1.04, "ga": 1.62, "dep": 75.0, "sfix": 40.0, "dma": 2000.0, "rem": 2500.0, "issue": 600.0,
+       "tries": 5000, "tied": 0.7, "pm": 0.015, "whi": 6.0, "pen0": 2.0, "seed": 0, "inorder": True}
+
+
+def sb(n, d):
+    return ("sbuf", [128, n], d)
+
+
+F, B, I, U16, X4, U8 = "float32", "bfloat16", "int32", "uint16", "float8_e4m3fn_x4", "uint8"
+SCRATCH = {
+    "ps": ("psum", [128, 4096], F),
+    "xi": sb(4 * C, B), "ut": sb(512, B), "vt": sb(512, B), "twi": sb(24, I),
+    "qx": sb(C, X4), "sx": sb(C, U8), "qb": sb(128, X4), "sq": sb(128, U8),
+    "qu": sb(128, X4), "su": sb(128, U8), "qu2": sb(128, X4), "su2": sb(128, U8),
+    "qv": sb(128, X4), "sv": sb(128, U8), "wq": sb(512, X4), "wp": sb(512, U8),
+    "ones": sb(512, B), "et": sb(2048, B), "qe": sb(512, X4), "se": sb(512, U8),
+    "bo1": sb(512, B), "bo2": sb(512, B), "qo": sb(128, X4), "so": sb(128, U8),
+    "zero": sb(1024, B), "qj": sb(256, X4),
+    "uli": sb(8, I), "ul": sb(8, U16), "pi": sb(1, I), "ri": sb(1, I), "rf": sb(1, F), "r97": sb(1, F), "kb": sb(2, F), "kq": sb(2, F),
+    "io1": sb(C, F), "iob": sb(C, B), "i16": sb(C, B), "cm": sb(C, B), "cm1": sb(C, B), "cm2": sb(C, B), "keep": sb(C, B),
+    "tie": sb(16, F), "iw": sb(24, F), "ths": sb(18, F), "thl": sb(6, F), "hf": sb(24, F), "hw": sb(24, U16),
+    "sr": sb(C, F), "st": sb(C, F), "d": sb(C, F), "un": sb(C, B), "cum": sb(C, B),
+    "twf": sb(24, U16), "arr": sb(16 * R, U16), "snd": sb(16, U16),
+    "junk": sb(4 * C, B), "acc": sb(4, F), "bw": sb(8, U16), "mo": sb(C, B), "mg": sb(C, B), "mq": sb(C, B),
+    "po": sb(C + 8, B), "pg": sb(C + 8, B), "pq": sb(C + 8, B),
+    "ow": sb(16, U16), "ow4": sb(64, U16), "lw": sb(16, U16), "qw": sb(32, U16),
+    "cap": sb(C, B), "cap2": sb(C, B), "capg": sb(C, B), "uf": sb(24, F), "uw": sb(24, U16),
+    "cw": sb(24, U16), "gw": sb(24, U16), "sw": sb(24, U16),
+    "dm": sb(M, F), "dh": sb(M, F), "dr": sb(M, F), "sg": sb(512, B),
+    "fl": sb(16 * M, B), "qf": sb(4 * M, X4), "sf": sb(4 * M, U8),
+    "ct": sb(C, B), "ctm": sb(M, B), "cth": sb(M, B), "ctw": sb(12, U16),
+    "xo": sb(4 * PL, B), "xa": sb(4 * PL, B), "z": sb(4 * M, B), "qz": sb(M, X4), "sz": sb(M, U8), "hx": sb(4 * PL, B),
+    "lv": sb(PL, B), "g1": sb(C, B), "g2": sb(C, B), "g2p": sb(C, B), "gn": sb(C, B), "ncs": sb(C, B), "e": sb(4 * C, B),
+    "sl": sb(512, B), "qs": sb(128, X4), "ss": sb(C, U8), "lq": sb(R * 224, X4), "ls": sb(R * 512, U8),
+    "t1": sb(C, B), "t2": sb(C, B), "nm": sb(C, B), "nh": sb(C, B),
+    "yo": sb(C, F), "otr": sb(C, F),
+}
+POOL = {"v": 56, "s": 36, "t": 10, "g": 10}
+NDMA = 24
+SEMAPHORES = (["%s%d" % (q, i) for q in POOL for i in range(POOL[q])] + ["m%d" % i for i in range(NDMA)]
+              + ["ac%d" % t for t in range(R)] + ["al%d" % t for t in range(R)] + ["lc", "ll"])
+
+
+def plan(ops):
+    n, dep = len(ops), OPT["dep"]
+    rng = np.random.default_rng(OPT["seed"])
+    pre = [[(j, 0.0 if j in o["soft"] and o["kind"] != "x" else ops[j]["lat"] + dep) for j in o["deps"] | o["soft"]] for o in ops]
+
+    def once(w, pen):
+        level = [0.0] * n
+        for i in range(n - 1, -1, -1):
+            level[i] += w[i] * min(c for (_, c) in ops[i]["alts"].values()) + ops[i]["lat"] + dep
+            for (j, _) in pre[i]:
+                level[j] = max(level[j], level[i])
+        busy, end, res = {q: [] for q in "vstgyx"}, [0.0] * n, [None] * n
+        for i in sorted(range(n), key=lambda k: -level[k]):
+            ready, best = max([end[j] + d for (j, d) in pre[i]] + [0.0]), None
+            for q in ops[i]["alts"]:
+                cost, at = ops[i]["alts"][q][1], ready
+                for (a, b) in busy[q]:
+                    if b <= at:
+                        continue
+                    if at + cost <= a:
+                        break
+                    at = b
+                score = at + cost + (pen[i] * cost if q == "v" else 0.0)
+                if best is None or score < best[0]:
+                    best = (score, q, at, cost)
+            res[i], end[i] = (best[1], best[2]), best[2] + best[3]
+            busy[best[1]].append((best[2], end[i]))
+            busy[best[1]].sort()
+        return max(end[i] + ops[i]["lat"] for i in range(n)), res
+
+    w, pen = np.ones(n), np.full(n, OPT["pen0"])
+    top, res = once(w, pen)
+    names = sorted(set(o["key"] for o in ops))
+    same = np.array([names.index(o["key"]) for o in ops])
+    for it in range(OPT["tries"]):
+        w2, pen2 = w.copy(), pen.copy()
+        ids = same if it < OPT["tied"] * OPT["tries"] else np.arange(n)
+        for arr, lo, hi in ((w2, 0.05, OPT["whi"]), (pen2, -1.0, 4.0)):
+            k, val = rng.random(n) < OPT["pm"], rng.uniform(lo, hi, n)
+            arr[k[ids]] = val[ids][k[ids]]
+        span, r = once(w2, pen2)
+        if span <= top:
+            top, res, w, pen = span, r, w2, pen2
+    OPT["span"] = top
+    return res
+
+
+def rank_program(g, core, T, topo):
+    rank = T.rank_of(core)
+    if rank is None:
+        return
+    n_ranks = len(T.cores)
+    op = AluOpType
+    fn = ActivationFunctionType
+    queue = {"v": g.vector, "s": g.scalar, "t": g.tensor, "g": g, "y": g.sync}
+    ops, hist = [], {}
+    cy, ga = OPT["cy"], OPT["ga"]
+
+    def A(name, a=0, b=None, st=1):
+        return (name, a, SCRATCH[name][1][1] if b is None else b, st, None, None)
+
+    def ind(w, off):
+        return w[:4] + (off, w[5])
+
+    def cast(w, d):
+        return w[:5] + (d,)
+
+    def real(x):
+        if not isinstance(x, tuple):
+            return x
+        v = T[x[0]][:, x[1]:x[2]:x[3]] if x[3] != 1 else T[x[0]][:, x[1]:x[2]]
+        if x[5] is not None:
+            v = v.bitcast(x[5])
+        if x[4] is not None:
+            v = v.indirect(real(x[4]))
+        return v
+
+    def bits(x):
+        if x[0] == "ps":
+            return 1 << (x[1] // 512)
+        if x[3] == 1:
+            return ((1 << (x[2] - x[1])) - 1) << x[1]
+        return sum(1 << i for i in range(x[1], x[2], x[3]))
+
+    def size(x):
+        return len(range(x[1], x[2], x[3]))
+
+    def add(alts, rd, wr, kind="c", sem=None, cnt=1, chain=False, lat=0.0, after=()):
+        me, deps, soft, use = len(ops), set(), set(after), []
+        for x in rd:
+            if isinstance(x, tuple):
+                use.append((x[0], bits(x), x[0] == "ps"))
+                if x[4] is not None:
+                    use.append((x[4][0], bits(x[4]), False))
+        for x in wr:
+            use.append((x[0], bits(x), True))
+        for name, m, w in use:
+            for (j, m2, w2) in hist.get(name, []):
+                if (w or w2) and m & m2:
+                    (soft if chain and name == "ps" and "t" in ops[j]["alts"] else deps).add(j)
+        for name, m, w in use:
+            hist.setdefault(name, []).append((me, m, w))
+        key = str([x[:3] if x[0] not in ("arr", "lq", "ls") else x[0] for x in wr + rd[:1] if isinstance(x, tuple)])
+        ops.append({"alts": alts, "deps": deps, "soft": soft, "kind": kind, "sem": sem, "cnt": cnt, "lat": lat, "key": key})
+        return me
+
+    def vcost(out, a, per, *more):
+        if a[4] is not None:
+            return 50 + ga * size(out)
+        if per == 1 and all(SCRATCH[x[0]][2] in (B, U16) for x in (out, a) + more):
+            per = 0.5
+        return max(64, size(out) * per) * cy
+
+    def scost(out, a):
+        return 65 + ga * size(out) if a[4] is not None else max(64, size(out)) * cy + OPT["sfix"]
+
+    def ts(out, a, s1, o0, s2=None, o1=None):
+        if o1 is None:
+            call = lambda: g.vector.tensor_scalar(real(out), real(a), real(s1), None, o0)
+        else:
+            call = lambda: g.vector.tensor_scalar(real(out), real(a), real(s1), real(s2), o0, o1)
+        add({"v": (call, vcost(out, a, 1))}, [a, s1, s2], [out])
+
+    def tt(out, a, b, o):
+        add({"v": (lambda: g.vector.tensor_tensor(real(out), real(a), real(b), o), vcost(out, a, 1 if b[0] == "ps" else 2, b))},
+            [a, b], [out])
+
+    def cp(out, a):
+        add({"v": (lambda: g.vector.tensor_copy(real(out), real(a)), vcost(out, a, 1))}, [a], [out])
+
+    def mov(out, a, scale=1.0, bias=0.0):
+        if scale == 1.0 and bias == 0.0:
+            call = lambda: g.vector.tensor_copy(real(out), real(a))
+        elif bias == 0.0:
+            call = lambda: g.vector.tensor_scalar(real(out), real(a), scale, None, op.mult)
+        else:
+            call = lambda: g.vector.tensor_scalar(real(out), real(a), bias, None, op.add)
+        if bias == 0.0:
+            call2 = lambda: g.scalar.activation(real(out), real(a), fn.Copy, scale=scale)
+        else:
+            call2 = lambda: g.scalar.activation(real(out), real(a), fn.Identity, bias=bias)
+        add({"v": (call, vcost(out, a, 1)), "s": (call2, scost(out, a))}, [a], [out])
+
+    def scan(out, a, b, o0, o1, init=0.0):
+        add({"v": (lambda: g.vector.tensor_tensor_scan(real(out), real(a), real(b), init, o0, o1), vcost(out, a, 1, b))}, [a, b], [out])
+
+    def ms(out, val):
+        add({"v": (lambda: g.vector.memset(real(out), val), vcost(out, out, 1))}, [], [out])
+
+    def quant(q, s, a):
+        add({"v": (lambda: g.vector.quantize_mx(real(q), real(s), real(a)), 15 + 0.275 * size(a))}, [a], [q, s])
+
+    def act(out, a, f, bias=0.0, scale=1.0, acc=None):
+        add({"s": (lambda: g.scalar.activation(real(out), real(a), f, bias=real(bias), scale=scale, accum_out=real(acc)),
+                   scost(out, a) + (20 if acc else 0))}, [a, bias], [out] + ([acc] if acc else []))
+
+    def mm(out, lq, lsc, rq, rsc, start=True, stop=True):
+        add({"t": (lambda: g.tensor.matmul_mx(real(out), real(lq), real(lsc), real(rq), real(rsc), start, stop),
+                   1.25 * (size(out) + 16))}, [lq, lsc, rq, rsc], [out], chain=not start, lat=60.0)
+
+    def iota(out, pat, base=0, cmul=0):
+        if SCRATCH[out[0]][2] == I:
+            call = lambda: g.iota(real(out), pat, base, cmul)
+        else:
+            call = lambda: g.iota(real(out), pat, base, cmul, allow_small_or_imprecise_dtypes=True)
+        add({"g": (call, 150 + 2 * cy * size(out))}, [], [out])
+
+    def sel(out, a, pat, cmp, base, cmul):
+        add({"g": (lambda: g.affine_select(real(out), real(a), pat, cmp, 0.0, base, cmul), 190 + 2 * cy * size(out))}, [a], [out])
+
+    nd = [0]
+
+    def dma(q, out, a, rd, wr, kb=0):
+        nd[0] += 1
+        add({q: (lambda: queue[q].dma_start(out, a), 100.0)}, rd, wr, kind="d",
+            sem="m%d" % (nd[0] - 1), cnt=16, lat=OPT["dma"] + 5.0 * kb)
+
+    def bank(b, a, n):
+        return A("ps", 512 * b + a, 512 * b + a + n)
+
+    def col(name, c):
+        return A(name, c, c + 1)
+
+    def halves(out, win, off, **kw):
+        for k in range(2):
+            mov(A(out, M * k, M * k + M), ind(win, A(off, 12 * k, 12 * k + 12)), **kw)
+
+    def invert(res, n, marks, row, idx, cnt, thr, scale, a0):
+        halves(marks, A("cm2"), idx)
+        scan(A(row, 1, C + 1), A(marks), A("iob"), op.max, op.min, -192.0)
+        for c in range(n):
+            lo = 256 * c
+            act(A("junk", C * (a0 + c) + lo, C * (a0 + c) + C), A(cnt, lo, C), fn.Sign, col(thr, c), scale, col("acc", a0 + c))
+            ts(col("bw", 2 * a0 + c), col("acc", a0 + c), 0.5, op.mult, (C + lo) / 2, op.add)
+        ts(A(res), ind(A(row, 0, C + 1), A("bw", 2 * a0, 2 * a0 + n)), 192.0, op.add)
+
+    dma("s", real(A("ut")), T.u[:], [], [A("ut")], 128)
+    dma("y", real(A("xi", 0, 4 * M)), T.x[:, 0:4 * M], [], [A("xi", 0, 4 * M)], 320)
+    dma("y", real(A("xi", 4 * M, 4 * C)), T.x[:, 4 * M:4 * C], [], [A("xi", 4 * M, 4 * C)], 512)
+    dma("s", real(A("twi")), T.tw[:], [], [A("twi")])
+    dma("y", real(cast(A("wq"), dt.uint8)), T.wc[:], [col("xi", 4 * M)], [A("wq")], 256)
+    dma("y", real(A("wp")), T.ws[:], [col("xi", 4 * M)], [A("wp")], 64)
+    dma("y", real(A("vt")), T.v[:], [col("wq", 0)], [A("vt")], 128)
+
+    iota(A("uli"), [[16, 8]])
+    iota(A("pi"), [[0, 1]], 0, 1)
+    iota(A("io1"), [[1, C]], 1)
+    iota(A("iob"), [[1, C]], -191)
+    iota(A("i16"), [[0, 24], [1, 16]])
+    iota(A("iw"), [[16, 24]])
+    iota(A("fl", 12 * M, 16 * M), [[0, 4 * M]])
+    iota(A("sl", 0, 128), [[0, 128]])
+    for p in (0, 2):
+        iota(A("xo", PL * p + M + 1, PL * p + PL), [[0, PL - M - 1]])
+    ms(A("ones"), 1.0)
+    ms(A("zero"), 0.0)
+    sel(A("bo1"), A("ones"), [[-16, 8], [0, 64]], op.is_ge, 0, 1)
+    sel(A("bo2"), A("bo1"), [[16, 8], [0, 64]], op.is_ge, 15, -1)
+    for p in range(4):
+        sel(A("et", 512 * p, 512 * p + 512), A("ones"), [[-1, 512]], op.is_equal, p, 4)
+    ms(col("lv", 0), 0.0)
+    ms(col("tie", 0), EPS)
+    ms(col("tie", 1), -EPS)
+    for name in ("po", "pg", "pq"):
+        ms(col(name, 0), -192.0)
+    cp(A("ul"), A("uli"))
+    ts(A("ri"), A("pi"), 15, op.bitwise_and)
+    cp(A("rf"), A("ri"))
+    ts(A("r97"), A("rf"), 97.0, op.add)
+    ts(col("kb", 0), A("rf"), 16.0, op.mult, 15.5, op.add)
+    ts(col("kq", 0), A("rf"), 16.0, op.mult, -128.5, op.add)
+    ts(col("kq", 1), A("rf"), 16.0, op.mult, 127.5, op.add)
+    ts(A("cm"), A("i16"), A("rf"), op.is_equal, BIG, op.mult)
+    ts(A("cm", 0, C, 16), A("cm", 0, C, 16), -1.0, op.add)
+    ts(A("keep"), A("cm"), 0.0, op.is_equal)
+    ts(A("cm2"), A("cm"), 2.0, op.mult, -BIG, op.add)
+    ts(A("cm1"), A("i16"), A("rf"), op.is_equal)
+    ts(A("iw"), A("iw"), A("rf"), op.add)
+    ts(A("ths"), A("iw", 0, 18), -512.0, op.mult, 512.0 * 143, op.add)
+    ts(A("thl"), A("iw", 0, 6), 512.0, op.mult, 512.0, op.add)
+    for t in range(R):
+        quant(A("lq", 224 * t + NL, 224 * t + 224), A("ls", 512 * t + C, 512 * t + 512), A("zero", 0, 512))
+    quant(A("qj"), A("ss", 0, 256), A("zero"))
+    quant(A("qo"), A("so"), A("bo2"))
+    for k in range(2):
+        quant(A("qe", 256 * k, 256 * k + 256), A("se", 256 * k, 256 * k + 256), A("et", 1024 * k, 1024 * k + 1024))
+    quant(A("qv"), A("sv"), A("vt"))
+    quant(A("qu"), A("su"), A("ut"))
+    cp(A("twf"), A("twi"))
+    cp(cast(A("qu2"), dt.uint32), ind(cast(A("qu"), dt.uint32), A("ul")))
+    cp(A("su2"), ind(A("su"), A("ul")))
+
+    for k in range(2):
+        quant(A("qx", M * k, M * k + M), A("sx", M * k, M * k + M), A("xi", 4 * M * k, 4 * M * k + 4 * M))
+        mm(bank(k, 0, M), A("qu2"), A("su2"), A("qx", M * k, M * k + M), A("sx", M * k, M * k + M))
+        mov(A("sr", M * k, M * k + M), bank(k, 0, M))
+    tt(A("hf"), A("twi"), A("iw"), op.is_lt)
+    cp(A("hw"), A("hf"))
+    halves("st", A("sr"), "twf")
+    for k in range(2):
+        tt(A("d", M * k, M * k + M), A("st", M * k, M * k + M), bank(k, 0, M), op.subtract)
+    tt(A("un"), ind(A("tie", 0, 2), A("hw")), A("d"), op.is_lt)
+
+    for t in range(R):
+        last = t == R - 1
+        scan(A("cum"), A("un"), A("un"), op.add, op.max)
+        scan(A("cap"), A("cm"), A("cum"), op.max, op.min)
+        cp(A("cw"), A("cap", 15, C, 16))
+        invert("ow", 1, "mo", "po", "cw", "cum", "kb", -1.0, 0)
+        ow = A("ow", 0, 12)
+        mov(A("dr"), ind(A("d"), ow))
+        tt(A("dm"), ind(A("d"), ow), A("cm", 0, M), op.min)
+        scan(A("dh"), A("keep", 0, M), A("dm"), op.mult, op.add)
+        for c in range(8, 12):
+            act(A("sg", c % 4, 512, 4), A("dr", 0, 128), fn.Sign, col("dh", 16 * c + 15), -1.0)
+        act(A("fl", 8 * M, 8 * M + 512), A("sg"), fn.Relu, 0.0, -1.0)
+        for c in range(12):
+            base, k, k0 = 4 * M * (c // 4) + c % 4, 16 * c + 16, 128 if c >= 8 else 0
+            ts(A("fl", base + 4 * k0, base + 4 * k - 3, 4), A("dr", k0, k), col("dh", k - 1), op.is_gt)
+            if k < M:
+                ts(A("fl", base + 4 * k, base + 4 * M - 3, 4), A("dr", k, M), col("dh", k - 1), op.is_ge)
+        tt(A("fl", 12 * M, 16 * M, 4), A("dh"), A("dr"), op.is_equal)
+        for s in range(2):
+            quant(A("qf", 2 * M * s, 2 * M * s + 2 * M), A("sf", 2 * M * s, 2 * M * s + 2 * M), A("fl", 8 * M * s, 8 * M * s + 8 * M))
+        for s in range(4):
+            mm(bank(2, 0, M), A("qo"), A("so"), A("qf", M * s, M * s + M), A("sf", M * s, M * s + M), s == 0, s == 3)
+        ts(A("lv", 1, 1 + M), bank(2, 0, M), 48.5, op.is_le, 512.0, op.mult)
+        mov(A("ct"), ind(A("cum"), A("twf")))
+        tt(A("ctm"), ind(A("ct"), ow), A("cm", 0, M), op.min)
+        scan(A("cth"), A("keep", 0, M), A("ctm"), op.mult, op.add)
+        cp(A("ctw"), A("cth", 15, M, 16))
+        for p in range(4):
+            ts(A("ow4", 16 * p, 16 * p + 16), ind(A("po", 0, C + 1), A("bw", 0, 1)), 4.0, op.mult, 768.0 + p, op.add)
+            mov(A("xo", PL * p + 1, PL * p + 1 + M), ind(A("xi"), A("ow4", 16 * p, 16 * p + 12)), 0.5)
+        mov(A("xo", 0, 4 * PL, PL), A("xo", M, 4 * PL, PL))
+        for p in range(4):
+            if p % 2 == 0:
+                mov(A("xa", PL * p, PL * p + PL + M), A("xo", PL * p, PL * p + PL + M))
+            tt(A("z", p, 4 * M, 4), ind(A("xo", PL * p, PL * p + M + 1), A("ctw")), A("xa", PL * p, PL * p + M), op.add)
+        quant(A("qz"), A("sz"), A("z"))
+        for p in range(4):
+            mm(bank(4 + p, 0, M), A("wq", 128 * p, 128 * p + 128), A("wp", 128 * p, 128 * p + 128), A("qz"), A("sz"))
+            mov(A("hx", PL * p + 1, PL * p + 1 + M), bank(4 + p, 0, M), 0.03125)
+        mov(A("hx", 0, 4 * PL, PL), A("hx", M, 4 * PL, PL))
+        for p in range(4):
+            tt(A("e", C * p, C * p + C), ind(A("hx", PL * p, PL * p + M + 1), A("cw")), A("xi", p, 4 * C, 4), op.add)
+        scan(A("cap2", 1, C), A("cm", 1, C), A("cum", 0, C - 1), op.max, op.min)
+        tt(A("uf"), A("cap", 15, C, 16), A("cap2", 15, C, 16), op.subtract)
+        tt(A("uf"), A("uf"), A("cap", 15, C, 16), op.mult)
+        cp(A("uw"), A("uf"))
+        halves("g1", A("lv", 0, M + 1), "uw")
+        halves("g2", A("g1"), "twf")
+        mov(A("g2p"), A("g1"), bias=-512.0)
+        scan(A("gn"), A("g1"), A("g2"), op.add, op.add)
+        scan(A("ncs"), A("g2"), A("g2p"), op.add, op.add, 512.0 * 144)
+        scan(A("capg"), A("cm"), A("gn"), op.max, op.min)
+        ts(A("gw"), A("capg", 15, C, 16), 1.0 / 512, op.mult)
+        ts(A("sw"), A("capg", 15, C, 16), -1.0 / 512, op.mult, A("r97"), op.add)
+        invert("lw", 1, "mg", "pg", "gw", "gn", "kb", -1.0 / 512, 1)
+        invert("qw", 2, "mq", "pq", "sw", "ncs", "kq", 1.0 / 512, 2)
+        lw, qw = A("lw", 0, 6), A("qw", 0, 18)
+        for p in range(4):
+            mov(A("sl", 128 + p, 512, 4), ind(A("e", C * p, C * p + C), lw))
+        quant(A("qs"), A("ss", 256, C), A("sl"))
+        dst = T.cores[(rank + STEP[t]) % n_ranks]
+        rid, pid = topo.addr(dst)[:2]
+        eng = topo.engines(core, dst)
+        half = len(eng) // 2
+        m0, m1 = sum(1 << k for k in eng[:half]), sum(1 << k for k in eng[half:])
+
+        def send_codes(t=t, rid=rid, pid=pid, m0=m0, m1=m1):
+            to = [DstId(rid=rid, pnc=pid)]
+            return g.remote_dma_fused([
+                RemoteDMATransfer(dst_ids=to, dma_engine_mask=m0, remote_sem=T.sem["ac%d" % t],
+                                  src=real(cast(A("qs", 32, 128), dt.uint8)), dst=real(cast(A("lq", 224 * t, 224 * t + NL), dt.uint8))),
+                RemoteDMATransfer(dst_ids=to, dma_engine_mask=m1, remote_sem=T.sem["ac%d" % t],
+                                  src=real(A("ss")), dst=real(A("ls", 512 * t, 512 * t + C)))], local_sem=T.sem.lc)
+
+        j = add({"g": (send_codes, OPT["issue"])}, [A("qs", 32, 128), A("ss")], [], kind="r", sem="lc", cnt=2 * half, lat=OPT["rem"])
+        add({"x": (None, 0.0)}, [], [A("lq", 224 * t, 224 * t + NL), A("ls", 512 * t, 512 * t + C)], kind="x",
+            sem="ac%d" % t, cnt=2 * half, after=[j])
+        wide = 6 if last else 12
+        arr, arh, land, snd = A("arr", 16 * t, 16 * t + 6), A("arr", 16 * t + 6, 16 * t + 12), A("arr", 16 * t, 16 * t + wide), A("snd", 0, wide)
+        mov(A("t1"), ind(A("gn"), A("twf")))
+        mov(A("t2"), ind(A("ncs"), A("twf")))
+        tt(A("nm", NS, C), ind(A("t1"), lw), A("cm", 0, NL), op.min)
+        scan(A("nh", NS, C), A("keep", 0, NL), A("nm", NS, C), op.mult, op.add)
+        ts(A("snd", 0, 6), A("nh", NS + 15, C, 16), 1.0 / 512, op.mult, -1.0, op.add)
+        if not last:
+            tt(A("hf", 18, 24), A("nh", NS + 15, C, 16), A("thl"), op.is_lt)
+            cp(A("snd", 6, 12), A("hf", 18, 24))
+        j = add({"g": (lambda t=t, rid=rid, pid=pid, m=m0 | m1, land=land, snd=snd: g.remote_dma(
+            real(land), real(snd), T.sem["al%d" % t], T.sem.ll, pid, rid, m), OPT["issue"])},
+            [snd], [], kind="r", sem="ll", cnt=2 * half, lat=OPT["rem"])
+        add({"x": (None, 0.0)}, [], [land], kind="x", sem="al%d" % t, cnt=2 * half, after=[j])
+        tt(A("nm", 0, NS), ind(A("t2"), qw), A("cm1", 0, NS), op.mult)
+        scan(A("nh", 0, NS), A("keep", 0, NS), A("nm", 0, NS), op.mult, op.add)
+        ts(A("twf", 0, 18), A("nh", 15, NS, 16), -1.0 / 512, op.mult, 143.0, op.add)
+        ts(A("twf", 18, 24), arr, float(NS), op.add)
+        for p in range(4):
+            mov(A("xi", p, 4 * NS, 4), ind(A("e", C * p, C * p + C), qw))
+        quant(A("qx", 0, NS), A("sx", 0, NS), A("xi", 0, 4 * NS))
+        for p in range(4):
+            mm(bank(4 + p, 0, 128), A("qe", 128 * p, 128 * p + 128), A("se", 128 * p, 128 * p + 128),
+               A("lq", 224 * t, 224 * t + 128), A("ls", 512 * t + NS, 512 * t + NS + 128))
+            mov(A("xi", 4 * NS + p, 4 * C, 4), bank(4 + p, 0, NL))
+        quant(A("qb"), A("sq"), A("xi", 4 * 256, 4 * C))
+        if last:
+            mm(bank(0, 0, NS), A("qv"), A("sv"), A("qx", 0, NS), A("sx", 0, NS))
+            mov(A("yo", 0, NS), bank(0, 0, NS))
+            mm(bank(1, 0, 128), A("qv"), A("sv"), A("qb"), A("sq"))
+            mov(A("yo", NS, C), bank(1, 32, NL))
+            dma("y", T.oc[:, 0:4 * NS], real(cast(A("qx", 0, NS), dt.uint8)), [A("qx", 0, NS)], [], 144)
+            for k in range(4):
+                dma("y", T.osc[4 * k:4 * k + 4, 0:NS], T.sx[32 * k:32 * k + 4, 0:NS], [A("sx", 0, NS)], [])
+            dma("y", T.y[:, 0:NS], real(A("yo", 0, NS)), [A("yo", 0, NS)], [], 144)
+            dma("y", T.oc[:, 4 * NS:4 * C], real(cast(A("qb", 32, 128), dt.uint8)), [A("qb")], [], 48)
+            for k in range(4):
+                dma("y" if k < 2 else "s", T.osc[4 * k:4 * k + 4, NS:C], T.sq[32 * k:32 * k + 4, 32:128], [A("sq")], [])
+            dma("s", T.y[:, NS:C], real(A("yo", NS, C)), [A("yo", NS, C)], [], 48)
+            halves("otr", A("io1"), "twf", bias=-1.0)
+            dma("y", T.ot[:], T.otr[0:128:16, :], [A("otr")], [])
+        else:
+            mm(bank(0, 0, NS), A("qu2"), A("su2"), A("qx", 0, NS), A("sx", 0, NS))
+            mov(A("sr", 0, NS), bank(0, 0, NS))
+            mm(bank(1, 0, 128), A("qu2"), A("su2"), A("qb"), A("sq"))
+            mov(A("sr", NS, C), bank(1, 32, NL))
+            tt(A("hf", 0, 18), A("nh", 15, NS, 16), A("ths"), op.is_gt)
+            cp(A("hw", 0, 18), A("hf", 0, 18))
+            mov(A("st", 0, 160), ind(A("sr", 0, NS), A("twf", 0, 10)))
+            mov(A("st", 160, NS), ind(A("sr", 0, NS), A("twf", 10, 18)))
+            mov(A("st", NS, C), ind(A("sr", NS, C), arr))
+            tt(A("d", 0, NS), A("st", 0, NS), bank(0, 0, NS), op.subtract)
+            tt(A("d", NS, C), A("st", NS, C), bank(1, 32, NL), op.subtract)
+            tt(A("un", 0, NS), ind(A("tie", 0, 2), A("hw", 0, 18)), A("d", 0, NS), op.is_lt)
+            tt(A("un", NS, C), ind(A("tie", 0, 2), arh), A("d", NS, C), op.is_lt)
+
+    n = len(ops)
+    if "plan" not in OPT:
+        OPT["plan"] = plan(ops)
+    for i in range(n):
+        ops[i]["q"], ops[i]["start"] = OPT["plan"][i]
+    order = sorted(range(n), key=lambda k: (ops[k]["start"], k))
+
+    ops.append({"q": "g", "alts": {"g": (None, 0.0)}, "deps": set(j for j in range(n) if ops[j]["kind"] != "c"), "kind": "e"})
+    order.append(n)
+    pos = {order[k]: k for k in range(n + 1)}
+    know, seen = {q: 0 for q in queue}, {}
+    for i in order:
+        o = ops[i]
+        o["waits"], o["sig"], o["know"], o["before"] = [], o["kind"] != "c", 0, 0
+        if o["q"] == "x":
+            continue
+        if o["kind"] == "c" and OPT["inorder"]:
+            o["before"] = seen.get(o["q"], 0)
+            seen[o["q"]] = o["before"] | 1 << i
+        for j in sorted(o["deps"], key=lambda k: -pos[k]):
+            if not know[o["q"]] >> j & 1:
+                o["waits"].append(j)
+                ops[j]["sig"] = True
+                know[o["q"]] |= ops[j]["know"] | 1 << j | ops[j]["before"]
+        o["know"] = know[o["q"]]
+    turn, prev, total = {q: 0 for q in POOL}, {}, {}
+    for i in order:
+        o = ops[i]
+        if not o["sig"] or o["kind"] == "e":
+            continue
+        if o["kind"] == "c":
+            o["sem"] = "%s%d" % (o["q"], turn[o["q"]] % POOL[o["q"]])
+            turn[o["q"]] += 1
+        j = prev.get(o["sem"])
+        if j is not None and not o["know"] >> j & 1:
+            o["waits"].append(j)
+        prev[o["sem"]] = i
+        total[o["sem"]] = total.get(o["sem"], 0) + o["cnt"]
+        o["val"] = total[o["sem"]]
+    for i in order:
+        o = ops[i]
+        if o["q"] == "x":
+            continue
+        for j in o["waits"]:
+            queue[o["q"]].wait_ge(T.sem[ops[j]["sem"]], ops[j]["val"])
+        call = o["alts"][o["q"]][0]
+        if call is not None:
+            ins = call()
+            if o["sig"] and o["kind"] != "r":
+                ins.then_inc(T.sem[o["sem"]], o["cnt"])

@@ -7,8 +7,10 @@ STEP = [1, 2, 4]
 PL = 208
 BIG = 2.0 ** 80
 EPS = 2.0 ** -110
-OPT = {"cy": 1.04, "ga": 1.62, "dep": 75.0, "sfix": 40.0, "dma": 2000.0, "rem": 2500.0, "issue": 600.0,
-       "tries": 5000, "tied": 0.7, "pm": 0.015, "whi": 6.0, "pen0": 2.0, "seed": 0, "inorder": True}
+OPT = {"cy": 0.85, "ga": 1.15, "dep": 190.0, "sfix": 40.0, "dma": 2000.0, "rem": 3000.0, "issue": 600.0,
+       "tries": 4500, "tied": 0.7, "pm": 0.015, "whi": 8.0, "pen0": 2.0, "seed": 0,
+       "sets": [(1.0, 0.0, 0.0, 0.0), (1.0, -80.0, 2000.0, 0.0), (1.4, 0.0, 0.0, 0.0), (1.15, -100.0, 0.0, 35.0)],
+       "w0": {"e'": 4.0, "z'": 4.0, "xo": 4.0, "xa": 2.0, "sl": 3.0, "xi": 2.0, "fl": 5.0, "hx": 2.0}}
 
 
 def sb(n, d):
@@ -28,13 +30,12 @@ SCRATCH = {
     "uli": sb(8, I), "ul": sb(8, U16), "pi": sb(1, I), "ri": sb(1, I), "rf": sb(1, F), "r97": sb(1, F), "kb": sb(2, F), "kq": sb(2, F),
     "io1": sb(C, F), "iob": sb(C, B), "i16": sb(C, B), "cm": sb(C, B), "cm1": sb(C, B), "cm2": sb(C, B), "keep": sb(C, B),
     "tie": sb(16, F), "iw": sb(24, F), "ths": sb(18, F), "thl": sb(6, F), "hf": sb(24, F), "hw": sb(24, U16),
-    "sr": sb(C, F), "st": sb(C, F), "d": sb(C, F), "un": sb(C, B), "cum": sb(C, B),
+    "sr": sb(C, F), "st": sb(C, F), "sr2": sb(NL, F), "d": sb(C, F), "un": sb(C, B), "cum": sb(C, B),
     "twf": sb(24, U16), "arr": sb(16 * R, U16), "snd": sb(16, U16),
     "junk": sb(4 * C, B), "acc": sb(4, F), "bw": sb(8, U16), "mo": sb(C, B), "mg": sb(C, B), "mq": sb(C, B),
     "po": sb(C + 8, B), "pg": sb(C + 8, B), "pq": sb(C + 8, B),
     "ow": sb(16, U16), "ow4": sb(64, U16), "lw": sb(16, U16), "qw": sb(32, U16),
-    "cap": sb(C, B), "cap2": sb(C, B), "capg": sb(C, B), "uf": sb(24, F), "uw": sb(24, U16),
-    "cw": sb(24, U16), "gw": sb(24, U16), "sw": sb(24, U16),
+    "cap": sb(C, B), "capg": sb(C, B), "cw": sb(24, U16), "gw": sb(24, U16), "sw": sb(24, U16),
     "dm": sb(M, F), "dh": sb(M, F), "dr": sb(M, F), "sg": sb(512, B),
     "fl": sb(16 * M, B), "qf": sb(4 * M, X4), "sf": sb(4 * M, U8),
     "ct": sb(C, B), "ctm": sb(M, B), "cth": sb(M, B), "ctw": sb(12, U16),
@@ -78,9 +79,17 @@ def plan(ops):
             res[i], end[i] = (best[1], best[2]), best[2] + best[3]
             busy[best[1]].append((best[2], end[i]))
             busy[best[1]].sort()
-        return max(end[i] + ops[i]["lat"] for i in range(n)), res
+        seq, span = sorted(range(n), key=lambda k: (res[k][1], k)), 0.0
+        for (f, more, far, fix) in OPT["sets"]:
+            free, fin = {q: 0.0 for q in busy}, [0.0] * n
+            for i in seq:
+                q = res[i][0]
+                at = max([free[q]] + [fin[j] + (d + more + (far if ops[j]["kind"] == "r" else 0.0) if d else 0.0) for (j, d) in pre[i]])
+                free[q] = fin[i] = at + ops[i]["alts"][q][1] * (f if ops[i]["kind"] == "c" else 1.0) + fix
+            span += max(fin[i] + ops[i]["lat"] for i in range(n)) / f
+        return span, res
 
-    w, pen = np.ones(n), np.full(n, OPT["pen0"])
+    w, pen = np.array([OPT["w0"].get(o["key"][3:5], 1.0) for o in ops]), np.full(n, OPT["pen0"])
     top, res = once(w, pen)
     names = sorted(set(o["key"] for o in ops))
     same = np.array([names.index(o["key"]) for o in ops])
@@ -194,7 +203,8 @@ def rank_program(g, core, T, topo):
         add({"v": (call, vcost(out, a, 1)), "s": (call2, scost(out, a))}, [a], [out])
 
     def scan(out, a, b, o0, o1, init=0.0):
-        add({"v": (lambda: g.vector.tensor_tensor_scan(real(out), real(a), real(b), init, o0, o1), vcost(out, a, 1, b))}, [a, b], [out])
+        add({"v": (lambda: g.vector.tensor_tensor_scan(real(out), real(a), real(b), real(init), o0, o1), vcost(out, a, 1, b))},
+            [a, b, init], [out])
 
     def ms(out, val):
         add({"v": (lambda: g.vector.memset(real(out), val), vcost(out, out, 1))}, [], [out])
@@ -238,8 +248,9 @@ def rank_program(g, core, T, topo):
             mov(A(out, M * k, M * k + M), ind(win, A(off, 12 * k, 12 * k + 12)), **kw)
 
     def invert(res, n, marks, row, idx, cnt, thr, scale, a0):
-        halves(marks, A("cm2"), idx)
-        scan(A(row, 1, C + 1), A(marks), A("iob"), op.max, op.min, -192.0)
+        if marks:
+            halves(marks, A("cm2"), idx)
+            scan(A(row, 1, C + 1), A(marks), A("iob"), op.max, op.min, -192.0)
         for c in range(n):
             lo = 256 * c
             act(A("junk", C * (a0 + c) + lo, C * (a0 + c) + C), A(cnt, lo, C), fn.Sign, col(thr, c), scale, col("acc", a0 + c))
@@ -315,10 +326,19 @@ def rank_program(g, core, T, topo):
 
     for t in range(R):
         last = t == R - 1
-        scan(A("cum"), A("un"), A("un"), op.add, op.max)
-        scan(A("cap"), A("cm"), A("cum"), op.max, op.min)
-        cp(A("cw"), A("cap", 15, C, 16))
-        invert("ow", 1, "mo", "po", "cw", "cum", "kb", -1.0, 0)
+        if t == 0:
+            scan(A("cum"), A("un"), A("un"), op.add, op.max)
+            scan(A("cap"), A("cm"), A("cum"), op.max, op.min)
+            cp(A("cw"), A("cap", 15, C, 16))
+            invert("ow", 1, "mo", "po", "cw", "cum", "kb", -1.0, 0)
+        else:
+            for (a, b) in ((0, NS), (NS, C)):
+                scan(A("cum", a, b), A("un", a, b), A("un", a, b), op.add, op.max, col("cum", a - 1) if a else 0.0)
+                scan(A("cap", a, b), A("cm", a, b), A("cum", a, b), op.max, op.min)
+                cp(A("cw", a // 16, b // 16), A("cap", a + 15, b, 16))
+                mov(A("mo", a, b), ind(A("cm2"), A("cw", a // 16, b // 16)))
+                scan(A("po", a + 1, b + 1), A("mo", a, b), A("iob", a, b), op.max, op.min, col("po", a) if a else -192.0)
+            invert("ow", 1, None, "po", "cw", "cum", "kb", -1.0, 0)
         ow = A("ow", 0, 12)
         mov(A("dr"), ind(A("d"), ow))
         tt(A("dm"), ind(A("d"), ow), A("cm", 0, M), op.min)
@@ -356,11 +376,7 @@ def rank_program(g, core, T, topo):
         mov(A("hx", 0, 4 * PL, PL), A("hx", M, 4 * PL, PL))
         for p in range(4):
             tt(A("e", C * p, C * p + C), ind(A("hx", PL * p, PL * p + M + 1), A("cw")), A("xi", p, 4 * C, 4), op.add)
-        scan(A("cap2", 1, C), A("cm", 1, C), A("cum", 0, C - 1), op.max, op.min)
-        tt(A("uf"), A("cap", 15, C, 16), A("cap2", 15, C, 16), op.subtract)
-        tt(A("uf"), A("uf"), A("cap", 15, C, 16), op.mult)
-        cp(A("uw"), A("uf"))
-        halves("g1", A("lv", 0, M + 1), "uw")
+        tt(A("g1"), ind(A("lv", 0, M + 1), A("cw")), A("un"), op.mult)
         halves("g2", A("g1"), "twf")
         mov(A("g2p"), A("g1"), bias=-512.0)
         scan(A("gn"), A("g1"), A("g2"), op.add, op.add)
@@ -441,9 +457,10 @@ def rank_program(g, core, T, topo):
             cp(A("hw", 0, 18), A("hf", 0, 18))
             mov(A("st", 0, 160), ind(A("sr", 0, NS), A("twf", 0, 10)))
             mov(A("st", 160, NS), ind(A("sr", 0, NS), A("twf", 10, 18)))
-            mov(A("st", NS, C), ind(A("sr", NS, C), arr))
+            mm(bank(3, 0, 128), A("qu2"), A("su2"), A("qb"), A("sq"))
+            mov(A("sr2"), bank(3, 32, NL))
             tt(A("d", 0, NS), A("st", 0, NS), bank(0, 0, NS), op.subtract)
-            tt(A("d", NS, C), A("st", NS, C), bank(1, 32, NL), op.subtract)
+            tt(A("d", NS, C), ind(A("sr", NS, C), arr), A("sr2"), op.subtract)
             tt(A("un", 0, NS), ind(A("tie", 0, 2), A("hw", 0, 18)), A("d", 0, NS), op.is_lt)
             tt(A("un", NS, C), ind(A("tie", 0, 2), arh), A("d", NS, C), op.is_lt)
 
@@ -463,7 +480,7 @@ def rank_program(g, core, T, topo):
         o["waits"], o["sig"], o["know"], o["before"] = [], o["kind"] != "c", 0, 0
         if o["q"] == "x":
             continue
-        if o["kind"] == "c" and OPT["inorder"]:
+        if o["kind"] == "c":
             o["before"] = seen.get(o["q"], 0)
             seen[o["q"]] = o["before"] | 1 << i
         for j in sorted(o["deps"], key=lambda k: -pos[k]):

@@ -3,14 +3,21 @@ from concourse.bass import DstId, RemoteDMATransfer
 from concourse.mybir import dt, AluOpType, ActivationFunctionType
 
 C, M, NL, NS, R = 384, 192, 96, 288, 3
+MS = NS // 2
 STEP = [1, 2, 4]
 PL = 208
 BIG = 2.0 ** 80
 EPS = 2.0 ** -110
+LEV = 3072.0
 OPT = {"cy": 0.85, "ga": 1.15, "dep": 190.0, "sfix": 40.0, "dma": 2000.0, "rem": 3000.0, "issue": 600.0,
-       "tries": 4500, "tied": 0.7, "pm": 0.015, "whi": 8.0, "pen0": 2.0, "seed": 0,
+       "moves": 60000, "heat": 0.001,
+       "fine": [(1.0, 1.15, 190.0, 0.0, 0.0, 0.0, 0.0), (1.22, 1.3, 100.0, -500.0, -1000.0, -100.0, 0.0),
+                (1.42, 1.6, 120.0, 0.0, -500.0, 0.0, 0.0), (1.1, 0.95, 150.0, -1000.0, -1500.0, -200.0, 20.0)],
+       "tries": 300, "tied": 0.7, "pm": 0.015, "whi": 8.0, "pen0": 2.0, "seed": 0,
        "sets": [(1.0, 0.0, 0.0, 0.0), (1.0, -80.0, 2000.0, 0.0), (1.4, 0.0, 0.0, 0.0), (1.15, -100.0, 0.0, 35.0)],
-       "w0": {"e'": 4.0, "z'": 4.0, "xo": 4.0, "xa": 2.0, "sl": 3.0, "xi": 2.0, "fl": 5.0, "hx": 2.0}}
+       "w0": {"e'": 4.0, "z'": 4.0, "xo": 4.0, "sl": 3.0, "xi": 2.0, "fl": 5.0, "f0": 5.0, "hx": 2.0},
+       "s0": [], "s1": [], "s2": [9, 10, 11], "ctm": 1, "nm": 1, "ow4": 1, "g1": 0, "g1m": 0, "dm": 0, "d0": 0, "d1": 1,
+       "every": 50}
 
 
 def sb(n, d):
@@ -20,30 +27,32 @@ def sb(n, d):
 F, B, I, U16, X4, U8 = "float32", "bfloat16", "int32", "uint16", "float8_e4m3fn_x4", "uint8"
 SCRATCH = {
     "ps": ("psum", [128, 4096], F),
-    "xi": sb(4 * C, B), "ut": sb(512, B), "vt": sb(512, B), "twi": sb(24, I),
+    "xi": sb(4 * C + 128, B), "ut": sb(512, B), "vt": sb(512, B), "twi": sb(24, I),
     "qx": sb(C, X4), "sx": sb(C, U8), "qb": sb(128, X4), "sq": sb(128, U8),
     "qu": sb(128, X4), "su": sb(128, U8), "qu2": sb(128, X4), "su2": sb(128, U8),
     "qv": sb(128, X4), "sv": sb(128, U8), "wq": sb(512, X4), "wp": sb(512, U8),
     "ones": sb(512, B), "et": sb(2048, B), "qe": sb(512, X4), "se": sb(512, U8),
-    "bo1": sb(512, B), "bo2": sb(512, B), "qo": sb(128, X4), "so": sb(128, U8),
-    "zero": sb(1024, B), "qj": sb(256, X4),
-    "uli": sb(8, I), "ul": sb(8, U16), "pi": sb(1, I), "ri": sb(1, I), "rf": sb(1, F), "r97": sb(1, F), "kb": sb(2, F), "kq": sb(2, F),
-    "io1": sb(C, F), "iob": sb(C, B), "i16": sb(C, B), "cm": sb(C, B), "cm1": sb(C, B), "cm2": sb(C, B), "keep": sb(C, B),
+    "bo1": sb(512, B), "bo2": sb(512, B), "qo": sb(128, X4), "so": sb(128, U8), "zero": sb(512, B),
+    "uli": sb(8, I), "ul": sb(8, U16), "pi": sb(1, I), "ri": sb(1, I), "rf": sb(1, F), "kb": sb(10, F),
+    "iob": sb(C, B), "pos": sb(C, B), "rev": sb(C, B), "i16": sb(C, B), "cm": sb(C, B), "cm1": sb(C, B), "keep": sb(C, B),
     "tie": sb(16, F), "iw": sb(24, F), "ths": sb(18, F), "thl": sb(6, F), "hf": sb(24, F), "hw": sb(24, U16),
-    "sr": sb(C, F), "st": sb(C, F), "sr2": sb(NL, F), "d": sb(C, F), "un": sb(C, B), "cum": sb(C, B),
-    "twf": sb(24, U16), "arr": sb(16 * R, U16), "snd": sb(16, U16),
-    "junk": sb(4 * C, B), "acc": sb(4, F), "bw": sb(8, U16), "mo": sb(C, B), "mg": sb(C, B), "mq": sb(C, B),
-    "po": sb(C + 8, B), "pg": sb(C + 8, B), "pq": sb(C + 8, B),
-    "ow": sb(16, U16), "ow4": sb(64, U16), "lw": sb(16, U16), "qw": sb(32, U16),
-    "cap": sb(C, B), "capg": sb(C, B), "cw": sb(24, U16), "gw": sb(24, U16), "sw": sb(24, U16),
-    "dm": sb(M, F), "dh": sb(M, F), "dr": sb(M, F), "sg": sb(512, B),
+    "sr": sb(C, F), "st": sb(C, F), "d": sb(C, F), "un": sb(C, B), "cum": sb(C, B),
+    "twf": sb(24, U16), "arr": sb(16 * R, U16), "snd": sb(16, U16), "srow": sb(NL, F), "lrow": sb(NL, F),
+    "junk": sb(5 * C, B), "acc": sb(8, F), "bw": sb(8, U16),
+    "yo": sb(C + 8, B), "yg": sb(C + 8, B), "yq": sb(C + 8, B), "mo": sb(C, B), "mg": sb(C, B), "mq": sb(C, B),
+    "po": sb(C, B), "pg": sb(C, B), "pq": sb(C, B),
+    "cto": sb(M, B), "xa": sb(4 * PL, B), "lk": sb(PL, B), "gk": sb(C + 8, B), "nr": sb(C, B),
+    "g1m": sb(C, B), "ow": sb(32, U16), "owf": sb(64, F), "ow4": sb(128, U16), "lw": sb(16, U16), "qw": sb(32, U16),
+    "cap": sb(C, B), "cw": sb(24, U16),
+    "dm": sb(M, F), "dh": sb(M, F), "dr": sb(M, F), "sg": sb(8 * M, B),
+    "f0": sb(16 * M, B), "q0": sb(4 * M, X4), "s0": sb(4 * M + 128, U8),
     "fl": sb(16 * M, B), "qf": sb(4 * M, X4), "sf": sb(4 * M, U8),
     "ct": sb(C, B), "ctm": sb(M, B), "cth": sb(M, B), "ctw": sb(12, U16),
-    "xo": sb(4 * PL, B), "xa": sb(4 * PL, B), "z": sb(4 * M, B), "qz": sb(M, X4), "sz": sb(M, U8), "hx": sb(4 * PL, B),
-    "lv": sb(PL, B), "g1": sb(C, B), "g2": sb(C, B), "g2p": sb(C, B), "gn": sb(C, B), "ncs": sb(C, B), "e": sb(4 * C, B),
-    "sl": sb(512, B), "qs": sb(128, X4), "ss": sb(C, U8), "lq": sb(R * 224, X4), "ls": sb(R * 512, U8),
+    "xo": sb(4 * PL, B), "z": sb(4 * M, B), "qz": sb(M, X4), "sz": sb(M, U8), "hx": sb(4 * PL, B),
+    "lv": sb(PL, B), "g1": sb(C, B), "g2": sb(C, B), "gn": sb(C, B), "ncs": sb(C, B), "e": sb(4 * C, B),
+    "sl": sb(512, B), "qs": sb(128, X4), "lq": sb(R * 224, X4), "ls": sb(R * 512, U8),
     "t1": sb(C, B), "t2": sb(C, B), "nm": sb(C, B), "nh": sb(C, B),
-    "yo": sb(C, F), "otr": sb(C, F),
+    "yr": sb(C, F), "otr": sb(NS, F),
 }
 POOL = {"v": 56, "s": 36, "t": 10, "g": 10}
 NDMA = 24
@@ -55,38 +64,53 @@ def plan(ops):
     n, dep = len(ops), OPT["dep"]
     rng = np.random.default_rng(OPT["seed"])
     pre = [[(j, 0.0 if j in o["soft"] and o["kind"] != "x" else ops[j]["lat"] + dep) for j in o["deps"] | o["soft"]] for o in ops]
+    least = [min(c for (_, c) in o["alts"].values()) for o in ops]
+    alts = [[(q, o["alts"][q][1]) for q in o["alts"]] for o in ops]
+    lat = [o["lat"] for o in ops]
+    comp = [o["kind"] == "c" for o in ops]
+    pres = [[[(j, d + more + (far if ops[j]["kind"] == "r" else 0.0) if d else 0.0) for (j, d) in pre[i]] for i in range(n)]
+            for (f, more, far, fix) in OPT["sets"]]
 
     def once(w, pen):
+        w, pen = w.tolist(), pen.tolist()
         level = [0.0] * n
         for i in range(n - 1, -1, -1):
-            level[i] += w[i] * min(c for (_, c) in ops[i]["alts"].values()) + ops[i]["lat"] + dep
+            level[i] += w[i] * least[i] + lat[i] + dep
             for (j, _) in pre[i]:
-                level[j] = max(level[j], level[i])
+                if level[j] < level[i]:
+                    level[j] = level[i]
         busy, end, res = {q: [] for q in "vstgyx"}, [0.0] * n, [None] * n
         for i in sorted(range(n), key=lambda k: -level[k]):
-            ready, best = max([end[j] + d for (j, d) in pre[i]] + [0.0]), None
-            for q in ops[i]["alts"]:
-                cost, at = ops[i]["alts"][q][1], ready
-                for (a, b) in busy[q]:
-                    if b <= at:
-                        continue
-                    if at + cost <= a:
-                        break
-                    at = b
+            ready, best = 0.0, None
+            for (j, d) in pre[i]:
+                if end[j] + d > ready:
+                    ready = end[j] + d
+            for (q, cost) in alts[i]:
+                at, line = ready, busy[q]
+                k = len(line)
+                while k > 0 and line[k - 1][1] > at:
+                    k -= 1
+                while k < len(line) and at + cost > line[k][0]:
+                    at = line[k][1]
+                    k += 1
                 score = at + cost + (pen[i] * cost if q == "v" else 0.0)
                 if best is None or score < best[0]:
-                    best = (score, q, at, cost)
-            res[i], end[i] = (best[1], best[2]), best[2] + best[3]
-            busy[best[1]].append((best[2], end[i]))
-            busy[best[1]].sort()
+                    best = (score, q, at, cost, k)
+            res[i], end[i] = (best[1], best[2], best[3]), best[2] + best[3]
+            busy[best[1]].insert(best[4], (best[2], end[i]))
         seq, span = sorted(range(n), key=lambda k: (res[k][1], k)), 0.0
-        for (f, more, far, fix) in OPT["sets"]:
-            free, fin = {q: 0.0 for q in busy}, [0.0] * n
+        for s, (f, more, far, fix) in enumerate(OPT["sets"]):
+            free, fin, last = {q: 0.0 for q in busy}, [0.0] * n, 0.0
             for i in seq:
                 q = res[i][0]
-                at = max([free[q]] + [fin[j] + (d + more + (far if ops[j]["kind"] == "r" else 0.0) if d else 0.0) for (j, d) in pre[i]])
-                free[q] = fin[i] = at + ops[i]["alts"][q][1] * (f if ops[i]["kind"] == "c" else 1.0) + fix
-            span += max(fin[i] + ops[i]["lat"] for i in range(n)) / f
+                at = free[q]
+                for (j, d) in pres[s][i]:
+                    if fin[j] + d > at:
+                        at = fin[j] + d
+                free[q] = fin[i] = at + res[i][2] * (f if comp[i] else 1.0) + fix
+                if fin[i] + lat[i] > last:
+                    last = fin[i] + lat[i]
+            span += last / f
         return span, res
 
     w, pen = np.array([OPT["w0"].get(o["key"][3:5], 1.0) for o in ops]), np.full(n, OPT["pen0"])
@@ -102,7 +126,143 @@ def plan(ops):
         span, r = once(w2, pen2)
         if span <= top:
             top, res, w, pen = span, r, w2, pen2
-    OPT["span"] = top
+    return refine(ops, sorted(range(n), key=lambda k: (res[k][1], k)), [r[0] for r in res])
+
+
+def refine(ops, seq, on):
+    n, sets = len(ops), OPT["fine"]
+    rng = np.random.default_rng(OPT["seed"])
+    above, pre = [0] * n, []
+    for i, o in enumerate(ops):
+        hard, mine = 0, []
+        for j in sorted(o["deps"] | o["soft"], reverse=True):
+            if not hard >> j & 1 or ops[j]["lat"] > 100.0:
+                mine.append(j)
+            hard |= above[j]
+        above[i] = hard | sum(1 << j for j in o["deps"] | o["soft"])
+        pre.append(mine)
+    post = [[] for _ in range(n)]
+    for i in range(n):
+        for j in pre[i]:
+            post[j].append(i)
+    edge, cost, tail = [], [], []
+    for (f, ga, dep, local, far, issue, fix) in sets:
+        lat = [o["lat"] + {"d": local, "r": far}.get(o["kind"], 0.0) for o in ops]
+        edge.append([[(j, 0.0 if j in ops[i]["soft"] and ops[i]["kind"] != "x" else lat[j] + dep) for j in pre[i]] for i in range(n)])
+        cost.append([{q: (f * (o["alts"][q][1] + (ga - OPT["ga"]) * o["gath"]) + fix if o["kind"] == "c" else
+                          o["alts"][q][1] + (issue if o["kind"] == "r" else 0.0)) for q in o["alts"]} for o in ops])
+        tail.append(lat)
+
+    def replay(s, seq, on, first, fin):
+        free, e, c = {}, edge[s], cost[s]
+        for k in range(first - 1, -1, -1):
+            if on[seq[k]] not in free:
+                free[on[seq[k]]] = fin[seq[k]]
+                if len(free) == 6:
+                    break
+        for k in range(first, n):
+            i = seq[k]
+            q = on[i]
+            at = free.get(q, 0.0)
+            for (j, d) in e[i]:
+                x = fin[j] + d
+                if x > at:
+                    at = x
+            free[q] = fin[i] = at + c[i][q]
+        return max(fin[i] + tail[s][i] for i in ends)
+
+    def pack(s, seq, on, e):
+        busy, end, begin = {q: [] for q in "vstgyx"}, [0.0] * n, [0.0] * n
+        for i in seq:
+            at, c, line = (0.0 if e is edge[s] or post[i] else tail[s][i]), cost[s][i][on[i]], busy[on[i]]
+            for (j, d) in e[i]:
+                if end[j] + d > at:
+                    at = end[j] + d
+            k = len(line)
+            while k > 0 and line[k - 1][1] > at:
+                k -= 1
+            while k < len(line) and at + c > line[k][0]:
+                at = line[k][1]
+                k += 1
+            begin[i], end[i] = at, at + c
+            line.insert(k, (at, end[i]))
+        rank = {i: k for k, i in enumerate(seq)}
+        return sorted(seq, key=lambda i: (begin[i], rank[i]))
+
+    back = [[[] for _ in range(n)] for _ in sets]
+    for s in range(len(sets)):
+        for i in range(n):
+            for (j, d) in edge[s][i]:
+                back[s][j].append((i, d))
+    ends = [i for i in range(n) if not post[i]]
+    fins = [[0.0] * n for _ in sets]
+    norm = [replay(s, seq, on, 0, fins[s]) for s in range(len(sets))]
+    now = best = float(len(sets))
+    keep, held = (seq, on), None
+    for it in range(OPT["moves"]):
+        if held is None:
+            s = int(rng.integers(len(sets)))
+            fin, pos, prev, last, held = fins[s], [0] * n, [None] * n, {}, []
+            for k, i in enumerate(seq):
+                pos[i], prev[i] = k, last.get(on[i])
+                last[on[i]] = i
+            i = max(ends, key=lambda k: fin[k] + tail[s][k])
+            while i is not None:
+                at, nxt = fin[i] - cost[s][i][on[i]], None
+                for (j, d) in edge[s][i]:
+                    if fin[j] + d >= at - 0.01:
+                        nxt = j
+                if nxt is None and prev[i] is not None and fin[prev[i]] >= at - 0.01:
+                    nxt = prev[i]
+                    held.append((i, nxt))
+                i = nxt
+            if not held:
+                break
+        i, j = held[int(rng.integers(len(held)))]
+        kind, seq2, on2 = rng.random(), seq, on
+        if it % OPT["every"] == 0:
+            s = int(rng.integers(len(sets)))
+            first, seq2 = 0, pack(s, pack(s, seq[::-1], on, back[s])[::-1], on, edge[s]) if rng.random() < 0.5 else pack(s, seq, on, edge[s])
+        elif kind < 0.3:
+            x = i if rng.random() < 0.5 else j
+            other = [q for q in ops[x]["alts"] if q != on[x]]
+            if not other:
+                continue
+            on2 = list(on)
+            on2[x] = other[int(rng.integers(len(other)))]
+            first = pos[x]
+        elif kind < 0.65:
+            for _ in range(int(rng.geometric(0.5)) - 1):
+                if prev[j] is not None:
+                    j = prev[j]
+            if above[i] >> j & 1:
+                continue
+            first, mid = pos[j], seq[pos[j]:pos[i]]
+            seq2 = (seq[:first] + [x for x in mid if above[i] >> x & 1] + [i] + [x for x in mid if not above[i] >> x & 1]
+                    + seq[pos[i] + 1:])
+        else:
+            if above[i] >> j & 1:
+                continue
+            end = min(n - 1, pos[i] + int(rng.geometric(0.15)) - 1)
+            first, mid = pos[j], seq[pos[j] + 1:end + 1]
+            seq2 = (seq[:first] + [x for x in mid if not above[x] >> j & 1] + [j] + [x for x in mid if above[x] >> j & 1]
+                    + seq[end + 1:])
+        limit = now - OPT["heat"] * (1.0 - it / OPT["moves"]) * float(np.log(rng.random() + 1e-12))
+        total, fins2 = 0.0, []
+        for s in range(len(sets)):
+            fins2.append(list(fins[s]))
+            total += replay(s, seq2, on2, first, fins2[s]) / norm[s]
+        if total <= limit:
+            seq, on, fins, now, held = seq2, on2, fins2, total, None
+            if now < best:
+                best, keep = now, (seq, on)
+        elif rng.random() < 0.1:
+            held = None
+    seq, on = keep
+    OPT["span"] = [int(replay(s, seq, on, 0, fins[s])) for s in range(len(sets))]
+    res = [None] * n
+    for k, i in enumerate(seq):
+        res[i] = (on[i], k)
     return res
 
 
@@ -160,9 +320,12 @@ def rank_program(g, core, T, topo):
                 if (w or w2) and m & m2:
                     (soft if chain and name == "ps" and "t" in ops[j]["alts"] else deps).add(j)
         for name, m, w in use:
+            if w:
+                hist[name] = [h for h in hist.get(name, []) if h[1] & ~m]
             hist.setdefault(name, []).append((me, m, w))
         key = str([x[:3] if x[0] not in ("arr", "lq", "ls") else x[0] for x in wr + rd[:1] if isinstance(x, tuple)])
-        ops.append({"alts": alts, "deps": deps, "soft": soft, "kind": kind, "sem": sem, "cnt": cnt, "lat": lat, "key": key})
+        ops.append({"alts": alts, "deps": deps, "soft": soft, "kind": kind, "sem": sem, "cnt": cnt, "lat": lat, "key": key,
+                    "gath": size(wr[0]) if any(isinstance(x, tuple) and x[4] is not None for x in rd) else 0})
         return me
 
     def vcost(out, a, per, *more):
@@ -175,12 +338,17 @@ def rank_program(g, core, T, topo):
     def scost(out, a):
         return 65 + ga * size(out) if a[4] is not None else max(64, size(out)) * cy + OPT["sfix"]
 
-    def ts(out, a, s1, o0, s2=None, o1=None):
+    def tsv(out, a, s1, o0, s2=None, o1=None):
         if o1 is None:
-            call = lambda: g.vector.tensor_scalar(real(out), real(a), real(s1), None, o0)
-        else:
-            call = lambda: g.vector.tensor_scalar(real(out), real(a), real(s1), real(s2), o0, o1)
-        add({"v": (call, vcost(out, a, 1))}, [a, s1, s2], [out])
+            return (lambda: g.vector.tensor_scalar(real(out), real(a), real(s1), None, o0), vcost(out, a, 1))
+        return (lambda: g.vector.tensor_scalar(real(out), real(a), real(s1), real(s2), o0, o1), vcost(out, a, 1))
+
+    def acs(out, a, f, bias=0.0, scale=1.0, acc=None):
+        return (lambda: g.scalar.activation(real(out), real(a), f, bias=real(bias), scale=scale, accum_out=real(acc)),
+                scost(out, a) + (20 if acc else 0))
+
+    def ts(out, a, s1, o0, s2=None, o1=None):
+        add({"v": tsv(out, a, s1, o0, s2, o1)}, [a, s1, s2], [out])
 
     def tt(out, a, b, o):
         add({"v": (lambda: g.vector.tensor_tensor(real(out), real(a), real(b), o), vcost(out, a, 1 if b[0] == "ps" else 2, b))},
@@ -189,18 +357,17 @@ def rank_program(g, core, T, topo):
     def cp(out, a):
         add({"v": (lambda: g.vector.tensor_copy(real(out), real(a)), vcost(out, a, 1))}, [a], [out])
 
-    def mov(out, a, scale=1.0, bias=0.0):
+    def mov(out, a, scale=1.0, bias=0.0, pool=False):
         if scale == 1.0 and bias == 0.0:
-            call = lambda: g.vector.tensor_copy(real(out), real(a))
+            v = (lambda: g.vector.tensor_copy(real(out), real(a)), vcost(out, a, 1))
         elif bias == 0.0:
-            call = lambda: g.vector.tensor_scalar(real(out), real(a), scale, None, op.mult)
+            v = tsv(out, a, scale, op.mult)
         else:
-            call = lambda: g.vector.tensor_scalar(real(out), real(a), bias, None, op.add)
-        if bias == 0.0:
-            call2 = lambda: g.scalar.activation(real(out), real(a), fn.Copy, scale=scale)
-        else:
-            call2 = lambda: g.scalar.activation(real(out), real(a), fn.Identity, bias=bias)
-        add({"v": (call, vcost(out, a, 1)), "s": (call2, scost(out, a))}, [a], [out])
+            v = tsv(out, a, scale, op.mult, bias, op.add)
+        alts = {"v": v, "s": acs(out, a, fn.Copy if bias == 0.0 else fn.Identity, bias, scale)}
+        if pool:
+            alts["g"] = (lambda: g.affine_select(real(out), real(a), [[0, size(out)]], op.is_ge, 0.0, 0, 0), 190 + 2 * cy * size(out))
+        add(alts, [a, bias], [out])
 
     def scan(out, a, b, o0, o1, init=0.0):
         add({"v": (lambda: g.vector.tensor_tensor_scan(real(out), real(a), real(b), real(init), o0, o1), vcost(out, a, 1, b))},
@@ -213,8 +380,7 @@ def rank_program(g, core, T, topo):
         add({"v": (lambda: g.vector.quantize_mx(real(q), real(s), real(a)), 15 + 0.275 * size(a))}, [a], [q, s])
 
     def act(out, a, f, bias=0.0, scale=1.0, acc=None):
-        add({"s": (lambda: g.scalar.activation(real(out), real(a), f, bias=real(bias), scale=scale, accum_out=real(acc)),
-                   scost(out, a) + (20 if acc else 0))}, [a, bias], [out] + ([acc] if acc else []))
+        add({"s": acs(out, a, f, bias, scale, acc)}, [a, bias], [out] + ([acc] if acc else []))
 
     def mm(out, lq, lsc, rq, rsc, start=True, stop=True):
         add({"t": (lambda: g.tensor.matmul_mx(real(out), real(lq), real(lsc), real(rq), real(rsc), start, stop),
@@ -226,6 +392,11 @@ def rank_program(g, core, T, topo):
         else:
             call = lambda: g.iota(real(out), pat, base, cmul, allow_small_or_imprecise_dtypes=True)
         add({"g": (call, 150 + 2 * cy * size(out))}, [], [out])
+
+    def fill(out):
+        add({"v": (lambda: g.vector.memset(real(out), 0.0), vcost(out, out, 1)),
+             "g": (lambda: g.iota(real(out), [[0, size(out)]], 0, 0, allow_small_or_imprecise_dtypes=True), 150 + 2 * cy * size(out))},
+            [], [out])
 
     def sel(out, a, pat, cmp, base, cmul):
         add({"g": (lambda: g.affine_select(real(out), real(a), pat, cmp, 0.0, base, cmul), 190 + 2 * cy * size(out))}, [a], [out])
@@ -247,15 +418,31 @@ def rank_program(g, core, T, topo):
         for k in range(2):
             mov(A(out, M * k, M * k + M), ind(win, A(off, 12 * k, 12 * k + 12)), **kw)
 
-    def invert(res, n, marks, row, idx, cnt, thr, scale, a0):
-        if marks:
-            halves(marks, A("cm2"), idx)
-            scan(A(row, 1, C + 1), A(marks), A("iob"), op.max, op.min, -192.0)
-        for c in range(n):
-            lo = 256 * c
-            act(A("junk", C * (a0 + c) + lo, C * (a0 + c) + C), A(cnt, lo, C), fn.Sign, col(thr, c), scale, col("acc", a0 + c))
-            ts(col("bw", 2 * a0 + c), col("acc", a0 + c), 0.5, op.mult, (C + lo) / 2, op.add)
-        ts(A(res), ind(A(row, 0, C + 1), A("bw", 2 * a0, 2 * a0 + n)), 192.0, op.add)
+    def steps(y, m, p, a, b, up=True):
+        now, before = A(y, a + 1, b + 1), A(y, a, b)
+        scan(A(m, a, b), now if up else before, before if up else now, op.max, op.subtract)
+        scan(A(p, a, b), A(m, a, b), A("pos", a, b), op.add, op.min, (a - 191) / 32.0)
+
+    def where(k, cnt, a, b, thr, scale, a0, j):
+        act(A("junk", C * j + a, C * j + b), A(cnt, a, b), fn.Sign, col("kb", thr), scale, col("acc", k))
+        ts(col("bw", k), col("acc", k), 0.5, op.mult, (b - a) / 2 + a - a0, op.add)
+
+    def compare(name, tiles, by_s):
+        for (at, a, b, planes) in tiles:
+            for s, c in enumerate(planes):
+                part = lambda lo, hi: A(name, 4 * (at + lo - a) + s, 4 * (at + hi - a), 4)
+                if c == 12:
+                    tt(part(a, b), A("dh", a, b), A("dr", a, b), op.is_equal)
+                    continue
+                k, lo, piv = min(max(16 * c + 16, a), b), a, col("dh", 16 * c + 15)
+                if c in by_s and a == 0:
+                    lo = min(k, by_s[c])
+                    act(A("sg", M * (c % 8), M * (c % 8) + lo), A("dr", 0, lo), fn.Sign, piv, -1.0)
+                    act(part(0, lo), A("sg", M * (c % 8), M * (c % 8) + lo), fn.Relu, 0.0, -1.0)
+                if lo < k:
+                    ts(part(lo, k), A("dr", lo, k), piv, op.is_gt)
+                if k < b:
+                    ts(part(k, b), A("dr", k, b), piv, op.is_ge)
 
     dma("s", real(A("ut")), T.u[:], [], [A("ut")], 128)
     dma("y", real(A("xi", 0, 4 * M)), T.x[:, 0:4 * M], [], [A("xi", 0, 4 * M)], 320)
@@ -267,43 +454,45 @@ def rank_program(g, core, T, topo):
 
     iota(A("uli"), [[16, 8]])
     iota(A("pi"), [[0, 1]], 0, 1)
-    iota(A("io1"), [[1, C]], 1)
     iota(A("iob"), [[1, C]], -191)
     iota(A("i16"), [[0, 24], [1, 16]])
     iota(A("iw"), [[16, 24]])
-    iota(A("fl", 12 * M, 16 * M), [[0, 4 * M]])
-    iota(A("sl", 0, 128), [[0, 128]])
-    for p in (0, 2):
-        iota(A("xo", PL * p + M + 1, PL * p + PL), [[0, PL - M - 1]])
+    mov(A("pos"), A("iob"), 1.0 / 32)
+    if not OPT["g1m"]:
+        mov(A("rev"), A("iob"), -1.0, -48.0)
+    fill(A("f0", 12 * M, 16 * M))
+    fill(A("fl", 4 * NL, 4 * MS))
+    fill(A("fl", 12 * MS, 16 * M))
+    fill(A("xi", 4 * C, 4 * C + 128))
+    fill(A("sl", 0, 128))
+    fill(A("zero"))
     ms(A("ones"), 1.0)
-    ms(A("zero"), 0.0)
     sel(A("bo1"), A("ones"), [[-16, 8], [0, 64]], op.is_ge, 0, 1)
     sel(A("bo2"), A("bo1"), [[16, 8], [0, 64]], op.is_ge, 15, -1)
     for p in range(4):
         sel(A("et", 512 * p, 512 * p + 512), A("ones"), [[-1, 512]], op.is_equal, p, 4)
-    ms(col("lv", 0), 0.0)
+    for name in ("lk", "gk") if OPT["g1"] else ("lv",):
+        ms(col(name, 0), 0.0)
     ms(col("tie", 0), EPS)
     ms(col("tie", 1), -EPS)
-    for name in ("po", "pg", "pq"):
-        ms(col(name, 0), -192.0)
+    for name in ("yo", "yg", "yq"):
+        ms(col(name, 0), LEV)
     cp(A("ul"), A("uli"))
     ts(A("ri"), A("pi"), 15, op.bitwise_and)
     cp(A("rf"), A("ri"))
-    ts(A("r97"), A("rf"), 97.0, op.add)
-    ts(col("kb", 0), A("rf"), 16.0, op.mult, 15.5, op.add)
-    ts(col("kq", 0), A("rf"), 16.0, op.mult, -128.5, op.add)
-    ts(col("kq", 1), A("rf"), 16.0, op.mult, 127.5, op.add)
+    for k, a, b in ((0, 16.0, 15.5), (2, 16.0, -128.5), (3, 16.0, 127.5), (4, -1.0, LEV + 7.5), (5, 1.0, LEV - 7.5),
+                    (6, 1.0, LEV - 7.5 - MS), (7, 1.0, MS + 0.5), (8, 1.0, MS + 16.5), (9, 1.0, MS + 32.5)):
+        if k != (6 if OPT["g1m"] else 5):
+            mov(col("kb", k), A("rf"), a, b)
     ts(A("cm"), A("i16"), A("rf"), op.is_equal, BIG, op.mult)
     ts(A("cm", 0, C, 16), A("cm", 0, C, 16), -1.0, op.add)
     ts(A("keep"), A("cm"), 0.0, op.is_equal)
-    ts(A("cm2"), A("cm"), 2.0, op.mult, -BIG, op.add)
-    ts(A("cm1"), A("i16"), A("rf"), op.is_equal)
-    ts(A("iw"), A("iw"), A("rf"), op.add)
-    ts(A("ths"), A("iw", 0, 18), -512.0, op.mult, 512.0 * 143, op.add)
-    ts(A("thl"), A("iw", 0, 6), 512.0, op.mult, 512.0, op.add)
+    ts(A("cm1", 0, NS), A("i16", 0, NS), A("rf"), op.is_equal)
+    mov(A("iw"), A("iw"), 1.0, A("rf"))
+    mov(A("ths"), A("iw", 0, 18), -1.0, 143.0)
+    mov(A("thl"), A("iw", 0, 6), 1.0, 1.0)
     for t in range(R):
-        quant(A("lq", 224 * t + NL, 224 * t + 224), A("ls", 512 * t + C, 512 * t + 512), A("zero", 0, 512))
-    quant(A("qj"), A("ss", 0, 256), A("zero"))
+        quant(A("lq", 224 * t + NL, 224 * t + 224), A("ls", 512 * t + C, 512 * t + 512), A("zero"))
     quant(A("qo"), A("so"), A("bo2"))
     for k in range(2):
         quant(A("qe", 256 * k, 256 * k + 256), A("se", 256 * k, 256 * k + 256), A("et", 1024 * k, 1024 * k + 1024))
@@ -327,47 +516,84 @@ def rank_program(g, core, T, topo):
     for t in range(R):
         last = t == R - 1
         if t == 0:
-            scan(A("cum"), A("un"), A("un"), op.add, op.max)
-            scan(A("cap"), A("cm"), A("cum"), op.max, op.min)
-            cp(A("cw"), A("cap", 15, C, 16))
-            invert("ow", 1, "mo", "po", "cw", "cum", "kb", -1.0, 0)
+            parts = [(0, C, 0, M, A("twf"))]
         else:
-            for (a, b) in ((0, NS), (NS, C)):
-                scan(A("cum", a, b), A("un", a, b), A("un", a, b), op.add, op.max, col("cum", a - 1) if a else 0.0)
-                scan(A("cap", a, b), A("cm", a, b), A("cum", a, b), op.max, op.min)
-                cp(A("cw", a // 16, b // 16), A("cap", a + 15, b, 16))
-                mov(A("mo", a, b), ind(A("cm2"), A("cw", a // 16, b // 16)))
-                scan(A("po", a + 1, b + 1), A("mo", a, b), A("iob", a, b), op.max, op.min, col("po", a) if a else -192.0)
-            invert("ow", 1, None, "po", "cw", "cum", "kb", -1.0, 0)
-        ow = A("ow", 0, 12)
-        mov(A("dr"), ind(A("d"), ow))
-        tt(A("dm"), ind(A("d"), ow), A("cm", 0, M), op.min)
-        scan(A("dh"), A("keep", 0, M), A("dm"), op.mult, op.add)
-        for c in range(8, 12):
-            act(A("sg", c % 4, 512, 4), A("dr", 0, 128), fn.Sign, col("dh", 16 * c + 15), -1.0)
-        act(A("fl", 8 * M, 8 * M + 512), A("sg"), fn.Relu, 0.0, -1.0)
-        for c in range(12):
-            base, k, k0 = 4 * M * (c // 4) + c % 4, 16 * c + 16, 128 if c >= 8 else 0
-            ts(A("fl", base + 4 * k0, base + 4 * k - 3, 4), A("dr", k0, k), col("dh", k - 1), op.is_gt)
-            if k < M:
-                ts(A("fl", base + 4 * k, base + 4 * M - 3, 4), A("dr", k, M), col("dh", k - 1), op.is_ge)
-        tt(A("fl", 12 * M, 16 * M, 4), A("dh"), A("dr"), op.is_equal)
-        for s in range(2):
-            quant(A("qf", 2 * M * s, 2 * M * s + 2 * M), A("sf", 2 * M * s, 2 * M * s + 2 * M), A("fl", 8 * M * s, 8 * M * s + 8 * M))
-        for s in range(4):
-            mm(bank(2, 0, M), A("qo"), A("so"), A("qf", M * s, M * s + M), A("sf", M * s, M * s + M), s == 0, s == 3)
-        ts(A("lv", 1, 1 + M), bank(2, 0, M), 48.5, op.is_le, 512.0, op.mult)
-        mov(A("ct"), ind(A("cum"), A("twf")))
-        tt(A("ctm"), ind(A("ct"), ow), A("cm", 0, M), op.min)
-        scan(A("cth"), A("keep", 0, M), A("ctm"), op.mult, op.add)
-        cp(A("ctw"), A("cth", 15, M, 16))
-        for p in range(4):
-            ts(A("ow4", 16 * p, 16 * p + 16), ind(A("po", 0, C + 1), A("bw", 0, 1)), 4.0, op.mult, 768.0 + p, op.add)
-            mov(A("xo", PL * p + 1, PL * p + 1 + M), ind(A("xi"), A("ow4", 16 * p, 16 * p + 12)), 0.5)
+            parts = [(0, NS, 0, MS, A("twf", 0, 18)), (NS, C, MS, M, A("arr", 16 * t - 16, 16 * t - 10))]
+        for s, (a, b, ka, kb, twin) in enumerate(parts):
+            un, n = A("un", a, b), (kb - ka) // 16
+            scan(A("cum", a, b), un, un, op.add, op.max, float(ka))
+            ow = A("ow", 16 * s, 16 * s + n)
+            if s:
+                for c in range(n):
+                    act(A("junk", C + NL * c, C + NL * c + NL), A("cum", a, b), fn.Sign, col("kb", 7 + c), -1.0, col("acc", 1 + c))
+                ts(ow, A("acc", 1, 1 + n), 0.5, op.mult, NL / 2, op.add)
+                for p in range(4):
+                    ts(A("ow4", 64 + 16 * p, 64 + 16 * p + n), A("acc", 1, 1 + n), 2.0, op.mult, 2.0 * NL + p, op.add)
+            else:
+                scan(A("yo", a + 1, b + 1), un, un, op.add, op.max, col("kb", 4))
+                steps("yo", "mo", "po", a, b)
+                where(0, "cum", a, b - 1, 0, -1.0, a, 0)
+                at = ind(A("po", a, b), col("bw", 0))
+                ts(A("ow", 0, 16), at, 32.0, op.mult, 191.0, op.add)
+                for p in range(4):
+                    if OPT["ow4"]:
+                        mov(A("owf", 16 * p, 16 * p + 16), at, 128.0, 4.0 * 191 + p)
+                    else:
+                        ts(A("ow4", 16 * p, 16 * p + 16), at, 128.0, op.mult, 4.0 * 191 + p, op.add)
+                if OPT["ow4"]:
+                    cp(A("ow4", 0, 64), A("owf"))
+            scan(A("cap", a, b), A("cm", a, b), A("cum", a, b), op.max, op.min)
+            cp(A("cw", a // 16, b // 16), A("cap", a + 15, b, 16))
+            mov(A("dr", ka, kb), ind(A("d", a, b), ow))
+            if OPT["dm"] and not s:
+                scan(A("dm", ka, kb), A("dr", ka, kb), A("cm", ka, kb), op.max, op.min)
+            else:
+                tt(A("dm", ka, kb), ind(A("d", a, b), ow), A("cm", ka, kb), op.min)
+            scan(A("dh", ka, kb), A("keep", ka, kb), A("dm", ka, kb), op.mult, op.add)
+            mov(A("ct", a, b), ind(A("cum", a, b), twin))
+            if OPT["ctm"] and not s:
+                mov(A("cto", ka, kb), ind(A("ct", a, b), ow))
+                scan(A("ctm", ka, kb), A("cto", ka, kb), A("cm", ka, kb), op.max, op.min)
+            else:
+                tt(A("ctm", ka, kb), ind(A("ct", a, b), ow), A("cm", ka, kb), op.min)
+            scan(A("cth", ka, kb), A("keep", ka, kb), A("ctm", ka, kb), op.mult, op.add)
+            cp(A("ctw", ka // 16, kb // 16), A("cth", ka + 15, kb, 16))
+            for p in range(4):
+                o4, lo, hi = 64 * s + 16 * p, PL * p + 1 + ka, PL * p + 1 + kb
+                src = ind(A("xi", 4 * a, 4 * b), A("ow4", o4, o4 + n))
+                mov(A("xo", lo, hi), src, 0.5)
+                if s:
+                    mov(A("xa", lo, hi), src, 0.5)
+                else:
+                    mov(A("xa", lo, hi), A("xo", lo, hi), pool=True)
+        if t == 0:
+            names, h = ("f0", "q0", "s0"), M - MS
+            calls = [[(0, 0, M, [0, 1, 2, 3]), (M, 0, M, [4, 5, 6, 7])], [(2 * M, 0, M, [8, 9, 10, 11]), (3 * M, 0, M, [12])]]
+            by_s = [{}, {c: 128 for c in OPT["s0"]}]
+        else:
+            names, h = ("fl", "qf", "sf"), M - MS
+            calls = [[(MS, 0, MS, [0, 1, 2, 3]), (2 * MS, 0, MS, [4, 5, 6, 7]), (3 * MS, 0, MS, [8, 12])],
+                     [(0, MS, M, [0, 1, 2, 3]), (h, MS, M, [4, 5, 6, 7]), (2 * h, MS, M, [8])],
+                     [(4 * MS, MS, M, [9, 10, 11, 12]), (4 * MS + h, 0, MS, [9, 10, 11])]]
+            by_s = [{c: MS for c in OPT["s1"]}, {}, {c: MS for c in OPT["s2"]}]
+        every = [x for tiles in calls for x in tiles]
+        for tiles, on_s in zip(calls, by_s):
+            compare(names[0], tiles, on_s)
+            lo, hi = tiles[0][0], tiles[-1][0] + tiles[-1][2] - tiles[-1][1]
+            quant(A(names[1], lo, hi), A(names[2], lo, hi), A(names[0], 4 * lo, 4 * hi))
+            for x in tiles:
+                mine, wide = [y for y in every if y[1] == x[1]], max(128, x[2] - x[1])
+                mm(bank(2 + (x[1] > 0), 0, wide), A("qo"), A("so"), A(names[1], x[0], x[0] + wide), A(names[2], x[0], x[0] + wide),
+                   x == mine[0], x == mine[-1])
+        for (a, b, ka, kb, twin) in parts:
+            out, cnt = A("lv", 1 + ka, 1 + kb), bank(2 + (ka > 0), 0, kb - ka)
+            if OPT["g1"]:
+                act(out, cnt, fn.Sign, 48.5, -1.0)
+            else:
+                add({"v": tsv(out, cnt, 48.5, op.is_le), "s": acs(out, cnt, fn.Relu, 49.0, -1.0)}, [cnt], [out])
+        mov(A("xa", 0, 4 * PL, PL), A("xo", M, 4 * PL, PL))
         mov(A("xo", 0, 4 * PL, PL), A("xo", M, 4 * PL, PL))
         for p in range(4):
-            if p % 2 == 0:
-                mov(A("xa", PL * p, PL * p + PL + M), A("xo", PL * p, PL * p + PL + M))
             tt(A("z", p, 4 * M, 4), ind(A("xo", PL * p, PL * p + M + 1), A("ctw")), A("xa", PL * p, PL * p + M), op.add)
         quant(A("qz"), A("sz"), A("z"))
         for p in range(4):
@@ -376,55 +602,84 @@ def rank_program(g, core, T, topo):
         mov(A("hx", 0, 4 * PL, PL), A("hx", M, 4 * PL, PL))
         for p in range(4):
             tt(A("e", C * p, C * p + C), ind(A("hx", PL * p, PL * p + M + 1), A("cw")), A("xi", p, 4 * C, 4), op.add)
-        tt(A("g1"), ind(A("lv", 0, M + 1), A("cw")), A("un"), op.mult)
+        if OPT["g1"]:
+            scan(A("lk", 1, M + 1), A("lv", 1, M + 1), A("ones", 0, M), op.add, op.add)
+            for k in range(2):
+                mov(A("gk", 1 + M * k, 1 + M * k + M), ind(A("lk", 0, M + 1), A("cw", 12 * k, 12 * k + 12)), 0.5)
+            scan(A("g1"), A("gk", 1, C + 1), A("gk", 0, C), op.max, op.subtract)
+        else:
+            tt(A("g1"), ind(A("lv", 0, M + 1), A("cw")), A("un"), op.min)
         halves("g2", A("g1"), "twf")
-        mov(A("g2p"), A("g1"), bias=-512.0)
         scan(A("gn"), A("g1"), A("g2"), op.add, op.add)
-        scan(A("ncs"), A("g2"), A("g2p"), op.add, op.add, 512.0 * 144)
-        scan(A("capg"), A("cm"), A("gn"), op.max, op.min)
-        ts(A("gw"), A("capg", 15, C, 16), 1.0 / 512, op.mult)
-        ts(A("sw"), A("capg", 15, C, 16), -1.0 / 512, op.mult, A("r97"), op.add)
-        invert("lw", 1, "mg", "pg", "gw", "gn", "kb", -1.0 / 512, 1)
-        invert("qw", 2, "mq", "pq", "sw", "ncs", "kq", 1.0 / 512, 2)
+        scan(A("yg", 1, C + 1), A("g1"), A("g2"), op.add, op.add, col("kb", 4))
+        steps("yg", "mg", "pg", 0, C)
+        where(4, "gn", 0, C - 1, 0, -1.0, 0, 2)
+        ts(A("lw"), ind(A("pg"), col("bw", 4)), 32.0, op.mult, 191.0, op.add)
+        if OPT["g1m"]:
+            mov(A("g1m"), A("g1"), 1.0, -1.0)
+            scan(A("ncs"), A("g1m"), A("g2"), op.add, op.add, float(MS))
+            scan(A("yq", 1, C + 1), A("g1m"), A("g2"), op.add, op.add, col("kb", 5))
+        else:
+            scan(A("ncs", 0, MS), A("gn", 0, MS), A("rev", 0, MS), op.min, op.add, 256.0)
+            scan(A("ncs", MS, C), A("gn", MS, C), A("rev", MS, C), op.max, op.add)
+            mov(A("yq", 1, C + 1), A("ncs"), 1.0, col("kb", 6))
+        steps("yq", "mq", "pq", 0, C, False)
+        where(6, "ncs", 0, 351, 2, 1.0, 0, 3)
+        where(7, "ncs", 256, C - 1, 3, 1.0, 0, 4)
+        ts(A("qw"), ind(A("pq"), A("bw", 6, 8)), 32.0, op.mult, 191.0, op.add)
         lw, qw = A("lw", 0, 6), A("qw", 0, 18)
         for p in range(4):
             mov(A("sl", 128 + p, 512, 4), ind(A("e", C * p, C * p + C), lw))
-        quant(A("qs"), A("ss", 256, C), A("sl"))
+        quant(A("qs"), A("s0", 4 * M, 4 * M + 128), A("sl"))
         dst = T.cores[(rank + STEP[t]) % n_ranks]
         rid, pid = topo.addr(dst)[:2]
         eng = topo.engines(core, dst)
         half = len(eng) // 2
         m0, m1 = sum(1 << k for k in eng[:half]), sum(1 << k for k in eng[half:])
+        scales = A("s0", 4 * M + 128 - C, 4 * M + 128)
 
-        def send_codes(t=t, rid=rid, pid=pid, m0=m0, m1=m1):
+        def send_codes(t=t, rid=rid, pid=pid, m0=m0, m1=m1, scales=scales):
             to = [DstId(rid=rid, pnc=pid)]
             return g.remote_dma_fused([
                 RemoteDMATransfer(dst_ids=to, dma_engine_mask=m0, remote_sem=T.sem["ac%d" % t],
                                   src=real(cast(A("qs", 32, 128), dt.uint8)), dst=real(cast(A("lq", 224 * t, 224 * t + NL), dt.uint8))),
                 RemoteDMATransfer(dst_ids=to, dma_engine_mask=m1, remote_sem=T.sem["ac%d" % t],
-                                  src=real(A("ss")), dst=real(A("ls", 512 * t, 512 * t + C)))], local_sem=T.sem.lc)
+                                  src=real(scales), dst=real(A("ls", 512 * t, 512 * t + C)))], local_sem=T.sem.lc)
 
-        j = add({"g": (send_codes, OPT["issue"])}, [A("qs", 32, 128), A("ss")], [], kind="r", sem="lc", cnt=2 * half, lat=OPT["rem"])
+        j = add({"g": (send_codes, OPT["issue"])}, [A("qs", 32, 128), scales], [], kind="r", sem="lc", cnt=2 * half, lat=OPT["rem"])
         add({"x": (None, 0.0)}, [], [A("lq", 224 * t, 224 * t + NL), A("ls", 512 * t, 512 * t + C)], kind="x",
             sem="ac%d" % t, cnt=2 * half, after=[j])
-        wide = 6 if last else 12
-        arr, arh, land, snd = A("arr", 16 * t, 16 * t + 6), A("arr", 16 * t + 6, 16 * t + 12), A("arr", 16 * t, 16 * t + wide), A("snd", 0, wide)
+        arr, arh = A("arr", 16 * t, 16 * t + 6), A("arr", 16 * t + 6, 16 * t + 12)
+        land, snd = (A("lrow"), A("srow")) if last else (A("arr", 16 * t, 16 * t + 12), A("snd", 0, 12))
         mov(A("t1"), ind(A("gn"), A("twf")))
         mov(A("t2"), ind(A("ncs"), A("twf")))
-        tt(A("nm", NS, C), ind(A("t1"), lw), A("cm", 0, NL), op.min)
-        scan(A("nh", NS, C), A("keep", 0, NL), A("nm", NS, C), op.mult, op.add)
-        ts(A("snd", 0, 6), A("nh", NS + 15, C, 16), 1.0 / 512, op.mult, -1.0, op.add)
-        if not last:
+        if last:
+            mov(snd, ind(A("t1"), lw), 1.0, NS - 1.0)
+        else:
+            if OPT["nm"]:
+                mov(A("nr", NS, C), ind(A("t1"), lw))
+                scan(A("nm", NS, C), A("nr", NS, C), A("cm", 0, NL), op.max, op.min)
+            else:
+                tt(A("nm", NS, C), ind(A("t1"), lw), A("cm", 0, NL), op.min)
+            scan(A("nh", NS, C), A("keep", 0, NL), A("nm", NS, C), op.mult, op.add)
+            ts(A("snd", 0, 6), A("nh", NS + 15, C, 16), -1.0, op.add)
             tt(A("hf", 18, 24), A("nh", NS + 15, C, 16), A("thl"), op.is_lt)
             cp(A("snd", 6, 12), A("hf", 18, 24))
         j = add({"g": (lambda t=t, rid=rid, pid=pid, m=m0 | m1, land=land, snd=snd: g.remote_dma(
             real(land), real(snd), T.sem["al%d" % t], T.sem.ll, pid, rid, m), OPT["issue"])},
             [snd], [], kind="r", sem="ll", cnt=2 * half, lat=OPT["rem"])
         add({"x": (None, 0.0)}, [], [land], kind="x", sem="al%d" % t, cnt=2 * half, after=[j])
-        tt(A("nm", 0, NS), ind(A("t2"), qw), A("cm1", 0, NS), op.mult)
-        scan(A("nh", 0, NS), A("keep", 0, NS), A("nm", 0, NS), op.mult, op.add)
-        ts(A("twf", 0, 18), A("nh", 15, NS, 16), -1.0 / 512, op.mult, 143.0, op.add)
-        ts(A("twf", 18, 24), arr, float(NS), op.add)
+        if last:
+            mov(A("otr"), ind(A("t2"), qw), -1.0, 143.0)
+        else:
+            if OPT["nm"]:
+                mov(A("nr", 0, NS), ind(A("t2"), qw))
+                scan(A("nm", 0, NS), A("nr", 0, NS), A("cm1", 0, NS), op.add, op.mult)
+            else:
+                tt(A("nm", 0, NS), ind(A("t2"), qw), A("cm1", 0, NS), op.mult)
+            scan(A("nh", 0, NS), A("keep", 0, NS), A("nm", 0, NS), op.mult, op.add)
+            ts(A("twf", 0, 18), A("nh", 15, NS, 16), -1.0, op.mult, 143.0, op.add)
+            ts(A("twf", 18, 24), arr, float(NS), op.add)
         for p in range(4):
             mov(A("xi", p, 4 * NS, 4), ind(A("e", C * p, C * p + C), qw))
         quant(A("qx", 0, NS), A("sx", 0, NS), A("xi", 0, 4 * NS))
@@ -432,35 +687,44 @@ def rank_program(g, core, T, topo):
             mm(bank(4 + p, 0, 128), A("qe", 128 * p, 128 * p + 128), A("se", 128 * p, 128 * p + 128),
                A("lq", 224 * t, 224 * t + 128), A("ls", 512 * t + NS, 512 * t + NS + 128))
             mov(A("xi", 4 * NS + p, 4 * C, 4), bank(4 + p, 0, NL))
-        quant(A("qb"), A("sq"), A("xi", 4 * 256, 4 * C))
+        quant(A("qb"), A("sq"), A("xi", 4 * NS, 4 * NS + 512))
         if last:
             mm(bank(0, 0, NS), A("qv"), A("sv"), A("qx", 0, NS), A("sx", 0, NS))
-            mov(A("yo", 0, NS), bank(0, 0, NS))
+            mov(A("yr", 0, NS), bank(0, 0, NS))
             mm(bank(1, 0, 128), A("qv"), A("sv"), A("qb"), A("sq"))
-            mov(A("yo", NS, C), bank(1, 32, NL))
+            mov(A("yr", NS, C), bank(1, 0, NL))
             dma("y", T.oc[:, 0:4 * NS], real(cast(A("qx", 0, NS), dt.uint8)), [A("qx", 0, NS)], [], 144)
             for k in range(4):
                 dma("y", T.osc[4 * k:4 * k + 4, 0:NS], T.sx[32 * k:32 * k + 4, 0:NS], [A("sx", 0, NS)], [])
-            dma("y", T.y[:, 0:NS], real(A("yo", 0, NS)), [A("yo", 0, NS)], [], 144)
-            dma("y", T.oc[:, 4 * NS:4 * C], real(cast(A("qb", 32, 128), dt.uint8)), [A("qb")], [], 48)
+            dma("y", T.y[:, 0:NS], real(A("yr", 0, NS)), [A("yr", 0, NS)], [], 144)
+            dma("y", T.oc[:, 4 * NS:4 * C], real(cast(A("qb", 0, NL), dt.uint8)), [A("qb")], [], 48)
             for k in range(4):
-                dma("y" if k < 2 else "s", T.osc[4 * k:4 * k + 4, NS:C], T.sq[32 * k:32 * k + 4, 32:128], [A("sq")], [])
-            dma("s", T.y[:, NS:C], real(A("yo", NS, C)), [A("yo", NS, C)], [], 48)
-            halves("otr", A("io1"), "twf", bias=-1.0)
-            dma("y", T.ot[:], T.otr[0:128:16, :], [A("otr")], [])
+                dma("y" if k < 2 else "s", T.osc[4 * k:4 * k + 4, NS:C], T.sq[32 * k:32 * k + 4, 0:NL], [A("sq")], [])
+            dma("s", T.y[:, NS:C], real(A("yr", NS, C)), [A("yr", NS, C)], [], 48)
+            dma("y", T.ot[:, 0:NS], T.otr[0:128:16, :], [A("otr")], [])
+            dma("y", T.ot[:, NS:C], T.lrow[0:128:16, :], [A("lrow")], [])
         else:
             mm(bank(0, 0, NS), A("qu2"), A("su2"), A("qx", 0, NS), A("sx", 0, NS))
             mov(A("sr", 0, NS), bank(0, 0, NS))
             mm(bank(1, 0, 128), A("qu2"), A("su2"), A("qb"), A("sq"))
-            mov(A("sr", NS, C), bank(1, 32, NL))
+            mov(A("sr", NS, C), bank(1, 0, NL))
             tt(A("hf", 0, 18), A("nh", 15, NS, 16), A("ths"), op.is_gt)
             cp(A("hw", 0, 18), A("hf", 0, 18))
-            mov(A("st", 0, 160), ind(A("sr", 0, NS), A("twf", 0, 10)))
-            mov(A("st", 160, NS), ind(A("sr", 0, NS), A("twf", 10, 18)))
-            mm(bank(3, 0, 128), A("qu2"), A("su2"), A("qb"), A("sq"))
-            mov(A("sr2"), bank(3, 32, NL))
-            tt(A("d", 0, NS), A("st", 0, NS), bank(0, 0, NS), op.subtract)
-            tt(A("d", NS, C), ind(A("sr", NS, C), arr), A("sr2"), op.subtract)
+            if OPT["d0"]:
+                mm(bank(2, 0, NS), A("qu2"), A("su2"), A("qx", 0, NS), A("sx", 0, NS))
+                mov(A("st", 0, NS), bank(2, 0, NS))
+                tt(A("d", 0, NS), ind(A("sr", 0, NS), A("twf", 0, 18)), A("st", 0, NS), op.subtract)
+            else:
+                mov(A("st", 0, 160), ind(A("sr", 0, NS), A("twf", 0, 10)))
+                mov(A("st", 160, NS), ind(A("sr", 0, NS), A("twf", 10, 18)))
+                tt(A("d", 0, NS), A("st", 0, NS), bank(0, 0, NS), op.subtract)
+            if OPT["d1"]:
+                mm(bank(3, 0, 128), A("qu2"), A("su2"), A("qb"), A("sq"))
+                mov(A("st", NS, C), bank(3, 0, NL))
+                tt(A("d", NS, C), ind(A("sr", NS, C), arr), A("st", NS, C), op.subtract)
+            else:
+                mov(A("st", NS, C), ind(A("sr", NS, C), arr))
+                tt(A("d", NS, C), A("st", NS, C), bank(1, 0, NL), op.subtract)
             tt(A("un", 0, NS), ind(A("tie", 0, 2), A("hw", 0, 18)), A("d", 0, NS), op.is_lt)
             tt(A("un", NS, C), ind(A("tie", 0, 2), arh), A("d", NS, C), op.is_lt)
 
@@ -468,7 +732,7 @@ def rank_program(g, core, T, topo):
     if "plan" not in OPT:
         OPT["plan"] = plan(ops)
     for i in range(n):
-        ops[i]["q"], ops[i]["start"] = OPT["plan"][i]
+        ops[i]["q"], ops[i]["start"] = OPT["plan"][i][:2]
     order = sorted(range(n), key=lambda k: (ops[k]["start"], k))
 
     ops.append({"q": "g", "alts": {"g": (None, 0.0)}, "deps": set(j for j in range(n) if ops[j]["kind"] != "c"), "kind": "e"})

@@ -1,3 +1,4 @@
+import math
 import numpy as np
 from concourse.bass import DstId, RemoteDMATransfer
 from concourse.mybir import dt, AluOpType, ActivationFunctionType
@@ -6,18 +7,20 @@ C, M, NL, NS, R = 384, 192, 96, 288, 3
 MS = NS // 2
 STEP = [1, 2, 4]
 PL = 208
+DUP = 8
 BIG = 2.0 ** 80
 EPS = 2.0 ** -110
 LEV = 3072.0
-OPT = {"cy": 0.85, "ga": 1.15, "dep": 190.0, "sfix": 40.0, "dma": 2000.0, "rem": 3000.0, "issue": 600.0,
-       "moves": 60000, "heat": 0.001,
-       "fine": [(1.0, 1.15, 190.0, 0.0, 0.0, 0.0, 0.0), (1.22, 1.3, 100.0, -500.0, -1000.0, -100.0, 0.0),
-                (1.42, 1.6, 120.0, 0.0, -500.0, 0.0, 0.0), (1.1, 0.95, 150.0, -1000.0, -1500.0, -200.0, 20.0)],
-       "tries": 300, "tied": 0.7, "pm": 0.015, "whi": 8.0, "pen0": 2.0, "seed": 0,
-       "sets": [(1.0, 0.0, 0.0, 0.0), (1.0, -80.0, 2000.0, 0.0), (1.4, 0.0, 0.0, 0.0), (1.15, -100.0, 0.0, 35.0)],
+OPT = {"cy": 0.83, "ga": 1.15, "dep": 240.0, "sfix": 0.0, "dma": 1100.0, "rem": 1500.0, "rem0": 500.0, "issue": 700.0,
+       "fine": [(1.07, 1.25, 265.0, 50.0, 0.0, 200.0, 100.0, 3.0, 20.0), (1.04, 1.0, 220.0, 50.0, 100.0, -200.0, 100.0, 5.0, 15.0),
+                (1.28, 1.35, 280.0, 280.0, 200.0, 300.0, 100.0, 8.0, 25.0)],
+       "tries": 300, "pm": 0.015, "whi": 8.0, "pen0": 0.5, "seed": 1,
+       "moves": 90000, "heat": 0.0018, "reach": 3.0, "flat": 0.15, "near": 300.0, "every": 20, "loose": 0.002,
+       "anew": 0.1, "wide": 35, "noise": 600.0, "lean": 1.5, "look": 100.0, "price": 0.0,
        "w0": {"e'": 4.0, "z'": 4.0, "xo": 4.0, "sl": 3.0, "xi": 2.0, "fl": 5.0, "f0": 5.0, "hx": 2.0},
-       "s0": [], "s1": [], "s2": [9, 10, 11], "ctm": 1, "nm": 1, "ow4": 1, "g1": 0, "g1m": 0, "dm": 0, "d0": 0, "d1": 1,
-       "every": 50}
+       "s0": [7, 8, 9, 10, 11], "s1": [], "s2": [9, 10, 11], "ctm": 1, "nm": 1, "dm": 0,
+       "se": 0, "sx": 1, "su": 1, "yg": 0, "split": 1, "xc": 2, "xa": 1, "zc": 2, "s0w": 192, "zero": 1, "es": [], "d1": 1, "join": 0,
+       "since": 260.0, "tm": 0, "jv": []}
 
 
 def sb(n, d):
@@ -33,25 +36,27 @@ SCRATCH = {
     "qv": sb(128, X4), "sv": sb(128, U8), "wq": sb(512, X4), "wp": sb(512, U8),
     "ones": sb(512, B), "et": sb(2048, B), "qe": sb(512, X4), "se": sb(512, U8),
     "bo1": sb(512, B), "bo2": sb(512, B), "qo": sb(128, X4), "so": sb(128, U8), "zero": sb(512, B),
-    "uli": sb(8, I), "ul": sb(8, U16), "pi": sb(1, I), "ri": sb(1, I), "rf": sb(1, F), "kb": sb(10, F),
-    "iob": sb(C, B), "pos": sb(C, B), "rev": sb(C, B), "i16": sb(C, B), "cm": sb(C, B), "cm1": sb(C, B), "keep": sb(C, B),
-    "tie": sb(16, F), "iw": sb(24, F), "ths": sb(18, F), "thl": sb(6, F), "hf": sb(24, F), "hw": sb(24, U16),
+    "uli": sb(8, I), "ul": sb(8, U16), "pi": sb(1, I), "ri": sb(3, I), "rf": sb(3, F), "kb": sb(14, F), "kn": sb(2, F), "tally": sb(C, B),
+    "lr": sb(M, B), "lm": sb(NL, B), "lh": sb(M, B), "l4": sb(48, U16), "xl": sb(C, B),
+    "i4": sb(M, B), "cm4": sb(M, B), "cm4n": sb(M, B), "keep4": sb(M, B), "orow": sb(M, B), "oh": sb(M, B),
+    "iob": sb(C, B), "pos": sb(C, B), "i16": sb(C, B), "cm": sb(C, B), "cm1": sb(C, B), "keep": sb(C, B),
+    "tie": sb(16, F), "iw": sb(24, F), "ths": sb(24, F), "hf": sb(24, F), "hw": sb(24, U16),
     "sr": sb(C, F), "st": sb(C, F), "d": sb(C, F), "un": sb(C, B), "cum": sb(C, B),
-    "twf": sb(24, U16), "arr": sb(16 * R, U16), "snd": sb(16, U16), "srow": sb(NL, F), "lrow": sb(NL, F),
-    "junk": sb(5 * C, B), "acc": sb(8, F), "bw": sb(8, U16),
+    "twf": sb(48 * R, U16), "srow": sb(NL, F), "lrow": sb(NL, F),
+    "junk": sb(5 * C, B), "acc": sb(12, F), "bw": sb(8, U16),
     "yo": sb(C + 8, B), "yg": sb(C + 8, B), "yq": sb(C + 8, B), "mo": sb(C, B), "mg": sb(C, B), "mq": sb(C, B),
     "po": sb(C, B), "pg": sb(C, B), "pq": sb(C, B),
-    "cto": sb(M, B), "xa": sb(4 * PL, B), "lk": sb(PL, B), "gk": sb(C + 8, B), "nr": sb(C, B),
-    "g1m": sb(C, B), "ow": sb(32, U16), "owf": sb(64, F), "ow4": sb(128, U16), "lw": sb(16, U16), "qw": sb(32, U16),
+    "cto": sb(M, B), "xa": sb(4 * PL, B), "nr": sb(C, B),
+    "ow": sb(32, U16), "ow4": sb(48, U16), "lqw": sb(48, U16),
     "cap": sb(C, B), "cw": sb(24, U16),
     "dm": sb(M, F), "dh": sb(M, F), "dr": sb(M, F), "sg": sb(8 * M, B),
     "f0": sb(16 * M, B), "q0": sb(4 * M, X4), "s0": sb(4 * M + 128, U8),
     "fl": sb(16 * M, B), "qf": sb(4 * M, X4), "sf": sb(4 * M, U8),
-    "ct": sb(C, B), "ctm": sb(M, B), "cth": sb(M, B), "ctw": sb(12, U16),
-    "xo": sb(4 * PL, B), "z": sb(4 * M, B), "qz": sb(M, X4), "sz": sb(M, U8), "hx": sb(4 * PL, B),
-    "lv": sb(PL, B), "g1": sb(C, B), "g2": sb(C, B), "gn": sb(C, B), "ncs": sb(C, B), "e": sb(4 * C, B),
+    "ct": sb(C, B), "ctm": sb(M, B), "cth": sb(M, B), "ctw": sb(48, U16),
+    "xo": sb(4 * PL, B), "z": sb(4 * (M + DUP), B), "qz": sb(M + DUP, X4), "sz": sb(M + DUP, U8), "hx": sb(4 * PL, B),
+    "lv": sb(PL, B), "g1": sb(C, B), "g2": sb(C, B), "gn": sb(C, B), "ncs": sb(C, B), "e": sb(5 * C, B),
     "sl": sb(512, B), "qs": sb(128, X4), "lq": sb(R * 224, X4), "ls": sb(R * 512, U8),
-    "t1": sb(C, B), "t2": sb(C, B), "nm": sb(C, B), "nh": sb(C, B),
+    "tn": sb(2 * C, B), "nm": sb(C, B), "nh": sb(C, B),
     "yr": sb(C, F), "otr": sb(NS, F),
 }
 POOL = {"v": 56, "s": 36, "t": 10, "g": 10}
@@ -67,9 +72,6 @@ def plan(ops):
     least = [min(c for (_, c) in o["alts"].values()) for o in ops]
     alts = [[(q, o["alts"][q][1]) for q in o["alts"]] for o in ops]
     lat = [o["lat"] for o in ops]
-    comp = [o["kind"] == "c" for o in ops]
-    pres = [[[(j, d + more + (far if ops[j]["kind"] == "r" else 0.0) if d else 0.0) for (j, d) in pre[i]] for i in range(n)]
-            for (f, more, far, fix) in OPT["sets"]]
 
     def once(w, pen):
         w, pen = w.tolist(), pen.tolist()
@@ -96,22 +98,9 @@ def plan(ops):
                 score = at + cost + (pen[i] * cost if q == "v" else 0.0)
                 if best is None or score < best[0]:
                     best = (score, q, at, cost, k)
-            res[i], end[i] = (best[1], best[2], best[3]), best[2] + best[3]
+            res[i], end[i] = (best[1], best[2]), best[2] + best[3]
             busy[best[1]].insert(best[4], (best[2], end[i]))
-        seq, span = sorted(range(n), key=lambda k: (res[k][1], k)), 0.0
-        for s, (f, more, far, fix) in enumerate(OPT["sets"]):
-            free, fin, last = {q: 0.0 for q in busy}, [0.0] * n, 0.0
-            for i in seq:
-                q = res[i][0]
-                at = free[q]
-                for (j, d) in pres[s][i]:
-                    if fin[j] + d > at:
-                        at = fin[j] + d
-                free[q] = fin[i] = at + res[i][2] * (f if comp[i] else 1.0) + fix
-                if fin[i] + lat[i] > last:
-                    last = fin[i] + lat[i]
-            span += last / f
-        return span, res
+        return max(end[i] + lat[i] for i in range(n)), res
 
     w, pen = np.array([OPT["w0"].get(o["key"][3:5], 1.0) for o in ops]), np.full(n, OPT["pen0"])
     top, res = once(w, pen)
@@ -119,10 +108,9 @@ def plan(ops):
     same = np.array([names.index(o["key"]) for o in ops])
     for it in range(OPT["tries"]):
         w2, pen2 = w.copy(), pen.copy()
-        ids = same if it < OPT["tied"] * OPT["tries"] else np.arange(n)
         for arr, lo, hi in ((w2, 0.05, OPT["whi"]), (pen2, -1.0, 4.0)):
             k, val = rng.random(n) < OPT["pm"], rng.uniform(lo, hi, n)
-            arr[k[ids]] = val[ids][k[ids]]
+            arr[k[same]] = val[same][k[same]]
         span, r = once(w2, pen2)
         if span <= top:
             top, res, w, pen = span, r, w2, pen2
@@ -131,6 +119,7 @@ def plan(ops):
 
 def refine(ops, seq, on):
     n, sets = len(ops), OPT["fine"]
+    ns = len(sets)
     rng = np.random.default_rng(OPT["seed"])
     above, pre = [0] * n, []
     for i, o in enumerate(ops):
@@ -141,125 +130,260 @@ def refine(ops, seq, on):
             hard |= above[j]
         above[i] = hard | sum(1 << j for j in o["deps"] | o["soft"])
         pre.append(mine)
-    post = [[] for _ in range(n)]
-    for i in range(n):
-        for j in pre[i]:
-            post[j].append(i)
-    edge, cost, tail = [], [], []
-    for (f, ga, dep, local, far, issue, fix) in sets:
+    edge, back, cost, wake, soon = [], [], [], [], []
+    for (f, ga, dep, early, local, far, issue, fix, more) in sets:
         lat = [o["lat"] + {"d": local, "r": far}.get(o["kind"], 0.0) for o in ops]
-        edge.append([[(j, 0.0 if j in ops[i]["soft"] and ops[i]["kind"] != "x" else lat[j] + dep) for j in pre[i]] for i in range(n)])
-        cost.append([{q: (f * (o["alts"][q][1] + (ga - OPT["ga"]) * o["gath"]) + fix if o["kind"] == "c" else
-                          o["alts"][q][1] + (issue if o["kind"] == "r" else 0.0)) for q in o["alts"]} for o in ops])
-        tail.append(lat)
-
-    def replay(s, seq, on, first, fin):
-        free, e, c = {}, edge[s], cost[s]
-        for k in range(first - 1, -1, -1):
-            if on[seq[k]] not in free:
-                free[on[seq[k]]] = fin[seq[k]]
-                if len(free) == 6:
-                    break
-        for k in range(first, n):
-            i = seq[k]
-            q = on[i]
-            at = free.get(q, 0.0)
-            for (j, d) in e[i]:
-                x = fin[j] + d
-                if x > at:
-                    at = x
-            free[q] = fin[i] = at + c[i][q]
-        return max(fin[i] + tail[s][i] for i in ends)
-
-    def pack(s, seq, on, e):
-        busy, end, begin = {q: [] for q in "vstgyx"}, [0.0] * n, [0.0] * n
-        for i in seq:
-            at, c, line = (0.0 if e is edge[s] or post[i] else tail[s][i]), cost[s][i][on[i]], busy[on[i]]
-            for (j, d) in e[i]:
-                if end[j] + d > at:
-                    at = end[j] + d
-            k = len(line)
-            while k > 0 and line[k - 1][1] > at:
-                k -= 1
-            while k < len(line) and at + c > line[k][0]:
-                at = line[k][1]
-                k += 1
-            begin[i], end[i] = at, at + c
-            line.insert(k, (at, end[i]))
-        rank = {i: k for k, i in enumerate(seq)}
-        return sorted(seq, key=lambda i: (begin[i], rank[i]))
-
-    back = [[[] for _ in range(n)] for _ in sets]
-    for s in range(len(sets)):
+        e = [[(j, -1e6 if j in ops[i]["soft"] and ops[i]["kind"] != "x" else lat[j]) for j in pre[i]] for i in range(n)]
+        wake.append([0.0 if o["kind"] == "x" else dep for o in ops] + [0.0])
+        soon.append([0.0 if o["kind"] == "x" else early for o in ops] + [0.0])
+        b = [[] for _ in range(n + 1)]
         for i in range(n):
-            for (j, d) in edge[s][i]:
-                back[s][j].append((i, d))
-    ends = [i for i in range(n) if not post[i]]
-    fins = [[0.0] * n for _ in sets]
-    norm = [replay(s, seq, on, 0, fins[s]) for s in range(len(sets))]
-    now = best = float(len(sets))
-    keep, held = (seq, on), None
-    for it in range(OPT["moves"]):
-        if held is None:
-            s = int(rng.integers(len(sets)))
-            fin, pos, prev, last, held = fins[s], [0] * n, [None] * n, {}, []
-            for k, i in enumerate(seq):
-                pos[i], prev[i] = k, last.get(on[i])
-                last[on[i]] = i
-            i = max(ends, key=lambda k: fin[k] + tail[s][k])
-            while i is not None:
-                at, nxt = fin[i] - cost[s][i][on[i]], None
-                for (j, d) in edge[s][i]:
-                    if fin[j] + d >= at - 0.01:
-                        nxt = j
-                if nxt is None and prev[i] is not None and fin[prev[i]] >= at - 0.01:
-                    nxt = prev[i]
-                    held.append((i, nxt))
-                i = nxt
-            if not held:
-                break
-        i, j = held[int(rng.integers(len(held)))]
-        kind, seq2, on2 = rng.random(), seq, on
-        if it % OPT["every"] == 0:
-            s = int(rng.integers(len(sets)))
-            first, seq2 = 0, pack(s, pack(s, seq[::-1], on, back[s])[::-1], on, edge[s]) if rng.random() < 0.5 else pack(s, seq, on, edge[s])
-        elif kind < 0.3:
-            x = i if rng.random() < 0.5 else j
+            for (j, d) in e[i]:
+                b[j].append((i, d))
+        e.append([(i, lat[i]) for i in range(n) if not b[i]])
+        for (i, d) in e[n]:
+            b[i].append((n, d))
+        edge.append(e)
+        back.append(b)
+        cost.append([{q: (f * (o["alts"][q][1] + (ga - OPT["ga"]) * o["gath"]) + fix + (more if q == "s" else 0.0) if o["kind"] == "c" else
+                          o["alts"][q][1] + (issue if o["kind"] == "r" else 0.0)) for q in o["alts"]} for o in ops])
+    ej = np.array([j for i in range(n + 1) for (j, d) in edge[0][i]])
+    ei = np.array([i for i in range(n + 1) for (j, d) in edge[0][i]])
+    ed = [np.array([d for i in range(n + 1) for (j, d) in edge[s][i]]) for s in range(ns)]
+    wk = np.array(wake)
+    fin, rest, idle = ([[0.0] * (n + 1) for _ in sets] for _ in range(3))
+
+    def survey(seq, on, first):
+        pos, prev, nxt, seen = [n] * (n + 1), [None] * n, [None] * n, {}
+        for k, i in enumerate(seq):
+            pos[i] = k
+            j = prev[i] = seen.get(on[i])
+            if j is not None:
+                nxt[j] = i
+            seen[on[i]] = i
+        span, over, held = [], [], []
+        p = np.array(pos)
+        qi = np.array([i for i in range(n) if prev[i] is not None])
+        qj = np.array([j for j in prev if j is not None])
+        for s in range(ns):
+            f, r, e, b, c, w, y, fr = fin[s], rest[s], edge[s], back[s], cost[s], wake[s], soon[s], idle[s]
+            for k in range(first, n):
+                i = seq[k]
+                j = prev[i]
+                at, sig = 0.0 if j is None else f[j], -1e9
+                fr[i] = at - y[i]
+                for (j, d) in e[i]:
+                    if f[j] + d > sig:
+                        sig = f[j] + d
+                if sig >= at - y[i]:
+                    at = sig + w[i]
+                f[i] = at + c[i][on[i]]
+            for k in range(n - 1, -1, -1):
+                i = seq[k]
+                j = nxt[i]
+                at = 0.0 if j is None else r[j]
+                for (j, d) in b[i]:
+                    x = r[j] + d + (w[j] if f[i] + d >= fr[j] else 0.0)
+                    if x > at:
+                        at = x
+                r[i] = at + c[i][on[i]]
+            top = max(f[j] + d for (j, d) in e[n])
+            span.append(top)
+            fa, ra, ia = np.array(f), np.array(r), np.array(fr)
+            sig = fa[ej] + ed[s]
+            late = sig >= ia[ei]
+            val, val2 = sig + np.where(late, wk[s][ei], 0.0) + ra[ei], fa[qj] + ra[qi]
+            a, z = np.flatnonzero(val > top - 600.0), np.flatnonzero(val2 > top - 600.0)
+            lst = (list(zip(val[a].tolist(), p[ej[a]].tolist(), p[ei[a]].tolist()))
+                   + list(zip(val2[z].tolist(), p[qj[z]].tolist(), p[qi[z]].tolist())))
+            lst.sort(reverse=True)
+            over.append(lst)
+            z = np.flatnonzero(val2 > top - OPT["near"])
+            held += list(zip(qi[z].tolist(), qj[z].tolist()))
+            for i in ei[np.flatnonzero(late & (val > top - OPT["near"]) & (ei < n))].tolist():
+                if nxt[i] is not None:
+                    held.append((nxt[i], i))
+        return pos, prev, nxt, span, over, held
+
+    def attempt(mid, first, last, on2):
+        before, after = {}, {}
+        for i in seq[first:last + 1]:
+            if on[i] not in before:
+                before[on[i]] = prev[i]
+            after[on[i]] = nxt[i]
+        for i in mid:
+            q = on2[i]
+            if q not in before:
+                before[q] = next((seq[k] for k in range(first - 1, -1, -1) if on[seq[k]] == q), None)
+                after[q] = next((seq[k] for k in range(last + 1, n) if on[seq[k]] == q), None)
+        total, nexts = 0.0, set(after.values())
+        for s in range(ns):
+            f, r, e, b, c, w, y, fr = fin[s], rest[s], edge[s], back[s], cost[s], wake[s], soon[s], idle[s]
+            top = span[s] - 600.0
+            for (v, a, z) in over[s]:
+                if a < first and z > last and (z == n or seq[z] not in nexts):
+                    top = v
+                    break
+            old = [f[i] for i in mid]
+            free = {q: (0.0 if j is None else f[j]) for q, j in before.items()}
+            for i in mid:
+                q = on2[i]
+                at, sig = free[q], -1e9
+                for (j, d) in e[i]:
+                    if f[j] + d > sig:
+                        sig = f[j] + d
+                if sig >= at - y[i]:
+                    at = sig + w[i]
+                at += c[i][q]
+                free[q] = f[i] = at
+                for (j, d) in b[i]:
+                    if pos[j] > last and j not in nexts:
+                        x = at + d + r[j] + (w[j] if at + d >= fr[j] else 0.0)
+                        if x > top:
+                            top = x
+            for q, i in after.items():
+                if i is not None:
+                    at, sig = free[q], max([f[j] + d for (j, d) in e[i]] + [-1e9])
+                    if sig >= at - y[i]:
+                        at = sig + w[i]
+                    if at + r[i] > top:
+                        top = at + r[i]
+            for i, v in zip(mid, old):
+                f[i] = v
+            total += top / norm[s]
+        return total
+
+    def exact(seq2, on2, first):
+        total, before = 0.0, {}
+        for k in range(first - 1, -1, -1):
+            before.setdefault(on[seq[k]], seq[k])
+        for s in range(ns):
+            f, e, c, w, y = list(fin[s]), edge[s], cost[s], wake[s], soon[s]
+            free = {q: f[j] for q, j in before.items()}
+            for i in seq2[first:]:
+                q = on2[i]
+                at, sig = free.get(q, 0.0), -1e9
+                for (j, d) in e[i]:
+                    if f[j] + d > sig:
+                        sig = f[j] + d
+                if sig >= at - y[i]:
+                    at = sig + w[i]
+                free[q] = f[i] = at + c[i][q]
+            total += max(f[j] + d for (j, d) in e[n]) / norm[s]
+        return total
+
+    def rebuild(s, first, last):
+        f, r, e, b, c = fin[s], rest[s], edge[s], back[s], cost[s]
+        part, on2, free = seq[first:last + 1], list(on), {}
+        noise, lean = (rng.random(len(part)) * OPT["noise"]).tolist(), rng.random() * OPT["lean"]
+        pr, left, ready, end = {}, {}, {}, {}
+        for k in range(len(part) - 1, -1, -1):
+            i = part[k]
+            pr[i] = c[i][on[i]] + max([d + pr.get(j, r[j]) for (j, d) in b[i]] + [0.0])
+        for k, i in enumerate(part):
+            pr[i] += noise[k]
+            left[i] = sum(1 for (j, d) in e[i] if pos[j] >= first)
+            if not left[i]:
+                ready[i] = max([f[j] + d for (j, d) in e[i]] + [-1e9])
+        for k in range(first - 1, max(-1, first - 80), -1):
+            free.setdefault(on[seq[k]], f[seq[k]])
+
+        def begin(i, at, q):
+            x = free.get(q, 0.0)
+            return at + wake[s][i] if at >= x - soon[s][i] else x
+
+        mid = []
+        while ready:
+            top, pick = None, None
+            for i, at in ready.items():
+                for q, x in c[i].items():
+                    t = begin(i, at, q)
+                    key = t + (lean * x if q == "v" and len(c[i]) > 1 else 0.0)
+                    if top is None or key < top[0]:
+                        top = (key, q, t)
+            q, until = top[1], top[2] + OPT["look"]
+            for i, at in ready.items():
+                if q in c[i] and begin(i, at, q) <= until:
+                    key = pr[i] - (lean * c[i][q] * 4.0 if q == "v" and len(c[i]) > 1 else 0.0)
+                    if pick is None or key > pick[0]:
+                        pick = (key, i)
+            i = pick[1]
+            free[q] = end[i] = begin(i, ready.pop(i), q) + c[i][q]
+            on2[i] = q
+            mid.append(i)
+            for (j, d) in b[i]:
+                if j in left:
+                    left[j] -= 1
+                    if not left[j]:
+                        ready[j] = max(end.get(x, f[x]) + y for (x, y) in e[j])
+        return mid, on2
+
+    pos, prev, nxt, span, over, held = survey(seq, on, 0)
+    norm = list(span)
+
+    def load(on, some):
+        return sum(cost[0][i]["v"] for i in some if on[i] == "v" and len(cost[0][i]) > 1) * OPT["price"] * ns / norm[0]
+
+    extra = load(on, range(n))
+    best = float(ns)
+    now = best + extra
+    keep, taken, moves = (seq, on), 0, OPT["moves"]
+    for it, u in enumerate(rng.random((moves, 6)).tolist()):
+        if not held:
+            break
+        i, j = held[int(u[0] * len(held))]
+        on2, far = on, int(-math.log(u[2] + 1e-9) * OPT["reach"])
+        if u[1] < OPT["anew"]:
+            wide = int(OPT["wide"] * (0.3 + u[2]))
+            first = max(0, pos[i] - int(wide * u[3]))
+            last = min(n - 1, first + wide)
+            mid, on2 = rebuild(int(u[5] * ns), first, last)
+        elif u[1] < 0.25:
+            x = i if u[2] < 0.5 else j
             other = [q for q in ops[x]["alts"] if q != on[x]]
             if not other:
                 continue
             on2 = list(on)
-            on2[x] = other[int(rng.integers(len(other)))]
-            first = pos[x]
-        elif kind < 0.65:
-            for _ in range(int(rng.geometric(0.5)) - 1):
+            on2[x] = other[int(u[3] * len(other))]
+            first = last = pos[x]
+            mid = [x]
+        elif u[1] < 0.65:
+            for _ in range(far):
                 if prev[j] is not None:
                     j = prev[j]
             if above[i] >> j & 1:
                 continue
-            first, mid = pos[j], seq[pos[j]:pos[i]]
-            seq2 = (seq[:first] + [x for x in mid if above[i] >> x & 1] + [i] + [x for x in mid if not above[i] >> x & 1]
-                    + seq[pos[i] + 1:])
+            first, last = pos[j], pos[i]
+            part = seq[first:last]
+            mid = [x for x in part if above[i] >> x & 1] + [i] + [x for x in part if not above[i] >> x & 1]
         else:
-            if above[i] >> j & 1:
+            for _ in range(far):
+                if nxt[i] is not None:
+                    i = nxt[i]
+            first, last = pos[j], pos[i]
+            part = seq[first + 1:last + 1]
+            mid = [x for x in part if not above[x] >> j & 1] + [j] + [x for x in part if above[x] >> j & 1]
+            if mid[0] == j:
                 continue
-            end = min(n - 1, pos[i] + int(rng.geometric(0.15)) - 1)
-            first, mid = pos[j], seq[pos[j] + 1:end + 1]
-            seq2 = (seq[:first] + [x for x in mid if not above[x] >> j & 1] + [j] + [x for x in mid if above[x] >> j & 1]
-                    + seq[end + 1:])
-        limit = now - OPT["heat"] * (1.0 - it / OPT["moves"]) * float(np.log(rng.random() + 1e-12))
-        total, fins2 = 0.0, []
-        for s in range(len(sets)):
-            fins2.append(list(fins[s]))
-            total += replay(s, seq2, on2, first, fins2[s]) / norm[s]
-        if total <= limit:
-            seq, on, fins, now, held = seq2, on2, fins2, total, None
-            if now < best:
-                best, keep = now, (seq, on)
-        elif rng.random() < 0.1:
-            held = None
+        total = attempt(mid, first, last, on2) + load(on2, mid) - load(on, mid) + extra
+        limit = now - OPT["heat"] * (1.0 - it / moves) * math.log(u[4] + 1e-12)
+        if total <= limit + OPT["loose"] and (abs(total - now) > 1e-9 or u[5] < OPT["flat"]):
+            seq2 = seq[:first] + mid + seq[last + 1:]
+            if exact(seq2, on2, first) + load(on2, mid) - load(on, mid) + extra > limit:
+                continue
+            seq, on = seq2, on2
+            taken += 1
+            pos, prev, nxt, span, over, held = survey(seq, on, first)
+            if taken % OPT["every"] == 0:
+                s = taken // OPT["every"] % ns
+                seq = sorted(seq, key=lambda x: (fin[s][x] - cost[s][x][on[x]], pos[x]))
+                pos, prev, nxt, span, over, held = survey(seq, on, 0)
+            extra = load(on, range(n))
+            now = sum(span[s] / norm[s] for s in range(ns)) + extra
+            if now - extra < best:
+                best, keep = now - extra, (seq, on)
     seq, on = keep
-    OPT["span"] = [int(replay(s, seq, on, 0, fins[s])) for s in range(len(sets))]
+    OPT["span"] = [int(x) for x in survey(seq, on, 0)[3]]
     res = [None] * n
     for k, i in enumerate(seq):
         res[i] = (on[i], k)
@@ -323,7 +447,7 @@ def rank_program(g, core, T, topo):
             if w:
                 hist[name] = [h for h in hist.get(name, []) if h[1] & ~m]
             hist.setdefault(name, []).append((me, m, w))
-        key = str([x[:3] if x[0] not in ("arr", "lq", "ls") else x[0] for x in wr + rd[:1] if isinstance(x, tuple)])
+        key = str([x[:3] if x[0] not in ("twf", "lq", "ls") else x[0] for x in wr + rd[:1] if isinstance(x, tuple)])
         ops.append({"alts": alts, "deps": deps, "soft": soft, "kind": kind, "sem": sem, "cnt": cnt, "lat": lat, "key": key,
                     "gath": size(wr[0]) if any(isinstance(x, tuple) and x[4] is not None for x in rd) else 0})
         return me
@@ -366,7 +490,7 @@ def rank_program(g, core, T, topo):
             v = tsv(out, a, scale, op.mult, bias, op.add)
         alts = {"v": v, "s": acs(out, a, fn.Copy if bias == 0.0 else fn.Identity, bias, scale)}
         if pool:
-            alts["g"] = (lambda: g.affine_select(real(out), real(a), [[0, size(out)]], op.is_ge, 0.0, 0, 0), 190 + 2 * cy * size(out))
+            alts["g"] = (lambda: g.affine_select(real(out), real(a), [[0, size(out)]], op.is_ge, 0.0, 0, 0), 210 + 2 * cy * size(out))
         add(alts, [a, bias], [out])
 
     def scan(out, a, b, o0, o1, init=0.0):
@@ -377,36 +501,37 @@ def rank_program(g, core, T, topo):
         add({"v": (lambda: g.vector.memset(real(out), val), vcost(out, out, 1))}, [], [out])
 
     def quant(q, s, a):
-        add({"v": (lambda: g.vector.quantize_mx(real(q), real(s), real(a)), 15 + 0.275 * size(a))}, [a], [q, s])
+        add({"v": (lambda: g.vector.quantize_mx(real(q), real(s), real(a)), 12 + 0.22 * size(a))}, [a], [q, s])
 
     def act(out, a, f, bias=0.0, scale=1.0, acc=None):
         add({"s": acs(out, a, f, bias, scale, acc)}, [a, bias], [out] + ([acc] if acc else []))
 
     def mm(out, lq, lsc, rq, rsc, start=True, stop=True):
         add({"t": (lambda: g.tensor.matmul_mx(real(out), real(lq), real(lsc), real(rq), real(rsc), start, stop),
-                   1.25 * (size(out) + 16))}, [lq, lsc, rq, rsc], [out], chain=not start, lat=60.0)
+                   25 + 0.8 * (size(out) + 16))}, [lq, lsc, rq, rsc], [out], chain=not start, lat=60.0)
 
     def iota(out, pat, base=0, cmul=0):
         if SCRATCH[out[0]][2] == I:
             call = lambda: g.iota(real(out), pat, base, cmul)
         else:
             call = lambda: g.iota(real(out), pat, base, cmul, allow_small_or_imprecise_dtypes=True)
-        add({"g": (call, 150 + 2 * cy * size(out))}, [], [out])
+        add({"g": (call, 170 + 2 * cy * size(out))}, [], [out])
 
-    def fill(out):
-        add({"v": (lambda: g.vector.memset(real(out), 0.0), vcost(out, out, 1)),
-             "g": (lambda: g.iota(real(out), [[0, size(out)]], 0, 0, allow_small_or_imprecise_dtypes=True), 150 + 2 * cy * size(out))},
-            [], [out])
+    def fill(out, val=0, early=False):
+        alts = {"g": (lambda: g.iota(real(out), [[0, size(out)]], val, 0, allow_small_or_imprecise_dtypes=True), 170 + 2 * cy * size(out))}
+        if early:
+            alts["v"] = (lambda: g.vector.memset(real(out), float(val)), vcost(out, out, 1))
+        add(alts, [], [out])
 
     def sel(out, a, pat, cmp, base, cmul):
-        add({"g": (lambda: g.affine_select(real(out), real(a), pat, cmp, 0.0, base, cmul), 190 + 2 * cy * size(out))}, [a], [out])
+        add({"g": (lambda: g.affine_select(real(out), real(a), pat, cmp, 0.0, base, cmul), 210 + 2 * cy * size(out))}, [a], [out])
 
     nd = [0]
 
     def dma(q, out, a, rd, wr, kb=0):
         nd[0] += 1
         add({q: (lambda: queue[q].dma_start(out, a), 100.0)}, rd, wr, kind="d",
-            sem="m%d" % (nd[0] - 1), cnt=16, lat=OPT["dma"] + 5.0 * kb)
+            sem="m%d" % (nd[0] - 1), cnt=16, lat=OPT["dma"] + 3.5 * kb)
 
     def bank(b, a, n):
         return A("ps", 512 * b + a, 512 * b + a + n)
@@ -414,18 +539,23 @@ def rank_program(g, core, T, topo):
     def col(name, c):
         return A(name, c, c + 1)
 
-    def halves(out, win, off, **kw):
-        for k in range(2):
-            mov(A(out, M * k, M * k + M), ind(win, A(off, 12 * k, 12 * k + 12)), **kw)
+    def tw(t, a=0, b=24):
+        return A("twf", 48 * t + 6 + a, 48 * t + 6 + b)
 
     def steps(y, m, p, a, b, up=True):
         now, before = A(y, a + 1, b + 1), A(y, a, b)
         scan(A(m, a, b), now if up else before, before if up else now, op.max, op.subtract)
         scan(A(p, a, b), A(m, a, b), A("pos", a, b), op.add, op.min, (a - 191) / 32.0)
 
-    def where(k, cnt, a, b, thr, scale, a0, j):
-        act(A("junk", C * j + a, C * j + b), A(cnt, a, b), fn.Sign, col("kb", thr), scale, col("acc", k))
-        ts(col("bw", k), col("acc", k), 0.5, op.mult, (b - a) / 2 + a - a0, op.add)
+    def where(k, cnt, a, b, thr, scale, j):
+        flags = A("junk", C * j + a, C * j + b)
+        if k in OPT["jv"]:
+            ts(flags, A(cnt, a, b), scale, op.mult, col("kn", thr), op.is_gt)
+            scan(A("tally", a, b), flags, A("zero", a, b), op.add, op.add, a - 128.0)
+            ts(col("bw", k), col("tally", b - 1), 128.0, op.add)
+        else:
+            act(flags, A(cnt, a, b), fn.Sign, col("kb", thr), scale, col("acc", k))
+            ts(col("bw", k), col("acc", k), 0.5, op.mult, (b - a) / 2 + a, op.add)
 
     def compare(name, tiles, by_s):
         for (at, a, b, planes) in tiles:
@@ -444,10 +574,10 @@ def rank_program(g, core, T, topo):
                 if k < b:
                     ts(part(k, b), A("dr", k, b), piv, op.is_ge)
 
-    dma("s", real(A("ut")), T.u[:], [], [A("ut")], 128)
-    dma("y", real(A("xi", 0, 4 * M)), T.x[:, 0:4 * M], [], [A("xi", 0, 4 * M)], 320)
-    dma("y", real(A("xi", 4 * M, 4 * C)), T.x[:, 4 * M:4 * C], [], [A("xi", 4 * M, 4 * C)], 512)
-    dma("s", real(A("twi")), T.tw[:], [], [A("twi")])
+    dma("s", real(A("ut")), T.u[:], [], [A("ut")], 200)
+    dma("y", real(A("xi", 0, 4 * M)), T.x[:, 0:4 * M], [], [A("xi", 0, 4 * M)], 360)
+    dma("y", real(A("xi", 4 * M, 4 * C)), T.x[:, 4 * M:4 * C], [], [A("xi", 4 * M, 4 * C)], 520)
+    dma("s", real(A("twi")), T.tw[:], [], [A("twi")], 540)
     dma("y", real(cast(A("wq"), dt.uint8)), T.wc[:], [col("xi", 4 * M)], [A("wq")], 256)
     dma("y", real(A("wp")), T.ws[:], [col("xi", 4 * M)], [A("wp")], 64)
     dma("y", real(A("vt")), T.v[:], [col("wq", 0)], [A("vt")], 128)
@@ -458,118 +588,129 @@ def rank_program(g, core, T, topo):
     iota(A("i16"), [[0, 24], [1, 16]])
     iota(A("iw"), [[16, 24]])
     mov(A("pos"), A("iob"), 1.0 / 32)
-    if not OPT["g1m"]:
-        mov(A("rev"), A("iob"), -1.0, -48.0)
-    fill(A("f0", 12 * M, 16 * M))
-    fill(A("fl", 4 * NL, 4 * MS))
-    fill(A("fl", 12 * MS, 16 * M))
+    mov(A("e", 0, C), A("iob"), -1.0, -48.0)
+    fill(A("f0", 12 * M, 16 * M), early=True)
+    if OPT["split"]:
+        fill(A("zero"), early=True)
+        fill(A("fl", 4 * NL, 4 * MS))
+        fill(A("fl", 12 * MS, 16 * MS))
+        fill(A("fl", 16 * MS + M, 16 * M))
     fill(A("xi", 4 * C, 4 * C + 128))
     fill(A("sl", 0, 128))
-    fill(A("zero"))
     ms(A("ones"), 1.0)
     sel(A("bo1"), A("ones"), [[-16, 8], [0, 64]], op.is_ge, 0, 1)
     sel(A("bo2"), A("bo1"), [[16, 8], [0, 64]], op.is_ge, 15, -1)
     for p in range(4):
         sel(A("et", 512 * p, 512 * p + 512), A("ones"), [[-1, 512]], op.is_equal, p, 4)
-    for name in ("lk", "gk") if OPT["g1"] else ("lv",):
-        ms(col(name, 0), 0.0)
+    fill(A("lv", 0, DUP))
+    for p in range(4 if OPT["es"] else 0):
+        fill(A("hx", PL * p + M + DUP, PL * p + PL))
     ms(col("tie", 0), EPS)
     ms(col("tie", 1), -EPS)
     for name in ("yo", "yg", "yq"):
-        ms(col(name, 0), LEV)
+        fill(col(name, 0), int(LEV))
     cp(A("ul"), A("uli"))
-    ts(A("ri"), A("pi"), 15, op.bitwise_and)
+    ts(col("ri", 0), A("pi"), 15, op.bitwise_and)
+    ts(col("ri", 1), A("pi"), 15, op.bitwise_and, 2, op.logical_shift_right)
+    ts(col("ri", 2), A("pi"), 3, op.bitwise_and)
     cp(A("rf"), A("ri"))
-    for k, a, b in ((0, 16.0, 15.5), (2, 16.0, -128.5), (3, 16.0, 127.5), (4, -1.0, LEV + 7.5), (5, 1.0, LEV - 7.5),
-                    (6, 1.0, LEV - 7.5 - MS), (7, 1.0, MS + 0.5), (8, 1.0, MS + 16.5), (9, 1.0, MS + 32.5)):
-        if k != (6 if OPT["g1m"] else 5):
-            mov(col("kb", k), A("rf"), a, b)
-    ts(A("cm"), A("i16"), A("rf"), op.is_equal, BIG, op.mult)
+    rf = col("rf", 0)
+    for k, c, a, b in ((0, 0, 16.0, 15.5), (1, 0, 16.0, M - MS + 15.5), (2, 0, 16.0, -128.5), (3, 0, 16.0, 127.5), (4, 0, -1.0, LEV + 7.5),
+                       (5, 0, 16.0, 15.5 - 160), (6, 0, 1.0, LEV - 7.5 - MS), (7, 0, 1.0, 0.5), (8, 0, 1.0, 16.5), (9, 0, 1.0, 32.5),
+                       (10, 2, 1.0, 4.0 * 191), (11, 2, 1.0, 4.0 * (191 - NS)), (12, 2, 1.0, 0.0), (13, 2, float(PL), DUP - 1.0)):
+        mov(col("kb", k), col("rf", c), a, b)
+    if OPT["jv"]:
+        mov(A("kn", 0, 2), A("kb", 0, 2), -1.0)
+    ts(A("cm"), A("i16"), rf, op.is_equal, BIG, op.mult)
     ts(A("cm", 0, C, 16), A("cm", 0, C, 16), -1.0, op.add)
     ts(A("keep"), A("cm"), 0.0, op.is_equal)
-    ts(A("cm1", 0, NS), A("i16", 0, NS), A("rf"), op.is_equal)
-    mov(A("iw"), A("iw"), 1.0, A("rf"))
-    mov(A("ths"), A("iw", 0, 18), -1.0, 143.0)
-    mov(A("thl"), A("iw", 0, 6), 1.0, 1.0)
+    ts(A("cm1"), A("i16"), rf, op.is_equal)
+    iota(A("i4"), [[0, M // 4], [1, 4]])
+    ts(A("cm4"), A("i4"), col("rf", 1), op.is_equal, BIG, op.mult)
+    ts(A("keep4"), A("i4"), col("rf", 1), op.not_equal)
+    mov(A("cm4n"), A("cm4"), 2.0, -BIG)
+    mov(A("iw"), A("iw"), 1.0, rf)
+    mov(A("ths", 0, 6), A("iw", 0, 6), -1.0, -145.0)
+    mov(A("ths", 6, 24), A("iw", 0, 18), -1.0, 143.0)
     for t in range(R):
-        quant(A("lq", 224 * t + NL, 224 * t + 224), A("ls", 512 * t + C, 512 * t + 512), A("zero"))
+        quant(A("lq", 224 * t + NL, 224 * t + 224), A("ls", 512 * t + C, 512 * t + 512), A("zero" if OPT["zero"] else "fl", 0, 512))
     quant(A("qo"), A("so"), A("bo2"))
     for k in range(2):
         quant(A("qe", 256 * k, 256 * k + 256), A("se", 256 * k, 256 * k + 256), A("et", 1024 * k, 1024 * k + 1024))
     quant(A("qv"), A("sv"), A("vt"))
     quant(A("qu"), A("su"), A("ut"))
-    cp(A("twf"), A("twi"))
+    cp(tw(0), A("twi"))
     cp(cast(A("qu2"), dt.uint32), ind(cast(A("qu"), dt.uint32), A("ul")))
     cp(A("su2"), ind(A("su"), A("ul")))
 
+    tt(A("hf"), A("twi"), A("iw"), op.is_lt)
+    cp(A("hw"), A("hf"))
     for k in range(2):
         quant(A("qx", M * k, M * k + M), A("sx", M * k, M * k + M), A("xi", 4 * M * k, 4 * M * k + 4 * M))
         mm(bank(k, 0, M), A("qu2"), A("su2"), A("qx", M * k, M * k + M), A("sx", M * k, M * k + M))
         mov(A("sr", M * k, M * k + M), bank(k, 0, M))
-    tt(A("hf"), A("twi"), A("iw"), op.is_lt)
-    cp(A("hw"), A("hf"))
-    halves("st", A("sr"), "twf")
     for k in range(2):
+        mov(A("st", M * k, M * k + M), ind(A("sr"), tw(0, 12 * k, 12 * k + 12)))
         tt(A("d", M * k, M * k + M), A("st", M * k, M * k + M), bank(k, 0, M), op.subtract)
     tt(A("un"), ind(A("tie", 0, 2), A("hw")), A("d"), op.is_lt)
 
     for t in range(R):
         last = t == R - 1
-        if t == 0:
-            parts = [(0, C, 0, M, A("twf"))]
-        else:
-            parts = [(0, NS, 0, MS, A("twf", 0, 18)), (NS, C, MS, M, A("arr", 16 * t - 16, 16 * t - 10))]
-        for s, (a, b, ka, kb, twin) in enumerate(parts):
+        whole = t == 0 or not OPT["split"]
+        parts = [(0, C, 0, M)] if whole else [(0, NS, 0, MS), (NS, C, MS, M)]
+        for s, (a, b, ka, kb) in enumerate(parts):
             un, n = A("un", a, b), (kb - ka) // 16
-            scan(A("cum", a, b), un, un, op.add, op.max, float(ka))
+            ra = 0 if whole or s else M - MS
+            rb = ra + kb - ka
+            scan(A("cum", a, b), un, un, op.add, op.max, float(ra))
             ow = A("ow", 16 * s, 16 * s + n)
             if s:
                 for c in range(n):
-                    act(A("junk", C + NL * c, C + NL * c + NL), A("cum", a, b), fn.Sign, col("kb", 7 + c), -1.0, col("acc", 1 + c))
-                ts(ow, A("acc", 1, 1 + n), 0.5, op.mult, NL / 2, op.add)
-                for p in range(4):
-                    ts(A("ow4", 64 + 16 * p, 64 + 16 * p + n), A("acc", 1, 1 + n), 2.0, op.mult, 2.0 * NL + p, op.add)
+                    act(A("junk", C + NL * c, C + NL * c + NL), A("cum", a, b), fn.Sign, col("kb", 7 + c), -1.0, col("acc", 8 + c))
+                ts(ow, A("acc", 8, 8 + n), 0.5, op.mult, NL / 2, op.add)
             else:
                 scan(A("yo", a + 1, b + 1), un, un, op.add, op.max, col("kb", 4))
                 steps("yo", "mo", "po", a, b)
-                where(0, "cum", a, b - 1, 0, -1.0, a, 0)
-                at = ind(A("po", a, b), col("bw", 0))
-                ts(A("ow", 0, 16), at, 32.0, op.mult, 191.0, op.add)
-                for p in range(4):
-                    if OPT["ow4"]:
-                        mov(A("owf", 16 * p, 16 * p + 16), at, 128.0, 4.0 * 191 + p)
-                    else:
-                        ts(A("ow4", 16 * p, 16 * p + 16), at, 128.0, op.mult, 4.0 * 191 + p, op.add)
-                if OPT["ow4"]:
-                    cp(A("ow4", 0, 64), A("owf"))
-            scan(A("cap", a, b), A("cm", a, b), A("cum", a, b), op.max, op.min)
-            cp(A("cw", a // 16, b // 16), A("cap", a + 15, b, 16))
+                where(0, "cum", a, b - 1, 1 if ra else 0, -1.0, 0)
+                ts(A("ow", 0, 16), ind(A("po", a, b), col("bw", 0)), 32.0, op.mult, 191.0, op.add)
+            mov(A("orow", ra, rb), ind(A("pos", a, b), ow))
+            scan(A("oh", ra, rb), A("cm4n", ra, rb), A("orow", ra, rb), op.max, op.min, -8.0)
+            ts(A("ow4", ra // 4, rb // 4), A("oh", ra + 3, rb, 4), 128.0, op.mult, col("kb", 10 + s), op.add)
             mov(A("dr", ka, kb), ind(A("d", a, b), ow))
             if OPT["dm"] and not s:
                 scan(A("dm", ka, kb), A("dr", ka, kb), A("cm", ka, kb), op.max, op.min)
             else:
                 tt(A("dm", ka, kb), ind(A("d", a, b), ow), A("cm", ka, kb), op.min)
             scan(A("dh", ka, kb), A("keep", ka, kb), A("dm", ka, kb), op.mult, op.add)
-            mov(A("ct", a, b), ind(A("cum", a, b), twin))
+            mov(A("ct", a, b), ind(A("cum", 0, b), tw(t, a // 16, b // 16)))
             if OPT["ctm"] and not s:
-                mov(A("cto", ka, kb), ind(A("ct", a, b), ow))
-                scan(A("ctm", ka, kb), A("cto", ka, kb), A("cm", ka, kb), op.max, op.min)
+                mov(A("cto", ra, rb), ind(A("ct", a, b), ow))
+                scan(A("ctm", ra, rb), A("cto", ra, rb), A("cm4", ra, rb), op.max, op.min)
             else:
-                tt(A("ctm", ka, kb), ind(A("ct", a, b), ow), A("cm", ka, kb), op.min)
-            scan(A("cth", ka, kb), A("keep", ka, kb), A("ctm", ka, kb), op.mult, op.add)
-            cp(A("ctw", ka // 16, kb // 16), A("cth", ka + 15, kb, 16))
-            for p in range(4):
-                o4, lo, hi = 64 * s + 16 * p, PL * p + 1 + ka, PL * p + 1 + kb
-                src = ind(A("xi", 4 * a, 4 * b), A("ow4", o4, o4 + n))
-                mov(A("xo", lo, hi), src, 0.5)
-                if s:
-                    mov(A("xa", lo, hi), src, 0.5)
+                tt(A("ctm", ra, rb), ind(A("ct", a, b), ow), A("cm4", ra, rb), op.min)
+            w = (rb - ra) // (1 if s else OPT["xc"])
+            for lo in range(ra, rb, w):
+                src = ind(A("xi", 4 * a, 4 * b), A("ow4", lo // 4, (lo + w) // 4))
+                mov(A("xo", 4 * lo + 4, 4 * (lo + w) + 4), src, 0.5)
+                if s and OPT["xa"]:
+                    mov(A("xa", 4 * lo + 4, 4 * (lo + w) + 4), src, 0.5)
                 else:
-                    mov(A("xa", lo, hi), A("xo", lo, hi), pool=True)
-        if t == 0:
+                    mov(A("xa", 4 * lo + 4, 4 * (lo + w) + 4), A("xo", 4 * lo + 4, 4 * (lo + w) + 4), pool=True)
+            if not s:
+                mov(A("xa", 0, 4), A("xo", 4 * M, 4 * M + 4), pool=True)
+                mov(A("xo", 0, 4), A("xo", 4 * M, 4 * M + 4), pool=True)
+            if not OPT["join"]:
+                scan(A("cth", ra, rb), A("keep4", ra, rb), A("ctm", ra, rb), op.mult, op.add)
+                scan(A("cap", a, b), A("cm", a, b), A("cum", a, b), op.max, op.min)
+        if OPT["join"]:
+            scan(A("cth"), A("keep4"), A("ctm"), op.mult, op.add)
+            scan(A("cap"), A("cm"), A("cum"), op.max, op.min)
+        ts(A("ctw"), A("cth", 3, M, 4), 4.0, op.mult, col("kb", 12), op.add)
+        ts(A("cw"), A("cap", 15, C, 16), DUP - 1.0, op.add)
+        if whole:
             names, h = ("f0", "q0", "s0"), M - MS
             calls = [[(0, 0, M, [0, 1, 2, 3]), (M, 0, M, [4, 5, 6, 7])], [(2 * M, 0, M, [8, 9, 10, 11]), (3 * M, 0, M, [12])]]
-            by_s = [{}, {c: 128 for c in OPT["s0"]}]
+            by_s = [{c: OPT["s0w"] for c in OPT["s0"]}] * 2
         else:
             names, h = ("fl", "qf", "sf"), M - MS
             calls = [[(MS, 0, MS, [0, 1, 2, 3]), (2 * MS, 0, MS, [4, 5, 6, 7]), (3 * MS, 0, MS, [8, 12])],
@@ -585,51 +726,53 @@ def rank_program(g, core, T, topo):
                 mine, wide = [y for y in every if y[1] == x[1]], max(128, x[2] - x[1])
                 mm(bank(2 + (x[1] > 0), 0, wide), A("qo"), A("so"), A(names[1], x[0], x[0] + wide), A(names[2], x[0], x[0] + wide),
                    x == mine[0], x == mine[-1])
-        for (a, b, ka, kb, twin) in parts:
-            out, cnt = A("lv", 1 + ka, 1 + kb), bank(2 + (ka > 0), 0, kb - ka)
-            if OPT["g1"]:
-                act(out, cnt, fn.Sign, 48.5, -1.0)
-            else:
-                add({"v": tsv(out, cnt, 48.5, op.is_le), "s": acs(out, cnt, fn.Relu, 49.0, -1.0)}, [cnt], [out])
-        mov(A("xa", 0, 4 * PL, PL), A("xo", M, 4 * PL, PL))
-        mov(A("xo", 0, 4 * PL, PL), A("xo", M, 4 * PL, PL))
-        for p in range(4):
-            tt(A("z", p, 4 * M, 4), ind(A("xo", PL * p, PL * p + M + 1), A("ctw")), A("xa", PL * p, PL * p + M), op.add)
+        for (a, b, ka, kb) in parts:
+            ra = 0 if whole or ka else M - MS
+            out, cnt = A("lv", DUP + ra, DUP + ra + kb - ka), bank(2 + (ka > 0), 0, kb - ka)
+            add({"v": tsv(out, cnt, 48.5, op.is_le), "s": acs(out, cnt, fn.Relu, 49.0, -1.0)}, [cnt], [out])
+        w = M // OPT["zc"]
+        for (at, lo, hi) in [(DUP + x, x, x + w) for x in range(0, M, w)] + [(0, M - DUP, M)]:
+            tt(A("z", 4 * at, 4 * (at + hi - lo)), ind(A("xo", 0, 4 * M + 4), A("ctw", lo // 4, hi // 4)), A("xa", 4 * lo, 4 * hi), op.add)
         quant(A("qz"), A("sz"), A("z"))
         for p in range(4):
-            mm(bank(4 + p, 0, M), A("wq", 128 * p, 128 * p + 128), A("wp", 128 * p, 128 * p + 128), A("qz"), A("sz"))
-            mov(A("hx", PL * p + 1, PL * p + 1 + M), bank(4 + p, 0, M), 0.03125)
-        mov(A("hx", 0, 4 * PL, PL), A("hx", M, 4 * PL, PL))
-        for p in range(4):
-            tt(A("e", C * p, C * p + C), ind(A("hx", PL * p, PL * p + M + 1), A("cw")), A("xi", p, 4 * C, 4), op.add)
-        if OPT["g1"]:
-            scan(A("lk", 1, M + 1), A("lv", 1, M + 1), A("ones", 0, M), op.add, op.add)
-            for k in range(2):
-                mov(A("gk", 1 + M * k, 1 + M * k + M), ind(A("lk", 0, M + 1), A("cw", 12 * k, 12 * k + 12)), 0.5)
-            scan(A("g1"), A("gk", 1, C + 1), A("gk", 0, C), op.max, op.subtract)
-        else:
-            tt(A("g1"), ind(A("lv", 0, M + 1), A("cw")), A("un"), op.min)
-        halves("g2", A("g1"), "twf")
+            mm(bank(4 + p, 0, M + DUP), A("wq", 128 * p, 128 * p + 128), A("wp", 128 * p, 128 * p + 128), A("qz"), A("sz"))
+            mov(A("hx", PL * p, PL * p + M + DUP), bank(4 + p, 0, M + DUP), 0.03125)
+        for (a, b) in ((0, 256), (256, C)) if OPT["se"] else ((0, C),):
+            for p in range(4):
+                tt(A("e", C * (p + 1) + a, C * (p + 1) + b), ind(A("hx", PL * p, PL * p + M + DUP), A("cw", a // 16, b // 16)),
+                   A("xi", 4 * a + p, 4 * b, 4), op.add)
+        tt(A("g1"), ind(A("lv", 0, M + DUP), A("cw")), A("un"), op.min)
+        for k in range(2):
+            mov(A("g2", M * k, M * k + M), ind(A("g1"), tw(t, 12 * k, 12 * k + 12)))
         scan(A("gn"), A("g1"), A("g2"), op.add, op.add)
-        scan(A("yg", 1, C + 1), A("g1"), A("g2"), op.add, op.add, col("kb", 4))
-        steps("yg", "mg", "pg", 0, C)
-        where(4, "gn", 0, C - 1, 0, -1.0, 0, 2)
-        ts(A("lw"), ind(A("pg"), col("bw", 4)), 32.0, op.mult, 191.0, op.add)
-        if OPT["g1m"]:
-            mov(A("g1m"), A("g1"), 1.0, -1.0)
-            scan(A("ncs"), A("g1m"), A("g2"), op.add, op.add, float(MS))
-            scan(A("yq", 1, C + 1), A("g1m"), A("g2"), op.add, op.add, col("kb", 5))
+        if OPT["yg"]:
+            mov(A("yg", 1, C + 1), A("gn"), 1.0, col("kb", 4))
         else:
-            scan(A("ncs", 0, MS), A("gn", 0, MS), A("rev", 0, MS), op.min, op.add, 256.0)
-            scan(A("ncs", MS, C), A("gn", MS, C), A("rev", MS, C), op.max, op.add)
-            mov(A("yq", 1, C + 1), A("ncs"), 1.0, col("kb", 6))
+            scan(A("yg", 1, C + 1), A("g1"), A("g2"), op.add, op.add, col("kb", 4))
+        steps("yg", "mg", "pg", 0, C)
+        where(4, "gn", 0, C - 1, 5, -1.0, 2)
+        ts(A("lqw", 0, 16), ind(A("pg"), col("bw", 4)), 32.0, op.mult, 191.0, op.add)
+        scan(A("ncs", 0, MS), A("gn", 0, MS), A("e", 0, MS), op.min, op.add, 256.0)
+        scan(A("ncs", MS, C), A("gn", MS, C), A("e", MS, C), op.max, op.add)
+        mov(A("yq", 1, C + 1), A("ncs"), 1.0, col("kb", 6))
         steps("yq", "mq", "pq", 0, C, False)
-        where(6, "ncs", 0, 351, 2, 1.0, 0, 3)
-        where(7, "ncs", 256, C - 1, 3, 1.0, 0, 4)
-        ts(A("qw"), ind(A("pq"), A("bw", 6, 8)), 32.0, op.mult, 191.0, op.add)
-        lw, qw = A("lw", 0, 6), A("qw", 0, 18)
-        for p in range(4):
-            mov(A("sl", 128 + p, 512, 4), ind(A("e", C * p, C * p + C), lw))
+        where(6, "ncs", 0, 351, 2, 1.0, 3)
+        where(7, "ncs", 256, C - 1, 3, 1.0, 4)
+        ts(A("lqw", 16, 48), ind(A("pq"), A("bw", 6, 8)), 32.0, op.mult, 191.0 + C, op.add)
+        lw, qw = A("lqw", 10, 16), A("lqw", 16, 34)
+        if t in OPT["es"]:
+            mov(A("lr", 0, NL), ind(A("pos"), lw))
+            mov(A("lr", NL, M), ind(A("cum"), lw))
+            scan(A("lh", 0, NL), A("cm4n", 0, NL), A("lr", 0, NL), op.max, op.min, -8.0)
+            ts(A("l4", 0, 24), A("lh", 3, NL, 4), 128.0, op.mult, col("kb", 10), op.add)
+            scan(A("lm"), A("lr", NL, M), A("cm4", 0, NL), op.max, op.min)
+            scan(A("lh", NL, M), A("keep4", 0, NL), A("lm"), op.mult, op.add)
+            ts(A("l4", 24, 48), A("lh", NL + 3, M, 4), col("kb", 13), op.add)
+            mov(A("xl"), ind(A("xi", 0, 4 * C), A("l4", 0, 24)))
+            tt(A("sl", 128, 512), ind(A("hx"), A("l4", 24, 48)), A("xl"), op.add)
+        else:
+            for p in range(4):
+                mov(A("sl", 128 + p, 512, 4), ind(A("e", C * (p + 1), C * (p + 2)), lw))
         quant(A("qs"), A("s0", 4 * M, 4 * M + 128), A("sl"))
         dst = T.cores[(rank + STEP[t]) % n_ranks]
         rid, pid = topo.addr(dst)[:2]
@@ -646,53 +789,54 @@ def rank_program(g, core, T, topo):
                 RemoteDMATransfer(dst_ids=to, dma_engine_mask=m1, remote_sem=T.sem["ac%d" % t],
                                   src=real(scales), dst=real(A("ls", 512 * t, 512 * t + C)))], local_sem=T.sem.lc)
 
-        j = add({"g": (send_codes, OPT["issue"])}, [A("qs", 32, 128), scales], [], kind="r", sem="lc", cnt=2 * half, lat=OPT["rem"])
+        j = add({"g": (send_codes, OPT["issue"])}, [A("qs", 32, 128), scales], [], kind="r", sem="lc", cnt=2 * half,
+                lat=OPT["rem"] + (OPT["rem0"] if t == 0 else 0.0))
         add({"x": (None, 0.0)}, [], [A("lq", 224 * t, 224 * t + NL), A("ls", 512 * t, 512 * t + C)], kind="x",
             sem="ac%d" % t, cnt=2 * half, after=[j])
-        arr, arh = A("arr", 16 * t, 16 * t + 6), A("arr", 16 * t + 6, 16 * t + 12)
-        land, snd = (A("lrow"), A("srow")) if last else (A("arr", 16 * t, 16 * t + 12), A("snd", 0, 12))
-        mov(A("t1"), ind(A("gn"), A("twf")))
-        mov(A("t2"), ind(A("ncs"), A("twf")))
+        mov(A("tn", 0, C), ind(A("gn"), tw(t)), -1.0, -float(MS))
+        mov(A("tn", C, 2 * C), ind(A("ncs"), tw(t)))
         if last:
-            mov(snd, ind(A("t1"), lw), 1.0, NS - 1.0)
+            mov(A("srow"), ind(A("tn", 0, C), lw), -1.0, 143.0)
+            mov(A("otr"), ind(A("tn"), qw), -1.0, 143.0)
+            pairs = [(A("srow"), A("lrow"), m0 | m1)]
         else:
-            if OPT["nm"]:
-                mov(A("nr", NS, C), ind(A("t1"), lw))
-                scan(A("nm", NS, C), A("nr", NS, C), A("cm", 0, NL), op.max, op.min)
-            else:
-                tt(A("nm", NS, C), ind(A("t1"), lw), A("cm", 0, NL), op.min)
-            scan(A("nh", NS, C), A("keep", 0, NL), A("nm", NS, C), op.mult, op.add)
-            ts(A("snd", 0, 6), A("nh", NS + 15, C, 16), -1.0, op.add)
-            tt(A("hf", 18, 24), A("nh", NS + 15, C, 16), A("thl"), op.is_lt)
-            cp(A("snd", 6, 12), A("hf", 18, 24))
-        j = add({"g": (lambda t=t, rid=rid, pid=pid, m=m0 | m1, land=land, snd=snd: g.remote_dma(
-            real(land), real(snd), T.sem["al%d" % t], T.sem.ll, pid, rid, m), OPT["issue"])},
-            [snd], [], kind="r", sem="ll", cnt=2 * half, lat=OPT["rem"])
-        add({"x": (None, 0.0)}, [], [land], kind="x", sem="al%d" % t, cnt=2 * half, after=[j])
-        if last:
-            mov(A("otr"), ind(A("t2"), qw), -1.0, 143.0)
-        else:
-            if OPT["nm"]:
-                mov(A("nr", 0, NS), ind(A("t2"), qw))
-                scan(A("nm", 0, NS), A("nr", 0, NS), A("cm1", 0, NS), op.add, op.mult)
-            else:
-                tt(A("nm", 0, NS), ind(A("t2"), qw), A("cm1", 0, NS), op.mult)
-            scan(A("nh", 0, NS), A("keep", 0, NS), A("nm", 0, NS), op.mult, op.add)
-            ts(A("twf", 0, 18), A("nh", 15, NS, 16), -1.0, op.mult, 143.0, op.add)
-            ts(A("twf", 18, 24), arr, float(NS), op.add)
-        for p in range(4):
-            mov(A("xi", p, 4 * NS, 4), ind(A("e", C * p, C * p + C), qw))
-        quant(A("qx", 0, NS), A("sx", 0, NS), A("xi", 0, 4 * NS))
+            for (a, b, w) in ((0, C, 2 * C),) if OPT["tm"] else ((0, NL, C), (NL, C, 2 * C)):
+                src = ind(A("tn", 0, w), A("lqw", 10 + a // 16, 10 + b // 16))
+                if OPT["nm"] and b == C:
+                    mov(A("nr", a, b), src)
+                    scan(A("nm", a, b), A("nr", a, b), A("cm1", a, b), op.add, op.mult)
+                else:
+                    tt(A("nm", a, b), src, A("cm1", a, b), op.mult)
+                scan(A("nh", a, b), A("keep", a, b), A("nm", a, b), op.mult, op.add)
+                ts(tw(t + 1, a // 16 - 6, b // 16 - 6), A("nh", a + 15, b, 16), -1.0, op.mult, 143.0, op.add)
+                tt(A("hf", a // 16, b // 16), A("nh", a + 15, b, 16), A("ths", a // 16, b // 16), op.is_gt)
+                cp(A("hw", a // 16, b // 16), A("hf", a // 16, b // 16))
+            pairs = [(tw(t + 1, -6, 0), tw(t + 1, 18, 24), m0), (A("hw", 0, 6), tw(t + 1, 24, 30), m1)]
+
+        def send_list(t=t, rid=rid, pid=pid, pairs=pairs):
+            return g.remote_dma_fused([
+                RemoteDMATransfer(dst_ids=[DstId(rid=rid, pnc=pid)], dma_engine_mask=m, remote_sem=T.sem["al%d" % t], src=real(a), dst=real(b))
+                for (a, b, m) in pairs], local_sem=T.sem.ll)
+
+        j = add({"g": (send_list, OPT["issue"])}, [a for (a, b, m) in pairs], [], kind="r", sem="ll", cnt=2 * half,
+                lat=OPT["rem"] + (OPT["rem0"] / 2 if t == 0 else 0.0))
+        add({"x": (None, 0.0)}, [], [b for (a, b, m) in pairs], kind="x", sem="al%d" % t, cnt=2 * half, after=[j])
+        cuts = ((0, 160, 256, 0), (160, NS, C, 2)) if OPT["sx"] else ((0, NS, C, 0),)
+        side = ("qv", "sv") if last else ("qu2", "su2")
+        for (a, b, w, k) in cuts:
+            for p in range(4):
+                mov(A("xi", 4 * a + p, 4 * b, 4), ind(A("e", C * p, C * (p + 1) + w), A("lqw", 16 + a // 16, 16 + b // 16)))
+            quant(A("qx", a, b), A("sx", a, b), A("xi", 4 * a, 4 * b))
+            mm(bank(k, 0, b - a), A(side[0]), A(side[1]), A("qx", a, b), A("sx", a, b))
+            mov(A("yr" if last else "sr", a, b), bank(k, 0, b - a))
         for p in range(4):
             mm(bank(4 + p, 0, 128), A("qe", 128 * p, 128 * p + 128), A("se", 128 * p, 128 * p + 128),
                A("lq", 224 * t, 224 * t + 128), A("ls", 512 * t + NS, 512 * t + NS + 128))
             mov(A("xi", 4 * NS + p, 4 * C, 4), bank(4 + p, 0, NL))
         quant(A("qb"), A("sq"), A("xi", 4 * NS, 4 * NS + 512))
+        mm(bank(1, 0, 128), A(side[0]), A(side[1]), A("qb"), A("sq"))
+        mov(A("yr" if last else "sr", NS, C), bank(1, 0, NL))
         if last:
-            mm(bank(0, 0, NS), A("qv"), A("sv"), A("qx", 0, NS), A("sx", 0, NS))
-            mov(A("yr", 0, NS), bank(0, 0, NS))
-            mm(bank(1, 0, 128), A("qv"), A("sv"), A("qb"), A("sq"))
-            mov(A("yr", NS, C), bank(1, 0, NL))
             dma("y", T.oc[:, 0:4 * NS], real(cast(A("qx", 0, NS), dt.uint8)), [A("qx", 0, NS)], [], 144)
             for k in range(4):
                 dma("y", T.osc[4 * k:4 * k + 4, 0:NS], T.sx[32 * k:32 * k + 4, 0:NS], [A("sx", 0, NS)], [])
@@ -704,29 +848,20 @@ def rank_program(g, core, T, topo):
             dma("y", T.ot[:, 0:NS], T.otr[0:128:16, :], [A("otr")], [])
             dma("y", T.ot[:, NS:C], T.lrow[0:128:16, :], [A("lrow")], [])
         else:
-            mm(bank(0, 0, NS), A("qu2"), A("su2"), A("qx", 0, NS), A("sx", 0, NS))
-            mov(A("sr", 0, NS), bank(0, 0, NS))
-            mm(bank(1, 0, 128), A("qu2"), A("su2"), A("qb"), A("sq"))
-            mov(A("sr", NS, C), bank(1, 0, NL))
-            tt(A("hf", 0, 18), A("nh", 15, NS, 16), A("ths"), op.is_gt)
-            cp(A("hw", 0, 18), A("hf", 0, 18))
-            if OPT["d0"]:
-                mm(bank(2, 0, NS), A("qu2"), A("su2"), A("qx", 0, NS), A("sx", 0, NS))
-                mov(A("st", 0, NS), bank(2, 0, NS))
-                tt(A("d", 0, NS), ind(A("sr", 0, NS), A("twf", 0, 18)), A("st", 0, NS), op.subtract)
-            else:
-                mov(A("st", 0, 160), ind(A("sr", 0, NS), A("twf", 0, 10)))
-                mov(A("st", 160, NS), ind(A("sr", 0, NS), A("twf", 10, 18)))
-                tt(A("d", 0, NS), A("st", 0, NS), bank(0, 0, NS), op.subtract)
+            mov(A("st", 0, 160), ind(A("sr", 0, NS), tw(t + 1, 0, 10)))
+            mov(A("st", 160, NS), ind(A("sr", 0, NS), tw(t + 1, 10, 18)))
+            for (a, b, w, k) in cuts:
+                tt(A("d", a, b), A("st", a, b), bank(k, 0, b - a), op.subtract)
             if OPT["d1"]:
                 mm(bank(3, 0, 128), A("qu2"), A("su2"), A("qb"), A("sq"))
                 mov(A("st", NS, C), bank(3, 0, NL))
-                tt(A("d", NS, C), ind(A("sr", NS, C), arr), A("st", NS, C), op.subtract)
+                tt(A("d", NS, C), ind(A("sr"), tw(t + 1, 18, 24)), A("st", NS, C), op.subtract)
             else:
-                mov(A("st", NS, C), ind(A("sr", NS, C), arr))
+                mov(A("st", NS, C), ind(A("sr"), tw(t + 1, 18, 24)))
                 tt(A("d", NS, C), A("st", NS, C), bank(1, 0, NL), op.subtract)
-            tt(A("un", 0, NS), ind(A("tie", 0, 2), A("hw", 0, 18)), A("d", 0, NS), op.is_lt)
-            tt(A("un", NS, C), ind(A("tie", 0, 2), arh), A("d", NS, C), op.is_lt)
+            for (a, b) in ((0, 160), (160, NS)) if OPT["su"] else ((0, NS),):
+                tt(A("un", a, b), ind(A("tie", 0, 2), A("hw", 6 + a // 16, 6 + b // 16)), A("d", a, b), op.is_lt)
+            tt(A("un", NS, C), ind(A("tie", 0, 2), tw(t + 1, 24, 30)), A("d", NS, C), op.is_lt)
 
     n = len(ops)
     if "plan" not in OPT:
@@ -738,7 +873,7 @@ def rank_program(g, core, T, topo):
     ops.append({"q": "g", "alts": {"g": (None, 0.0)}, "deps": set(j for j in range(n) if ops[j]["kind"] != "c"), "kind": "e"})
     order.append(n)
     pos = {order[k]: k for k in range(n + 1)}
-    know, seen = {q: 0 for q in queue}, {}
+    know, seen, line = {q: 0 for q in queue}, {}, {q: [] for q in queue}
     for i in order:
         o = ops[i]
         o["waits"], o["sig"], o["know"], o["before"] = [], o["kind"] != "c", 0, 0
@@ -749,10 +884,19 @@ def rank_program(g, core, T, topo):
             seen[o["q"]] = o["before"] | 1 << i
         for j in sorted(o["deps"], key=lambda k: -pos[k]):
             if not know[o["q"]] >> j & 1:
+                if ops[j]["q"] == o["q"] and ops[j]["kind"] == "c":
+                    since = 0.0
+                    for x in reversed(line[o["q"]]):
+                        if x == j or since >= OPT["since"]:
+                            j = x
+                            break
+                        since += ops[x]["alts"][o["q"]][1]
                 o["waits"].append(j)
                 ops[j]["sig"] = True
                 know[o["q"]] |= ops[j]["know"] | 1 << j | ops[j]["before"]
         o["know"] = know[o["q"]]
+        if o["kind"] == "c":
+            line[o["q"]].append(i)
     turn, prev, total = {q: 0 for q in POOL}, {}, {}
     for i in order:
         o = ops[i]

@@ -1,26 +1,23 @@
 import math
 import numpy as np
 from concourse.bass import DstId, RemoteDMATransfer
-from concourse.mybir import dt, AluOpType, ActivationFunctionType
+from concourse.mybir import dt, AluOpType, ActivationFunctionType, AxisListType
 
 C, M, NL, NS, R = 384, 192, 96, 288, 3
 MS = NS // 2
 STEP = [1, 2, 4]
 PL = 208
 DUP = 8
+OFF = 16
+TT = 320
 BIG = 2.0 ** 80
 EPS = 2.0 ** -110
 LEV = 3072.0
-OPT = {"cy": 0.83, "ga": 1.15, "dep": 240.0, "sfix": 0.0, "dma": 1100.0, "rem": 1500.0, "rem0": 500.0, "issue": 700.0,
-       "fine": [(1.07, 1.25, 265.0, 50.0, 0.0, 200.0, 100.0, 3.0, 20.0), (1.04, 1.0, 220.0, 50.0, 100.0, -200.0, 100.0, 5.0, 15.0),
-                (1.28, 1.35, 280.0, 280.0, 200.0, 300.0, 100.0, 8.0, 25.0)],
-       "tries": 300, "pm": 0.015, "whi": 8.0, "pen0": 0.5, "seed": 1,
-       "moves": 90000, "heat": 0.0018, "reach": 3.0, "flat": 0.15, "near": 300.0, "every": 20, "loose": 0.002,
-       "anew": 0.1, "wide": 35, "noise": 600.0, "lean": 1.5, "look": 100.0, "price": 0.0,
-       "w0": {"e'": 4.0, "z'": 4.0, "xo": 4.0, "sl": 3.0, "xi": 2.0, "fl": 5.0, "f0": 5.0, "hx": 2.0},
-       "s0": [7, 8, 9, 10, 11], "s1": [], "s2": [9, 10, 11], "ctm": 1, "nm": 1, "dm": 0,
-       "se": 0, "sx": 1, "su": 1, "yg": 0, "split": 1, "xc": 2, "xa": 1, "zc": 2, "s0w": 192, "zero": 1, "es": [], "d1": 1, "join": 0,
-       "since": 260.0, "tm": 0, "jv": []}
+OPT = {"cy": 0.83, "ga": 1.15, "dma": 1100.0, "rem": 1500.0, "rem0": 500.0, "issue": 800.0,
+       "fine": [(1.0, 1.3, 210.0, 0.0, 200.0, 3.0, 20.0), (1.0, 1.0, 190.0, 100.0, -200.0, 3.0, 20.0), (1.35, 1.6, 270.0, 200.0, 300.0, 5.0, 25.0)],
+       "seed": 4, "stages": [(1, 50000, 20.0), (3, 10000, 12.0), (3, 10000, 6.0)], "wide": 70, "some": 0.15, "shake": 500.0,
+       "chain": 0.3, "pull": 800.0, "flips": 2, "free": 0.1, "since": 260.0, "lean": 1.0, "price": 0.07,
+       "both": [7, 8, 11]}
 
 
 def sb(n, d):
@@ -34,356 +31,217 @@ SCRATCH = {
     "qx": sb(C, X4), "sx": sb(C, U8), "qb": sb(128, X4), "sq": sb(128, U8),
     "qu": sb(128, X4), "su": sb(128, U8), "qu2": sb(128, X4), "su2": sb(128, U8),
     "qv": sb(128, X4), "sv": sb(128, U8), "wq": sb(512, X4), "wp": sb(512, U8),
-    "ones": sb(512, B), "et": sb(2048, B), "qe": sb(512, X4), "se": sb(512, U8),
+    "ones": sb(512, B), "et": sb(520, B), "qe": sb(512, X4), "se": sb(512, U8),
     "bo1": sb(512, B), "bo2": sb(512, B), "qo": sb(128, X4), "so": sb(128, U8), "zero": sb(512, B),
-    "uli": sb(8, I), "ul": sb(8, U16), "pi": sb(1, I), "ri": sb(3, I), "rf": sb(3, F), "kb": sb(14, F), "kn": sb(2, F), "tally": sb(C, B),
-    "lr": sb(M, B), "lm": sb(NL, B), "lh": sb(M, B), "l4": sb(48, U16), "xl": sb(C, B),
+    "uli": sb(8, I), "ul": sb(8, U16), "pi": sb(1, I), "ri": sb(3, I), "rf": sb(3, F), "kb": sb(13, F),
     "i4": sb(M, B), "cm4": sb(M, B), "cm4n": sb(M, B), "keep4": sb(M, B), "orow": sb(M, B), "oh": sb(M, B),
     "iob": sb(C, B), "pos": sb(C, B), "i16": sb(C, B), "cm": sb(C, B), "cm1": sb(C, B), "keep": sb(C, B),
-    "tie": sb(16, F), "iw": sb(24, F), "ths": sb(24, F), "hf": sb(24, F), "hw": sb(24, U16),
-    "sr": sb(C, F), "st": sb(C, F), "d": sb(C, F), "un": sb(C, B), "cum": sb(C, B),
-    "twf": sb(48 * R, U16), "srow": sb(NL, F), "lrow": sb(NL, F),
+    "tie": sb(16, F), "iw": sb(24, F), "ths": sb(38, F), "hf": sb(38, F), "hw": sb(24, U16),
+    "sr": sb(C, F), "st": sb(C, F), "d": sb(C, F), "un": sb(C, B), "cum": sb(C + 16, B),
+    "cap2": sb(C, B), "uw": sb(24, F), "uc": sb(24, F), "cwu": sb(24, U16), "ud": sb(24, F), "cim": sb(C, B), "cih": sb(C, B),
+    "twf": sb(64 * R, U16), "srow": sb(NL, F), "lrow": sb(NL, F),
     "junk": sb(5 * C, B), "acc": sb(12, F), "bw": sb(8, U16),
     "yo": sb(C + 8, B), "yg": sb(C + 8, B), "yq": sb(C + 8, B), "mo": sb(C, B), "mg": sb(C, B), "mq": sb(C, B),
     "po": sb(C, B), "pg": sb(C, B), "pq": sb(C, B),
-    "cto": sb(M, B), "xa": sb(4 * PL, B), "nr": sb(C, B),
-    "ow": sb(32, U16), "ow4": sb(48, U16), "lqw": sb(48, U16),
-    "cap": sb(C, B), "cw": sb(24, U16),
-    "dm": sb(M, F), "dh": sb(M, F), "dr": sb(M, F), "sg": sb(8 * M, B),
-    "f0": sb(16 * M, B), "q0": sb(4 * M, X4), "s0": sb(4 * M + 128, U8),
-    "fl": sb(16 * M, B), "qf": sb(4 * M, X4), "sf": sb(4 * M, U8),
+    "cto": sb(M, B), "xa": sb(4 * (M + DUP), B), "nr": sb(C, B),
+    "ow": sb(32, U16), "ow4": sb(48, U16), "lqw": sb(48, U16), "cap": sb(C, B), "cw": sb(24, U16),
+    "dm": sb(M, F), "dh": sb(M, F), "dr": sb(M, F), "sg": sb(11 * M, B),
+    "cmb": sb(M, B), "mr": sb(M, B), "r2": sb(M, B), "ra": sb(12, F), "thf": sb(12, F), "thw": sb(14, U16), "tb": sb(64, B), "thr": sb(M, B),
+    "fl": sb(2048, B), "qf": sb(512, X4), "sf": sb(640, U8),
     "ct": sb(C, B), "ctm": sb(M, B), "cth": sb(M, B), "ctw": sb(48, U16),
-    "xo": sb(4 * PL, B), "z": sb(4 * (M + DUP), B), "qz": sb(M + DUP, X4), "sz": sb(M + DUP, U8), "hx": sb(4 * PL, B),
-    "lv": sb(PL, B), "g1": sb(C, B), "g2": sb(C, B), "gn": sb(C, B), "ncs": sb(C, B), "e": sb(5 * C, B),
+    "xo": sb(4 * (M + DUP), B), "z": sb(4 * (M + DUP), B), "qz": sb(M + DUP, X4), "sz": sb(M + DUP, U8), "hx": sb(4 * PL, B),
+    "lv": sb(M + 1, B), "gone": sb(C, B), "gn": sb(C, B), "ncs": sb(C, B), "e": sb(4 * C, B),
     "sl": sb(512, B), "qs": sb(128, X4), "lq": sb(R * 224, X4), "ls": sb(R * 512, U8),
-    "tn": sb(2 * C, B), "nm": sb(C, B), "nh": sb(C, B),
+    "tn": sb(2 * C, B), "nq": sb(NL, B), "nm": sb(NL, B), "nh": sb(NL, B),
     "yr": sb(C, F), "otr": sb(NS, F),
 }
 POOL = {"v": 56, "s": 36, "t": 10, "g": 10}
 NDMA = 24
 SEMAPHORES = (["%s%d" % (q, i) for q in POOL for i in range(POOL[q])] + ["m%d" % i for i in range(NDMA)]
               + ["ac%d" % t for t in range(R)] + ["al%d" % t for t in range(R)] + ["lc", "ll"])
+QS = "vstgyx"
+
+
+def graph(ops, par):
+    f, ga, wake, local, far, fix, more = par
+    cost = [{q: (f * (v[1] + (ga - OPT["ga"]) * o["gath"]) + fix + (more if q == "s" else 0.0) if o["kind"] == "c" else v[1])
+             for q, v in o["alts"].items()} for o in ops]
+    lat = [o["lat"] + {"d": local, "r": far}.get(o["kind"], 0.0) for o in ops]
+    above, pre, suc = [], [], [[] for _ in ops]
+    for i, o in enumerate(ops):
+        known, mine = 0, []
+        for j in sorted(o["deps"] | o["soft"], reverse=True):
+            if not known >> j & 1 or ops[j]["lat"] > 100.0:
+                mine.append((j, lat[j] if o["kind"] == "x" else 0.0 if j in o["soft"] else lat[j] + wake))
+                suc[j].append((i, mine[-1][1]))
+            known |= above[j] | 1 << j
+        above.append(known)
+        pre.append(mine)
+    return cost, lat, pre, suc, above
+
+
+def place(order, on, edges, base, low, choose, inside, cost):
+    S, E, end, lean = {q: [-1.0] for q in QS}, {q: [low[q]] for q in QS}, {}, OPT["lean"]
+    for i in order:
+        ready = base[i]
+        for (j, d) in edges[i]:
+            if inside[j] and end[j] + d > ready:
+                ready = end[j] + d
+        best = None
+        for q in (cost[i] if i in choose else on[i]):
+            c, s, e = cost[i][q], S[q], E[q]
+            k = m = len(e)
+            at = ready
+            if e[-1] > ready:
+                while k > 1 and e[k - 1] > ready:
+                    k -= 1
+                if e[0] > at:
+                    at = e[0]
+                while k < m and at + c > s[k]:
+                    at = e[k]
+                    k += 1
+            if best is None or at + c < best[0] + (lean * (best[0] - best[2]) if best[1] == "v" else 0.0):
+                best = (at + c, q, at, k)
+        end[i], on[i] = best[0], best[1]
+        S[best[1]].insert(best[3], best[2])
+        E[best[1]].insert(best[3], best[0])
+    return end
+
+
+def search(ops, sets, seq, on, moves, heat, rng):
+    G = [graph(ops, par) for par in sets]
+    n, ns, none = len(ops), len(sets), set()
+    above = G[0][4]
+    fin, rest = [[0.0] * n for _ in sets], [[0.0] * n for _ in sets]
+
+    def survey(first, last):
+        for s in range(ns):
+            cost, lat, pre, suc = G[s][:4]
+            for (f, e, low, near, part) in ((fin[s], pre, None, seq[:first][::-1], seq[first:]),
+                                            (rest[s], suc, lat, seq[last + 1:], seq[:last + 1][::-1])):
+                free = {}
+                for i in near:
+                    if on[i] not in free:
+                        free[on[i]] = f[i]
+                for i in part:
+                    q = on[i]
+                    at = free.get(q, 0.0)
+                    if low and low[i] > at:
+                        at = low[i]
+                    for (j, d) in e[i]:
+                        if f[j] + d > at:
+                            at = f[j] + d
+                    free[q] = f[i] = at + cost[i][q]
+        return [max(r) for r in rest]
+
+    span = survey(0, n - 1)
+    norm = [span[0] / x / ns for x in span]
+    best, keep = span[0], (list(seq), list(on), span)
+    inside = [False] * n
+    for it, u in enumerate(rng.random((moves, 12)).tolist()):
+        w = int(OPT["wide"] * (0.3 + u[0]))
+        first = max(0, int(u[1] * n) - w // 2)
+        last = min(n - 1, first + w)
+        W = seq[first:last + 1]
+        for i in W:
+            inside[i] = True
+        before, after, edge, old = {}, {}, [], 0.0
+        for i in seq[max(0, first - 150):first][::-1]:
+            before.setdefault(on[i], i)
+        for i in seq[last + 1:last + 150]:
+            after.setdefault(on[i], i)
+        for s in range(ns):
+            cost, lat, pre, suc = G[s][:4]
+            f, r, head, tail, top = fin[s], rest[s], {}, {}, 0.0
+            for i in W:
+                a = 0.0
+                for (j, d) in pre[i]:
+                    if not inside[j] and f[j] + d > a:
+                        a = f[j] + d
+                head[i], a = a, lat[i]
+                for (j, d) in suc[i]:
+                    if not inside[j] and r[j] + d > a:
+                        a = r[j] + d
+                tail[i], a = a, f[i] - cost[i][on[i]] + r[i]
+                if a > top:
+                    top = a
+            lo = {q: (f[before[q]] if q in before else 0.0) for q in QS}
+            hi = {q: (r[after[q]] if q in after else 0.0) for q in QS}
+            edge.append((head, tail, lo, hi))
+            old += max([top] + [lo[q] + hi[q] for q in QS]) * norm[s]
+        s = int(u[2] * ns)
+        cost, lat, pre, suc = G[s][:4]
+        f, (head, tail, lo, hi) = fin[s], edge[s]
+        noise = (rng.standard_normal(len(W)) * (rng.random(len(W)) < u[4] * OPT["some"]) * (2 * u[3] * OPT["shake"])).tolist()
+        key = {i: f[i] - cost[i][on[i]] + x for i, x in zip(W, noise)}
+        if u[8] < OPT["chain"]:
+            x, far = W[int(u[9] * len(W))], -OPT["pull"] * math.log(u[10] + 1e-9)
+            for i in W:
+                if u[11] < 0.5 and (i == x or above[x] >> i & 1):
+                    key[i] -= far
+                if u[11] >= 0.5 and (i == x or above[i] >> x & 1):
+                    key[i] += far
+        for i in W:
+            for (j, d) in pre[i]:
+                if inside[j] and key[j] >= key[i]:
+                    key[i] = key[j] + 1e-3
+        on2, choose, open_ = list(on), none, [i for i in W if len(cost[i]) > 1]
+        if open_:
+            for x in rng.random((int(u[5] * (OPT["flips"] + 1)), 2)).tolist():
+                i = open_[int(x[0] * len(open_))]
+                other = [q for q in cost[i] if q != on[i]]
+                on2[i] = other[int(x[1] * len(other))]
+            if u[6] < OPT["free"]:
+                choose = set(i for i, x in zip(open_, rng.random(len(open_)).tolist()) if x < 0.3)
+        end = place(sorted(W, key=key.get), on2, pre, head, lo, choose, inside, cost)
+        back = place(sorted(W, key=lambda i: -end[i] - 1e-6 * i), on2, suc, tail, hi, none, inside, cost)
+        end = place(sorted(W, key=lambda i: 1e-6 * i - back[i]), on2, pre, head, lo, none, inside, cost)
+        mid = sorted(W, key=lambda i: (end[i] - cost[i][on2[i]], end[i], i))
+        new = 0.0
+        for s in range(ns):
+            cost, pre = G[s][0], G[s][2]
+            head, tail, lo, hi = edge[s]
+            free, e, top = dict(lo), {}, 0.0
+            for i in mid:
+                q = on2[i]
+                at = free[q] if free[q] > head[i] else head[i]
+                for (j, d) in pre[i]:
+                    if inside[j] and e[j] + d > at:
+                        at = e[j] + d
+                free[q] = e[i] = at = at + cost[i][q]
+                if at + tail[i] > top:
+                    top = at + tail[i]
+            new += max([top] + [free[q] + hi[q] for q in QS]) * norm[s]
+        for i in W:
+            inside[i] = False
+        for i in open_:
+            if on2[i] != on[i]:
+                new += OPT["price"] * cost[i]["v"] * ((on2[i] == "v") - (on[i] == "v")) if "v" in cost[i] else 0.0
+        if new <= old - heat * (1.0 - it / moves) * math.log(u[7] + 1e-12) and (mid != W or on2 != on):
+            seq[first:last + 1] = mid
+            on[:] = on2
+            span = survey(first, last)
+            start = [fin[0][i] - G[0][0][i][on[i]] for i in range(n)]
+            seq.sort(key=lambda i: start[i])
+            now = sum(a * b for a, b in zip(span, norm))
+            if now < best:
+                best, keep = now, (list(seq), list(on), span)
+    return keep
 
 
 def plan(ops):
-    n, dep = len(ops), OPT["dep"]
-    rng = np.random.default_rng(OPT["seed"])
-    pre = [[(j, 0.0 if j in o["soft"] and o["kind"] != "x" else ops[j]["lat"] + dep) for j in o["deps"] | o["soft"]] for o in ops]
-    least = [min(c for (_, c) in o["alts"].values()) for o in ops]
-    alts = [[(q, o["alts"][q][1]) for q in o["alts"]] for o in ops]
-    lat = [o["lat"] for o in ops]
-
-    def once(w, pen):
-        w, pen = w.tolist(), pen.tolist()
-        level = [0.0] * n
-        for i in range(n - 1, -1, -1):
-            level[i] += w[i] * least[i] + lat[i] + dep
-            for (j, _) in pre[i]:
-                if level[j] < level[i]:
-                    level[j] = level[i]
-        busy, end, res = {q: [] for q in "vstgyx"}, [0.0] * n, [None] * n
-        for i in sorted(range(n), key=lambda k: -level[k]):
-            ready, best = 0.0, None
-            for (j, d) in pre[i]:
-                if end[j] + d > ready:
-                    ready = end[j] + d
-            for (q, cost) in alts[i]:
-                at, line = ready, busy[q]
-                k = len(line)
-                while k > 0 and line[k - 1][1] > at:
-                    k -= 1
-                while k < len(line) and at + cost > line[k][0]:
-                    at = line[k][1]
-                    k += 1
-                score = at + cost + (pen[i] * cost if q == "v" else 0.0)
-                if best is None or score < best[0]:
-                    best = (score, q, at, cost, k)
-            res[i], end[i] = (best[1], best[2]), best[2] + best[3]
-            busy[best[1]].insert(best[4], (best[2], end[i]))
-        return max(end[i] + lat[i] for i in range(n)), res
-
-    w, pen = np.array([OPT["w0"].get(o["key"][3:5], 1.0) for o in ops]), np.full(n, OPT["pen0"])
-    top, res = once(w, pen)
-    names = sorted(set(o["key"] for o in ops))
-    same = np.array([names.index(o["key"]) for o in ops])
-    for it in range(OPT["tries"]):
-        w2, pen2 = w.copy(), pen.copy()
-        for arr, lo, hi in ((w2, 0.05, OPT["whi"]), (pen2, -1.0, 4.0)):
-            k, val = rng.random(n) < OPT["pm"], rng.uniform(lo, hi, n)
-            arr[k[same]] = val[same][k[same]]
-        span, r = once(w2, pen2)
-        if span <= top:
-            top, res, w, pen = span, r, w2, pen2
-    return refine(ops, sorted(range(n), key=lambda k: (res[k][1], k)), [r[0] for r in res])
-
-
-def refine(ops, seq, on):
     n, sets = len(ops), OPT["fine"]
-    ns = len(sets)
     rng = np.random.default_rng(OPT["seed"])
-    above, pre = [0] * n, []
-    for i, o in enumerate(ops):
-        hard, mine = 0, []
-        for j in sorted(o["deps"] | o["soft"], reverse=True):
-            if not hard >> j & 1 or ops[j]["lat"] > 100.0:
-                mine.append(j)
-            hard |= above[j]
-        above[i] = hard | sum(1 << j for j in o["deps"] | o["soft"])
-        pre.append(mine)
-    edge, back, cost, wake, soon = [], [], [], [], []
-    for (f, ga, dep, early, local, far, issue, fix, more) in sets:
-        lat = [o["lat"] + {"d": local, "r": far}.get(o["kind"], 0.0) for o in ops]
-        e = [[(j, -1e6 if j in ops[i]["soft"] and ops[i]["kind"] != "x" else lat[j]) for j in pre[i]] for i in range(n)]
-        wake.append([0.0 if o["kind"] == "x" else dep for o in ops] + [0.0])
-        soon.append([0.0 if o["kind"] == "x" else early for o in ops] + [0.0])
-        b = [[] for _ in range(n + 1)]
-        for i in range(n):
-            for (j, d) in e[i]:
-                b[j].append((i, d))
-        e.append([(i, lat[i]) for i in range(n) if not b[i]])
-        for (i, d) in e[n]:
-            b[i].append((n, d))
-        edge.append(e)
-        back.append(b)
-        cost.append([{q: (f * (o["alts"][q][1] + (ga - OPT["ga"]) * o["gath"]) + fix + (more if q == "s" else 0.0) if o["kind"] == "c" else
-                          o["alts"][q][1] + (issue if o["kind"] == "r" else 0.0)) for q in o["alts"]} for o in ops])
-    ej = np.array([j for i in range(n + 1) for (j, d) in edge[0][i]])
-    ei = np.array([i for i in range(n + 1) for (j, d) in edge[0][i]])
-    ed = [np.array([d for i in range(n + 1) for (j, d) in edge[s][i]]) for s in range(ns)]
-    wk = np.array(wake)
-    fin, rest, idle = ([[0.0] * (n + 1) for _ in sets] for _ in range(3))
-
-    def survey(seq, on, first):
-        pos, prev, nxt, seen = [n] * (n + 1), [None] * n, [None] * n, {}
-        for k, i in enumerate(seq):
-            pos[i] = k
-            j = prev[i] = seen.get(on[i])
-            if j is not None:
-                nxt[j] = i
-            seen[on[i]] = i
-        span, over, held = [], [], []
-        p = np.array(pos)
-        qi = np.array([i for i in range(n) if prev[i] is not None])
-        qj = np.array([j for j in prev if j is not None])
-        for s in range(ns):
-            f, r, e, b, c, w, y, fr = fin[s], rest[s], edge[s], back[s], cost[s], wake[s], soon[s], idle[s]
-            for k in range(first, n):
-                i = seq[k]
-                j = prev[i]
-                at, sig = 0.0 if j is None else f[j], -1e9
-                fr[i] = at - y[i]
-                for (j, d) in e[i]:
-                    if f[j] + d > sig:
-                        sig = f[j] + d
-                if sig >= at - y[i]:
-                    at = sig + w[i]
-                f[i] = at + c[i][on[i]]
-            for k in range(n - 1, -1, -1):
-                i = seq[k]
-                j = nxt[i]
-                at = 0.0 if j is None else r[j]
-                for (j, d) in b[i]:
-                    x = r[j] + d + (w[j] if f[i] + d >= fr[j] else 0.0)
-                    if x > at:
-                        at = x
-                r[i] = at + c[i][on[i]]
-            top = max(f[j] + d for (j, d) in e[n])
-            span.append(top)
-            fa, ra, ia = np.array(f), np.array(r), np.array(fr)
-            sig = fa[ej] + ed[s]
-            late = sig >= ia[ei]
-            val, val2 = sig + np.where(late, wk[s][ei], 0.0) + ra[ei], fa[qj] + ra[qi]
-            a, z = np.flatnonzero(val > top - 600.0), np.flatnonzero(val2 > top - 600.0)
-            lst = (list(zip(val[a].tolist(), p[ej[a]].tolist(), p[ei[a]].tolist()))
-                   + list(zip(val2[z].tolist(), p[qj[z]].tolist(), p[qi[z]].tolist())))
-            lst.sort(reverse=True)
-            over.append(lst)
-            z = np.flatnonzero(val2 > top - OPT["near"])
-            held += list(zip(qi[z].tolist(), qj[z].tolist()))
-            for i in ei[np.flatnonzero(late & (val > top - OPT["near"]) & (ei < n))].tolist():
-                if nxt[i] is not None:
-                    held.append((nxt[i], i))
-        return pos, prev, nxt, span, over, held
-
-    def attempt(mid, first, last, on2):
-        before, after = {}, {}
-        for i in seq[first:last + 1]:
-            if on[i] not in before:
-                before[on[i]] = prev[i]
-            after[on[i]] = nxt[i]
-        for i in mid:
-            q = on2[i]
-            if q not in before:
-                before[q] = next((seq[k] for k in range(first - 1, -1, -1) if on[seq[k]] == q), None)
-                after[q] = next((seq[k] for k in range(last + 1, n) if on[seq[k]] == q), None)
-        total, nexts = 0.0, set(after.values())
-        for s in range(ns):
-            f, r, e, b, c, w, y, fr = fin[s], rest[s], edge[s], back[s], cost[s], wake[s], soon[s], idle[s]
-            top = span[s] - 600.0
-            for (v, a, z) in over[s]:
-                if a < first and z > last and (z == n or seq[z] not in nexts):
-                    top = v
-                    break
-            old = [f[i] for i in mid]
-            free = {q: (0.0 if j is None else f[j]) for q, j in before.items()}
-            for i in mid:
-                q = on2[i]
-                at, sig = free[q], -1e9
-                for (j, d) in e[i]:
-                    if f[j] + d > sig:
-                        sig = f[j] + d
-                if sig >= at - y[i]:
-                    at = sig + w[i]
-                at += c[i][q]
-                free[q] = f[i] = at
-                for (j, d) in b[i]:
-                    if pos[j] > last and j not in nexts:
-                        x = at + d + r[j] + (w[j] if at + d >= fr[j] else 0.0)
-                        if x > top:
-                            top = x
-            for q, i in after.items():
-                if i is not None:
-                    at, sig = free[q], max([f[j] + d for (j, d) in e[i]] + [-1e9])
-                    if sig >= at - y[i]:
-                        at = sig + w[i]
-                    if at + r[i] > top:
-                        top = at + r[i]
-            for i, v in zip(mid, old):
-                f[i] = v
-            total += top / norm[s]
-        return total
-
-    def exact(seq2, on2, first):
-        total, before = 0.0, {}
-        for k in range(first - 1, -1, -1):
-            before.setdefault(on[seq[k]], seq[k])
-        for s in range(ns):
-            f, e, c, w, y = list(fin[s]), edge[s], cost[s], wake[s], soon[s]
-            free = {q: f[j] for q, j in before.items()}
-            for i in seq2[first:]:
-                q = on2[i]
-                at, sig = free.get(q, 0.0), -1e9
-                for (j, d) in e[i]:
-                    if f[j] + d > sig:
-                        sig = f[j] + d
-                if sig >= at - y[i]:
-                    at = sig + w[i]
-                free[q] = f[i] = at + c[i][q]
-            total += max(f[j] + d for (j, d) in e[n]) / norm[s]
-        return total
-
-    def rebuild(s, first, last):
-        f, r, e, b, c = fin[s], rest[s], edge[s], back[s], cost[s]
-        part, on2, free = seq[first:last + 1], list(on), {}
-        noise, lean = (rng.random(len(part)) * OPT["noise"]).tolist(), rng.random() * OPT["lean"]
-        pr, left, ready, end = {}, {}, {}, {}
-        for k in range(len(part) - 1, -1, -1):
-            i = part[k]
-            pr[i] = c[i][on[i]] + max([d + pr.get(j, r[j]) for (j, d) in b[i]] + [0.0])
-        for k, i in enumerate(part):
-            pr[i] += noise[k]
-            left[i] = sum(1 for (j, d) in e[i] if pos[j] >= first)
-            if not left[i]:
-                ready[i] = max([f[j] + d for (j, d) in e[i]] + [-1e9])
-        for k in range(first - 1, max(-1, first - 80), -1):
-            free.setdefault(on[seq[k]], f[seq[k]])
-
-        def begin(i, at, q):
-            x = free.get(q, 0.0)
-            return at + wake[s][i] if at >= x - soon[s][i] else x
-
-        mid = []
-        while ready:
-            top, pick = None, None
-            for i, at in ready.items():
-                for q, x in c[i].items():
-                    t = begin(i, at, q)
-                    key = t + (lean * x if q == "v" and len(c[i]) > 1 else 0.0)
-                    if top is None or key < top[0]:
-                        top = (key, q, t)
-            q, until = top[1], top[2] + OPT["look"]
-            for i, at in ready.items():
-                if q in c[i] and begin(i, at, q) <= until:
-                    key = pr[i] - (lean * c[i][q] * 4.0 if q == "v" and len(c[i]) > 1 else 0.0)
-                    if pick is None or key > pick[0]:
-                        pick = (key, i)
-            i = pick[1]
-            free[q] = end[i] = begin(i, ready.pop(i), q) + c[i][q]
-            on2[i] = q
-            mid.append(i)
-            for (j, d) in b[i]:
-                if j in left:
-                    left[j] -= 1
-                    if not left[j]:
-                        ready[j] = max(end.get(x, f[x]) + y for (x, y) in e[j])
-        return mid, on2
-
-    pos, prev, nxt, span, over, held = survey(seq, on, 0)
-    norm = list(span)
-
-    def load(on, some):
-        return sum(cost[0][i]["v"] for i in some if on[i] == "v" and len(cost[0][i]) > 1) * OPT["price"] * ns / norm[0]
-
-    extra = load(on, range(n))
-    best = float(ns)
-    now = best + extra
-    keep, taken, moves = (seq, on), 0, OPT["moves"]
-    for it, u in enumerate(rng.random((moves, 6)).tolist()):
-        if not held:
-            break
-        i, j = held[int(u[0] * len(held))]
-        on2, far = on, int(-math.log(u[2] + 1e-9) * OPT["reach"])
-        if u[1] < OPT["anew"]:
-            wide = int(OPT["wide"] * (0.3 + u[2]))
-            first = max(0, pos[i] - int(wide * u[3]))
-            last = min(n - 1, first + wide)
-            mid, on2 = rebuild(int(u[5] * ns), first, last)
-        elif u[1] < 0.25:
-            x = i if u[2] < 0.5 else j
-            other = [q for q in ops[x]["alts"] if q != on[x]]
-            if not other:
-                continue
-            on2 = list(on)
-            on2[x] = other[int(u[3] * len(other))]
-            first = last = pos[x]
-            mid = [x]
-        elif u[1] < 0.65:
-            for _ in range(far):
-                if prev[j] is not None:
-                    j = prev[j]
-            if above[i] >> j & 1:
-                continue
-            first, last = pos[j], pos[i]
-            part = seq[first:last]
-            mid = [x for x in part if above[i] >> x & 1] + [i] + [x for x in part if not above[i] >> x & 1]
-        else:
-            for _ in range(far):
-                if nxt[i] is not None:
-                    i = nxt[i]
-            first, last = pos[j], pos[i]
-            part = seq[first + 1:last + 1]
-            mid = [x for x in part if not above[x] >> j & 1] + [j] + [x for x in part if above[x] >> j & 1]
-            if mid[0] == j:
-                continue
-        total = attempt(mid, first, last, on2) + load(on2, mid) - load(on, mid) + extra
-        limit = now - OPT["heat"] * (1.0 - it / moves) * math.log(u[4] + 1e-12)
-        if total <= limit + OPT["loose"] and (abs(total - now) > 1e-9 or u[5] < OPT["flat"]):
-            seq2 = seq[:first] + mid + seq[last + 1:]
-            if exact(seq2, on2, first) + load(on2, mid) - load(on, mid) + extra > limit:
-                continue
-            seq, on = seq2, on2
-            taken += 1
-            pos, prev, nxt, span, over, held = survey(seq, on, first)
-            if taken % OPT["every"] == 0:
-                s = taken // OPT["every"] % ns
-                seq = sorted(seq, key=lambda x: (fin[s][x] - cost[s][x][on[x]], pos[x]))
-                pos, prev, nxt, span, over, held = survey(seq, on, 0)
-            extra = load(on, range(n))
-            now = sum(span[s] / norm[s] for s in range(ns)) + extra
-            if now - extra < best:
-                best, keep = now - extra, (seq, on)
-    seq, on = keep
-    OPT["span"] = [int(x) for x in survey(seq, on, 0)[3]]
+    cost, lat, pre, suc = graph(ops, sets[0])[:4]
+    tail = list(lat)
+    for i in range(n - 1, -1, -1):
+        tail[i] = min(cost[i].values()) + max([lat[i]] + [d + tail[j] for (j, d) in suc[i]])
+    on = [list(x)[0] for x in cost]
+    end = place(sorted(range(n), key=lambda i: 1e-6 * i - tail[i]), on, pre, [0.0] * n, {q: 0.0 for q in QS}, set(range(n)), [True] * n, cost)
+    seq = sorted(range(n), key=lambda i: (end[i] - cost[i][on[i]], end[i], i))
+    for (k, moves, heat) in OPT["stages"]:
+        seq, on, span = search(ops, sets[:k], seq, on, moves, heat, rng)
+    OPT["span"] = [int(x) for x in span]
     res = [None] * n
     for k, i in enumerate(seq):
         res[i] = (on[i], k)
@@ -447,8 +305,8 @@ def rank_program(g, core, T, topo):
             if w:
                 hist[name] = [h for h in hist.get(name, []) if h[1] & ~m]
             hist.setdefault(name, []).append((me, m, w))
-        key = str([x[:3] if x[0] not in ("twf", "lq", "ls") else x[0] for x in wr + rd[:1] if isinstance(x, tuple)])
-        ops.append({"alts": alts, "deps": deps, "soft": soft, "kind": kind, "sem": sem, "cnt": cnt, "lat": lat, "key": key,
+        ops.append({"alts": alts, "deps": deps, "soft": soft, "kind": kind, "sem": sem, "cnt": cnt, "lat": lat,
+                    "key": str([x[:3] for x in wr + rd[:1] if isinstance(x, tuple)]),
                     "gath": size(wr[0]) if any(isinstance(x, tuple) and x[4] is not None for x in rd) else 0})
         return me
 
@@ -459,9 +317,6 @@ def rank_program(g, core, T, topo):
             per = 0.5
         return max(64, size(out) * per) * cy
 
-    def scost(out, a):
-        return 65 + ga * size(out) if a[4] is not None else max(64, size(out)) * cy + OPT["sfix"]
-
     def tsv(out, a, s1, o0, s2=None, o1=None):
         if o1 is None:
             return (lambda: g.vector.tensor_scalar(real(out), real(a), real(s1), None, o0), vcost(out, a, 1))
@@ -469,7 +324,7 @@ def rank_program(g, core, T, topo):
 
     def acs(out, a, f, bias=0.0, scale=1.0, acc=None):
         return (lambda: g.scalar.activation(real(out), real(a), f, bias=real(bias), scale=scale, accum_out=real(acc)),
-                scost(out, a) + (20 if acc else 0))
+                (65 + ga * size(out) if a[4] is not None else max(64, size(out)) * cy) + (20 if acc else 0))
 
     def ts(out, a, s1, o0, s2=None, o1=None):
         add({"v": tsv(out, a, s1, o0, s2, o1)}, [a, s1, s2], [out])
@@ -528,10 +383,10 @@ def rank_program(g, core, T, topo):
 
     nd = [0]
 
-    def dma(q, out, a, rd, wr, kb=0):
+    def dma(q, out, a, rd, wr, kb=0, after=()):
         nd[0] += 1
-        add({q: (lambda: queue[q].dma_start(out, a), 100.0)}, rd, wr, kind="d",
-            sem="m%d" % (nd[0] - 1), cnt=16, lat=OPT["dma"] + 3.5 * kb)
+        return add({q: (lambda: queue[q].dma_start(out, a), 100.0)}, rd, wr, kind="d",
+                   sem="m%d" % (nd[0] - 1), cnt=16, lat=OPT["dma"] + 3.5 * kb, after=after)
 
     def bank(b, a, n):
         return A("ps", 512 * b + a, 512 * b + a + n)
@@ -540,44 +395,44 @@ def rank_program(g, core, T, topo):
         return A(name, c, c + 1)
 
     def tw(t, a=0, b=24):
-        return A("twf", 48 * t + 6 + a, 48 * t + 6 + b)
+        return A("twf", 64 * t + 22 + a, 64 * t + 22 + b)
 
     def steps(y, m, p, a, b, up=True):
         now, before = A(y, a + 1, b + 1), A(y, a, b)
         scan(A(m, a, b), now if up else before, before if up else now, op.max, op.subtract)
         scan(A(p, a, b), A(m, a, b), A("pos", a, b), op.add, op.min, (a - 191) / 32.0)
 
-    def where(k, cnt, a, b, thr, scale, j):
-        flags = A("junk", C * j + a, C * j + b)
-        if k in OPT["jv"]:
-            ts(flags, A(cnt, a, b), scale, op.mult, col("kn", thr), op.is_gt)
-            scan(A("tally", a, b), flags, A("zero", a, b), op.add, op.add, a - 128.0)
-            ts(col("bw", k), col("tally", b - 1), 128.0, op.add)
-        else:
-            act(flags, A(cnt, a, b), fn.Sign, col("kb", thr), scale, col("acc", k))
-            ts(col("bw", k), col("acc", k), 0.5, op.mult, (b - a) / 2 + a, op.add)
+    def cum(a, b):
+        return A("cum", 16 + a, 16 + b)
 
-    def compare(name, tiles, by_s):
-        for (at, a, b, planes) in tiles:
-            for s, c in enumerate(planes):
-                part = lambda lo, hi: A(name, 4 * (at + lo - a) + s, 4 * (at + hi - a), 4)
-                if c == 12:
-                    tt(part(a, b), A("dh", a, b), A("dr", a, b), op.is_equal)
-                    continue
-                k, lo, piv = min(max(16 * c + 16, a), b), a, col("dh", 16 * c + 15)
-                if c in by_s and a == 0:
-                    lo = min(k, by_s[c])
-                    act(A("sg", M * (c % 8), M * (c % 8) + lo), A("dr", 0, lo), fn.Sign, piv, -1.0)
-                    act(part(0, lo), A("sg", M * (c % 8), M * (c % 8) + lo), fn.Relu, 0.0, -1.0)
-                if lo < k:
-                    ts(part(lo, k), A("dr", lo, k), piv, op.is_gt)
-                if k < b:
-                    ts(part(k, b), A("dr", k, b), piv, op.is_ge)
+    def where(k, cnt, a, thr, scale, j):
+        act(A("junk", C * j, C * j + size(cnt)), cnt, fn.Sign, col("kb", thr), scale, col("acc", k))
+        ts(col("bw", k), col("acc", k), 0.5, op.mult, size(cnt) / 2 + a, op.add)
+
+    def plane(c, lo, hi):
+        at = (128, 0, TT)[(c - 1) // 4]
+        return A("fl", 4 * (at + lo) + (c - 1) % 4, 4 * (at + hi), 4)
+
+    def compare(c, by_s):
+        w, piv = 16 * c, col("dh", 16 * c + 15)
+        sg, out, acc = A("sg", M * (c - 1), M * (c - 1) + w), plane(c, 0, w), col("ra", c)
+        if c in by_s:
+            add({"s": acs(sg, A("dr", 0, w), fn.Sign, piv, -1.0), "v": tsv(sg, A("dr", 0, w), piv, op.is_gt, -1.0, op.mult)},
+                [A("dr", 0, w), piv], [sg])
+            act(out, sg, fn.Relu, 0.0, -1.0, acc)
+        else:
+            ts(out, A("dr", 0, w), piv, op.is_gt)
+            add({"v": (lambda: g.vector.tensor_reduce(real(acc), real(out), AxisListType.X, op.add), max(64, w) * cy),
+                 "s": acs(sg, out, fn.Copy, 0.0, 1.0, acc)}, [out], [sg, acc])
+
+    def again(a, b, k):
+        mm(bank(k, 0, b - a), A("qu2"), A("su2"), A("qx", a, b), A("sx", a, b))
+        mov(A("st", a, b), bank(k, 0, b - a))
 
     dma("s", real(A("ut")), T.u[:], [], [A("ut")], 200)
-    dma("y", real(A("xi", 0, 4 * M)), T.x[:, 0:4 * M], [], [A("xi", 0, 4 * M)], 360)
-    dma("y", real(A("xi", 4 * M, 4 * C)), T.x[:, 4 * M:4 * C], [], [A("xi", 4 * M, 4 * C)], 520)
-    dma("s", real(A("twi")), T.tw[:], [], [A("twi")], 540)
+    j = dma("y", real(A("xi", 0, 4 * M)), T.x[:, 0:4 * M], [], [A("xi", 0, 4 * M)], 332)
+    j = dma("y", real(A("xi", 4 * M, 4 * C)), T.x[:, 4 * M:4 * C], [], [A("xi", 4 * M, 4 * C)], 520, [j])
+    dma("y", real(A("twi")), T.tw[:], [], [A("twi")], 520, [j])
     dma("y", real(cast(A("wq"), dt.uint8)), T.wc[:], [col("xi", 4 * M)], [A("wq")], 256)
     dma("y", real(A("wp")), T.ws[:], [col("xi", 4 * M)], [A("wp")], 64)
     dma("y", real(A("vt")), T.v[:], [col("wq", 0)], [A("vt")], 128)
@@ -588,23 +443,21 @@ def rank_program(g, core, T, topo):
     iota(A("i16"), [[0, 24], [1, 16]])
     iota(A("iw"), [[16, 24]])
     mov(A("pos"), A("iob"), 1.0 / 32)
-    mov(A("e", 0, C), A("iob"), -1.0, -48.0)
-    fill(A("f0", 12 * M, 16 * M), early=True)
-    if OPT["split"]:
-        fill(A("zero"), early=True)
-        fill(A("fl", 4 * NL, 4 * MS))
-        fill(A("fl", 12 * MS, 16 * MS))
-        fill(A("fl", 16 * MS + M, 16 * M))
+    fill(A("zero"), early=True)
+    fill(A("fl", 4 * 80, 4 * M), early=True)
+    fill(A("fl", 4 * (TT + MS), 4 * (TT + M)), early=True)
     fill(A("xi", 4 * C, 4 * C + 128))
     fill(A("sl", 0, 128))
     ms(A("ones"), 1.0)
     sel(A("bo1"), A("ones"), [[-16, 8], [0, 64]], op.is_ge, 0, 1)
     sel(A("bo2"), A("bo1"), [[16, 8], [0, 64]], op.is_ge, 15, -1)
+    fill(A("et", 0, 4))
+    fill(A("et", 516, 520))
+    sel(A("et", 4, 516), A("ones"), [[-1, 512]], op.is_equal, 0, 4)
+    fill(col("lv", 0))
+    fill(cum(-1, 0))
     for p in range(4):
-        sel(A("et", 512 * p, 512 * p + 512), A("ones"), [[-1, 512]], op.is_equal, p, 4)
-    fill(A("lv", 0, DUP))
-    for p in range(4 if OPT["es"] else 0):
-        fill(A("hx", PL * p + M + DUP, PL * p + PL))
+        fill(A("hx", PL * p, PL * p + OFF - DUP))
     ms(col("tie", 0), EPS)
     ms(col("tie", 1), -EPS)
     for name in ("yo", "yg", "yq"):
@@ -615,14 +468,16 @@ def rank_program(g, core, T, topo):
     ts(col("ri", 2), A("pi"), 3, op.bitwise_and)
     cp(A("rf"), A("ri"))
     rf = col("rf", 0)
-    for k, c, a, b in ((0, 0, 16.0, 15.5), (1, 0, 16.0, M - MS + 15.5), (2, 0, 16.0, -128.5), (3, 0, 16.0, 127.5), (4, 0, -1.0, LEV + 7.5),
-                       (5, 0, 16.0, 15.5 - 160), (6, 0, 1.0, LEV - 7.5 - MS), (7, 0, 1.0, 0.5), (8, 0, 1.0, 16.5), (9, 0, 1.0, 32.5),
-                       (10, 2, 1.0, 4.0 * 191), (11, 2, 1.0, 4.0 * (191 - NS)), (12, 2, 1.0, 0.0), (13, 2, float(PL), DUP - 1.0)):
+    for k, c, a, b in ((0, 0, 16.0, 15.5), (1, 0, 2.0, 32.0), (2, 0, 16.0, -352.5), (3, 0, 16.0, -96.5), (4, 0, -1.0, LEV + 7.5),
+                       (5, 0, 16.0, 15.5 - 160), (6, 0, 1.0, LEV - 7.5), (7, 0, 1.0, MS + 0.5), (8, 0, 1.0, MS + 16.5), (9, 0, 1.0, MS + 32.5),
+                       (10, 2, 1.0, 4.0 * 191), (11, 2, 1.0, 4.0 * (191 - NS)), (12, 2, 1.0, 4.0 * (DUP - 1))):
         mov(col("kb", k), col("rf", c), a, b)
-    if OPT["jv"]:
-        mov(A("kn", 0, 2), A("kb", 0, 2), -1.0)
     ts(A("cm"), A("i16"), rf, op.is_equal, BIG, op.mult)
-    ts(A("cm", 0, C, 16), A("cm", 0, C, 16), -1.0, op.add)
+    ms(A("cm", 0, C, 16), BIG)
+    ts(A("cmb"), A("i16", 0, M), rf, op.not_equal, BIG, op.mult)
+    iota(A("tb"), [[1, 64]])
+    fill(A("mr"), 256, early=True)
+    fill(col("ra", 0))
     ts(A("keep"), A("cm"), 0.0, op.is_equal)
     ts(A("cm1"), A("i16"), rf, op.is_equal)
     iota(A("i4"), [[0, M // 4], [1, 4]])
@@ -630,156 +485,129 @@ def rank_program(g, core, T, topo):
     ts(A("keep4"), A("i4"), col("rf", 1), op.not_equal)
     mov(A("cm4n"), A("cm4"), 2.0, -BIG)
     mov(A("iw"), A("iw"), 1.0, rf)
+    mov(A("mr", 0, M, 16), A("iw", 0, 12), -1.0, col("kb", 1))
     mov(A("ths", 0, 6), A("iw", 0, 6), -1.0, -145.0)
-    mov(A("ths", 6, 24), A("iw", 0, 18), -1.0, 143.0)
+    fill(A("ths", 6, 20))
+    mov(A("ths", 20, 38), A("iw", 0, 18), -16.0, 16 * 143.0)
     for t in range(R):
-        quant(A("lq", 224 * t + NL, 224 * t + 224), A("ls", 512 * t + C, 512 * t + 512), A("zero" if OPT["zero"] else "fl", 0, 512))
+        quant(A("lq", 224 * t + NL, 224 * t + 224), A("ls", 512 * t + C, 512 * t + 512), A("zero"))
+    quant(A("qf", M, TT), A("sf", M, TT), A("zero"))
     quant(A("qo"), A("so"), A("bo2"))
-    for k in range(2):
-        quant(A("qe", 256 * k, 256 * k + 256), A("se", 256 * k, 256 * k + 256), A("et", 1024 * k, 1024 * k + 1024))
+    for k in range(4):
+        quant(A("qe", 128 * k, 128 * k + 128), A("se", 128 * k, 128 * k + 128), A("et", 4 - k, 516 - k))
     quant(A("qv"), A("sv"), A("vt"))
     quant(A("qu"), A("su"), A("ut"))
     cp(tw(0), A("twi"))
     cp(cast(A("qu2"), dt.uint32), ind(cast(A("qu"), dt.uint32), A("ul")))
     cp(A("su2"), ind(A("su"), A("ul")))
 
-    tt(A("hf"), A("twi"), A("iw"), op.is_lt)
-    cp(A("hw"), A("hf"))
-    for k in range(2):
-        quant(A("qx", M * k, M * k + M), A("sx", M * k, M * k + M), A("xi", 4 * M * k, 4 * M * k + 4 * M))
-        mm(bank(k, 0, M), A("qu2"), A("su2"), A("qx", M * k, M * k + M), A("sx", M * k, M * k + M))
-        mov(A("sr", M * k, M * k + M), bank(k, 0, M))
-    for k in range(2):
-        mov(A("st", M * k, M * k + M), ind(A("sr"), tw(0, 12 * k, 12 * k + 12)))
-        tt(A("d", M * k, M * k + M), A("st", M * k, M * k + M), bank(k, 0, M), op.subtract)
-    tt(A("un"), ind(A("tie", 0, 2), A("hw")), A("d"), op.is_lt)
+    tt(A("hf", 0, 24), A("twi"), A("iw"), op.is_lt)
+    cp(A("hw"), A("hf", 0, 24))
+    for (a, b, k) in ((0, M, 0), (M, C, 1)):
+        quant(A("qx", a, b), A("sx", a, b), A("xi", 4 * a, 4 * b))
+        mm(bank(k, 0, M), A("qu2"), A("su2"), A("qx", a, b), A("sx", a, b))
+        mov(A("sr", a, b), bank(k, 0, M))
+        again(a, b, 2 + k)
+    for (a, b) in ((0, M), (M, C)):
+        tt(A("d", a, b), ind(A("sr"), tw(0, a // 16, b // 16)), A("st", a, b), op.subtract)
+        tt(A("un", a, b), ind(A("tie", 0, 2), A("hw", a // 16, b // 16)), A("d", a, b), op.is_lt)
 
     for t in range(R):
         last = t == R - 1
-        whole = t == 0 or not OPT["split"]
-        parts = [(0, C, 0, M)] if whole else [(0, NS, 0, MS), (NS, C, MS, M)]
+        parts = [(0, C, 0, M)] if t == 0 else [(0, NS, 0, MS), (NS, C, MS, M)]
         for s, (a, b, ka, kb) in enumerate(parts):
             un, n = A("un", a, b), (kb - ka) // 16
-            ra = 0 if whole or s else M - MS
-            rb = ra + kb - ka
-            scan(A("cum", a, b), un, un, op.add, op.max, float(ra))
+            scan(cum(a, b), un, un, op.add, op.max, float(ka))
             ow = A("ow", 16 * s, 16 * s + n)
             if s:
                 for c in range(n):
-                    act(A("junk", C + NL * c, C + NL * c + NL), A("cum", a, b), fn.Sign, col("kb", 7 + c), -1.0, col("acc", 8 + c))
+                    act(A("junk", C + NL * c, C + NL * c + NL), cum(a, b), fn.Sign, col("kb", 7 + c), -1.0, col("acc", 8 + c))
                 ts(ow, A("acc", 8, 8 + n), 0.5, op.mult, NL / 2, op.add)
             else:
                 scan(A("yo", a + 1, b + 1), un, un, op.add, op.max, col("kb", 4))
                 steps("yo", "mo", "po", a, b)
-                where(0, "cum", a, b - 1, 1 if ra else 0, -1.0, 0)
+                where(0, cum(a, b - 1), a, 0, -1.0, 0)
                 ts(A("ow", 0, 16), ind(A("po", a, b), col("bw", 0)), 32.0, op.mult, 191.0, op.add)
-            mov(A("orow", ra, rb), ind(A("pos", a, b), ow))
-            scan(A("oh", ra, rb), A("cm4n", ra, rb), A("orow", ra, rb), op.max, op.min, -8.0)
-            ts(A("ow4", ra // 4, rb // 4), A("oh", ra + 3, rb, 4), 128.0, op.mult, col("kb", 10 + s), op.add)
+            mov(A("orow", ka, kb), ind(A("pos", a, b), ow))
+            scan(A("oh", ka, kb), A("cm4n", ka, kb), A("orow", ka, kb), op.max, op.min, -8.0)
+            ts(A("ow4", ka // 4, kb // 4), A("oh", ka + 3, kb, 4), 128.0, op.mult, col("kb", 10 + s), op.add)
             mov(A("dr", ka, kb), ind(A("d", a, b), ow))
-            if OPT["dm"] and not s:
-                scan(A("dm", ka, kb), A("dr", ka, kb), A("cm", ka, kb), op.max, op.min)
-            else:
-                tt(A("dm", ka, kb), ind(A("d", a, b), ow), A("cm", ka, kb), op.min)
-            scan(A("dh", ka, kb), A("keep", ka, kb), A("dm", ka, kb), op.mult, op.add)
-            mov(A("ct", a, b), ind(A("cum", 0, b), tw(t, a // 16, b // 16)))
-            if OPT["ctm"] and not s:
-                mov(A("cto", ra, rb), ind(A("ct", a, b), ow))
-                scan(A("ctm", ra, rb), A("cto", ra, rb), A("cm4", ra, rb), op.max, op.min)
-            else:
-                tt(A("ctm", ra, rb), ind(A("ct", a, b), ow), A("cm4", ra, rb), op.min)
-            w = (rb - ra) // (1 if s else OPT["xc"])
-            for lo in range(ra, rb, w):
-                src = ind(A("xi", 4 * a, 4 * b), A("ow4", lo // 4, (lo + w) // 4))
-                mov(A("xo", 4 * lo + 4, 4 * (lo + w) + 4), src, 0.5)
-                if s and OPT["xa"]:
-                    mov(A("xa", 4 * lo + 4, 4 * (lo + w) + 4), src, 0.5)
+            tt(A("dm", ka, kb), ind(A("d", a, b), ow), A("cmb", ka, kb), op.max)
+            scan(A("dh", ka, kb), A("cm", ka, kb), A("dm", ka, kb), op.max, op.min)
+            mov(A("ct", a, b), ind(cum(0, b), tw(t, a // 16, b // 16)))
+            mov(A("cto", ka, kb), ind(A("ct", a, b), ow))
+            w = (kb - ka) // (1 if s else 2)
+            for lo in range(ka, kb, w):
+                src, at = ind(A("xi", 4 * a, 4 * b), A("ow4", lo // 4, (lo + w) // 4)), 4 * (DUP + lo)
+                mov(A("xo", at, at + 4 * w), src, 0.5)
+                if s:
+                    mov(A("xa", at, at + 4 * w), src, 0.5)
                 else:
-                    mov(A("xa", 4 * lo + 4, 4 * (lo + w) + 4), A("xo", 4 * lo + 4, 4 * (lo + w) + 4), pool=True)
-            if not s:
-                mov(A("xa", 0, 4), A("xo", 4 * M, 4 * M + 4), pool=True)
-                mov(A("xo", 0, 4), A("xo", 4 * M, 4 * M + 4), pool=True)
-            if not OPT["join"]:
-                scan(A("cth", ra, rb), A("keep4", ra, rb), A("ctm", ra, rb), op.mult, op.add)
-                scan(A("cap", a, b), A("cm", a, b), A("cum", a, b), op.max, op.min)
-        if OPT["join"]:
-            scan(A("cth"), A("keep4"), A("ctm"), op.mult, op.add)
-            scan(A("cap"), A("cm"), A("cum"), op.max, op.min)
+                    mov(A("xa", at, at + 4 * w), A("xo", at, at + 4 * w), pool=True)
+            scan(A("cap", a, b), A("cm", a, b), cum(a, b), op.max, op.min)
+            scan(A("cap2", a, b), A("cm", a, b), cum(a - 1, b - 1), op.max, op.min)
+        for name in ("xo", "xa"):
+            mov(A(name, 0, 4 * DUP), ind(A("xi", 4 * a, 4 * b), A("ow4", (M - DUP) // 4, M // 4)), 0.5)
+        scan(A("ctm"), A("cto"), A("cm4"), op.max, op.min)
+        scan(A("cth"), A("keep4"), A("ctm"), op.mult, op.add)
         ts(A("ctw"), A("cth", 3, M, 4), 4.0, op.mult, col("kb", 12), op.add)
-        ts(A("cw"), A("cap", 15, C, 16), DUP - 1.0, op.add)
-        if whole:
-            names, h = ("f0", "q0", "s0"), M - MS
-            calls = [[(0, 0, M, [0, 1, 2, 3]), (M, 0, M, [4, 5, 6, 7])], [(2 * M, 0, M, [8, 9, 10, 11]), (3 * M, 0, M, [12])]]
-            by_s = [{c: OPT["s0w"] for c in OPT["s0"]}] * 2
-        else:
-            names, h = ("fl", "qf", "sf"), M - MS
-            calls = [[(MS, 0, MS, [0, 1, 2, 3]), (2 * MS, 0, MS, [4, 5, 6, 7]), (3 * MS, 0, MS, [8, 12])],
-                     [(0, MS, M, [0, 1, 2, 3]), (h, MS, M, [4, 5, 6, 7]), (2 * h, MS, M, [8])],
-                     [(4 * MS, MS, M, [9, 10, 11, 12]), (4 * MS + h, 0, MS, [9, 10, 11])]]
-            by_s = [{c: MS for c in OPT["s1"]}, {}, {c: MS for c in OPT["s2"]}]
-        every = [x for tiles in calls for x in tiles]
-        for tiles, on_s in zip(calls, by_s):
-            compare(names[0], tiles, on_s)
-            lo, hi = tiles[0][0], tiles[-1][0] + tiles[-1][2] - tiles[-1][1]
-            quant(A(names[1], lo, hi), A(names[2], lo, hi), A(names[0], 4 * lo, 4 * hi))
-            for x in tiles:
-                mine, wide = [y for y in every if y[1] == x[1]], max(128, x[2] - x[1])
-                mm(bank(2 + (x[1] > 0), 0, wide), A("qo"), A("so"), A(names[1], x[0], x[0] + wide), A(names[2], x[0], x[0] + wide),
-                   x == mine[0], x == mine[-1])
-        for (a, b, ka, kb) in parts:
-            ra = 0 if whole or ka else M - MS
-            out, cnt = A("lv", DUP + ra, DUP + ra + kb - ka), bank(2 + (ka > 0), 0, kb - ka)
-            add({"v": tsv(out, cnt, 48.5, op.is_le), "s": acs(out, cnt, fn.Relu, 49.0, -1.0)}, [cnt], [out])
-        w = M // OPT["zc"]
-        for (at, lo, hi) in [(DUP + x, x, x + w) for x in range(0, M, w)] + [(0, M - DUP, M)]:
-            tt(A("z", 4 * at, 4 * (at + hi - lo)), ind(A("xo", 0, 4 * M + 4), A("ctw", lo // 4, hi // 4)), A("xa", 4 * lo, 4 * hi), op.add)
+        ts(A("cw"), A("cap", 15, C, 16), OFF - 1.0, op.add)
+        scan(A("cim"), A("ct"), A("cm1"), op.add, op.mult)
+        scan(A("cih"), A("keep"), A("cim"), op.mult, op.add)
+        tt(A("uw"), A("cap", 15, C, 16), A("cap2", 15, C, 16), op.subtract)
+        tt(A("ud"), A("cap", 15, C, 16), A("cih", 15, C, 16), op.subtract)
+        tt(A("uc"), A("uw"), A("ud"), op.mult)
+        tt(A("uw"), A("uc"), A("cih", 15, C, 16), op.add)
+        cp(A("cwu"), A("uw"))
+        for c in range(1, 12):
+            compare(c, OPT["both"])
+        for s, (a, b, ka, kb) in enumerate(parts):
+            lo, hi = ka // 16, kb // 16
+            tt(plane(12, ka, kb), A("dh", ka, kb), A("dr", ka, kb), op.is_le)
+            scan(A("r2", ka, kb), A("mr", ka, kb), plane(12, ka, kb), op.min, op.add, 256.0)
+            if s:
+                for c in range(lo, hi):
+                    ts(col("thw", c + s), col("ra", c), col("r2", 16 * c + 15), op.add)
+            else:
+                tt(A("thf", lo, hi), A("ra", lo, hi), A("r2", ka + 15, kb, 16), op.add)
+                cp(A("thw", lo, hi), A("thf", lo, hi))
+            mov(A("thr", ka, kb), ind(A("tb"), A("thw", lo + s, hi + s)))
+        for (lo, tiles) in ((0, ((128, M), (0, 128))), (TT, ((TT, M),))):
+            quant(A("qf", lo, lo + M), A("sf", lo, lo + M), A("fl", 4 * lo, 4 * (lo + M)))
+            for (at, wide) in tiles:
+                mm(bank(2, 0, wide), A("qo"), A("so"), A("qf", at, at + wide), A("sf", at, at + wide), at == 128, at == TT)
+        tt(A("lv", 1, M + 1), A("thr"), bank(2, 0, M), op.is_ge)
+        for (at, lo, hi) in ((DUP, 0, NL), (DUP + NL, NL, M), (0, M - DUP, M)):
+            tt(A("z", 4 * at, 4 * (at + hi - lo)), ind(A("xo"), A("ctw", lo // 4, hi // 4)), A("xa", 4 * (DUP - 1 + lo), 4 * (DUP - 1 + hi)), op.add)
         quant(A("qz"), A("sz"), A("z"))
         for p in range(4):
             mm(bank(4 + p, 0, M + DUP), A("wq", 128 * p, 128 * p + 128), A("wp", 128 * p, 128 * p + 128), A("qz"), A("sz"))
-            mov(A("hx", PL * p, PL * p + M + DUP), bank(4 + p, 0, M + DUP), 0.03125)
-        for (a, b) in ((0, 256), (256, C)) if OPT["se"] else ((0, C),):
-            for p in range(4):
-                tt(A("e", C * (p + 1) + a, C * (p + 1) + b), ind(A("hx", PL * p, PL * p + M + DUP), A("cw", a // 16, b // 16)),
-                   A("xi", 4 * a + p, 4 * b, 4), op.add)
-        tt(A("g1"), ind(A("lv", 0, M + DUP), A("cw")), A("un"), op.min)
-        for k in range(2):
-            mov(A("g2", M * k, M * k + M), ind(A("g1"), tw(t, 12 * k, 12 * k + 12)))
-        scan(A("gn"), A("g1"), A("g2"), op.add, op.add)
-        if OPT["yg"]:
-            mov(A("yg", 1, C + 1), A("gn"), 1.0, col("kb", 4))
-        else:
-            scan(A("yg", 1, C + 1), A("g1"), A("g2"), op.add, op.add, col("kb", 4))
+            mov(A("hx", PL * p + OFF - DUP, PL * p + PL), bank(4 + p, 0, M + DUP), 0.03125)
+        for p in range(4):
+            tt(A("e", C * p, C * p + C), ind(A("hx", PL * p, PL * p + PL), A("cw")), A("xi", p, 4 * C, 4), op.add)
+        for lo in (0, M):
+            mov(A("gone", lo, lo + M), ind(A("lv"), A("cwu", lo // 16, (lo + M) // 16)))
+        scan(A("gn"), A("gone"), A("zero", 0, C), op.add, op.add)
+        scan(A("yg", 1, C + 1), A("gone"), A("zero", 0, C), op.add, op.add, col("kb", 4))
         steps("yg", "mg", "pg", 0, C)
-        where(4, "gn", 0, C - 1, 5, -1.0, 2)
+        where(4, A("gn", 0, C - 1), 0, 5, -1.0, 2)
         ts(A("lqw", 0, 16), ind(A("pg"), col("bw", 4)), 32.0, op.mult, 191.0, op.add)
-        scan(A("ncs", 0, MS), A("gn", 0, MS), A("e", 0, MS), op.min, op.add, 256.0)
-        scan(A("ncs", MS, C), A("gn", MS, C), A("e", MS, C), op.max, op.add)
-        mov(A("yq", 1, C + 1), A("ncs"), 1.0, col("kb", 6))
+        scan(A("ncs"), A("gone"), A("ones", 0, C), op.add, op.subtract, float(MS))
+        scan(A("yq", 1, C + 1), A("gone"), A("ones", 0, C), op.add, op.subtract, col("kb", 6))
         steps("yq", "mq", "pq", 0, C, False)
-        where(6, "ncs", 0, 351, 2, 1.0, 3)
-        where(7, "ncs", 256, C - 1, 3, 1.0, 4)
-        ts(A("lqw", 16, 48), ind(A("pq"), A("bw", 6, 8)), 32.0, op.mult, 191.0 + C, op.add)
-        lw, qw = A("lqw", 10, 16), A("lqw", 16, 34)
-        if t in OPT["es"]:
-            mov(A("lr", 0, NL), ind(A("pos"), lw))
-            mov(A("lr", NL, M), ind(A("cum"), lw))
-            scan(A("lh", 0, NL), A("cm4n", 0, NL), A("lr", 0, NL), op.max, op.min, -8.0)
-            ts(A("l4", 0, 24), A("lh", 3, NL, 4), 128.0, op.mult, col("kb", 10), op.add)
-            scan(A("lm"), A("lr", NL, M), A("cm4", 0, NL), op.max, op.min)
-            scan(A("lh", NL, M), A("keep4", 0, NL), A("lm"), op.mult, op.add)
-            ts(A("l4", 24, 48), A("lh", NL + 3, M, 4), col("kb", 13), op.add)
-            mov(A("xl"), ind(A("xi", 0, 4 * C), A("l4", 0, 24)))
-            tt(A("sl", 128, 512), ind(A("hx"), A("l4", 24, 48)), A("xl"), op.add)
-        else:
-            for p in range(4):
-                mov(A("sl", 128 + p, 512, 4), ind(A("e", C * (p + 1), C * (p + 2)), lw))
-        quant(A("qs"), A("s0", 4 * M, 4 * M + 128), A("sl"))
+        where(6, A("ncs", 0, 128), 0, 2, 1.0, 3)
+        where(7, A("ncs", 47, C - 1), 47, 3, 1.0, 4)
+        ts(A("lqw", 16, 48), ind(A("pq"), A("bw", 6, 8)), 32.0, op.mult, 191.0, op.add)
+        lw, qw = A("lqw", 10, 16), A("lqw", 30, 48)
+        for p in range(4):
+            mov(A("sl", 128 + p, 512, 4), ind(A("e", C * p, C * p + C), lw))
+        quant(A("qs"), A("sf", 512, 640), A("sl"))
         dst = T.cores[(rank + STEP[t]) % n_ranks]
         rid, pid = topo.addr(dst)[:2]
         eng = topo.engines(core, dst)
         half = len(eng) // 2
         m0, m1 = sum(1 << k for k in eng[:half]), sum(1 << k for k in eng[half:])
-        scales = A("s0", 4 * M + 128 - C, 4 * M + 128)
+        scales = A("sf", 640 - C, 640)
 
         def send_codes(t=t, rid=rid, pid=pid, m0=m0, m1=m1, scales=scales):
             to = [DstId(rid=rid, pnc=pid)]
@@ -797,21 +625,22 @@ def rank_program(g, core, T, topo):
         mov(A("tn", C, 2 * C), ind(A("ncs"), tw(t)))
         if last:
             mov(A("srow"), ind(A("tn", 0, C), lw), -1.0, 143.0)
-            mov(A("otr"), ind(A("tn"), qw), -1.0, 143.0)
+            mov(A("otr"), ind(A("tn", C, 2 * C), qw), -1.0, 143.0)
             pairs = [(A("srow"), A("lrow"), m0 | m1)]
         else:
-            for (a, b, w) in ((0, C, 2 * C),) if OPT["tm"] else ((0, NL, C), (NL, C, 2 * C)):
-                src = ind(A("tn", 0, w), A("lqw", 10 + a // 16, 10 + b // 16))
-                if OPT["nm"] and b == C:
-                    mov(A("nr", a, b), src)
-                    scan(A("nm", a, b), A("nr", a, b), A("cm1", a, b), op.add, op.mult)
-                else:
-                    tt(A("nm", a, b), src, A("cm1", a, b), op.mult)
-                scan(A("nh", a, b), A("keep", a, b), A("nm", a, b), op.mult, op.add)
-                ts(tw(t + 1, a // 16 - 6, b // 16 - 6), A("nh", a + 15, b, 16), -1.0, op.mult, 143.0, op.add)
-                tt(A("hf", a // 16, b // 16), A("nh", a + 15, b, 16), A("ths", a // 16, b // 16), op.is_gt)
-                cp(A("hw", a // 16, b // 16), A("hf", a // 16, b // 16))
-            pairs = [(tw(t + 1, -6, 0), tw(t + 1, 18, 24), m0), (A("hw", 0, 6), tw(t + 1, 24, 30), m1)]
+            mov(A("nq"), ind(A("tn", 0, C), lw))
+            scan(A("nm"), A("nq"), A("cm1", 0, NL), op.add, op.mult)
+            scan(A("nh"), A("keep", 0, NL), A("nm"), op.mult, op.add)
+            ts(tw(t + 1, -22, -16), A("nh", 15, NL, 16), -1.0, op.mult, 143.0, op.add)
+            tt(A("hf", 0, 6), A("nh", 15, NL, 16), A("ths", 0, 6), op.is_gt)
+            cp(A("hw", 0, 6), A("hf", 0, 6))
+            ts(A("po"), A("mq"), 0.0, op.is_equal)
+            scan(A("nr"), A("tn", C, 2 * C), A("mq"), op.add, op.mult)
+            scan(A("mo"), A("po"), A("nr"), op.mult, op.add)
+            ts(tw(t + 1, -14, 18), ind(A("mo"), A("bw", 6, 8)), -1.0 / 16, op.mult, 143.0, op.add)
+            tt(A("hf", 6, 38), ind(A("mo"), A("bw", 6, 8)), A("ths", 6, 38), op.is_gt)
+            cp(A("hw", 6, 24), A("hf", 20, 38))
+            pairs = [(tw(t + 1, -22, -16), tw(t + 1, 18, 24), m0), (A("hw", 0, 6), tw(t + 1, 24, 30), m1)]
 
         def send_list(t=t, rid=rid, pid=pid, pairs=pairs):
             return g.remote_dma_fused([
@@ -821,14 +650,15 @@ def rank_program(g, core, T, topo):
         j = add({"g": (send_list, OPT["issue"])}, [a for (a, b, m) in pairs], [], kind="r", sem="ll", cnt=2 * half,
                 lat=OPT["rem"] + (OPT["rem0"] / 2 if t == 0 else 0.0))
         add({"x": (None, 0.0)}, [], [b for (a, b, m) in pairs], kind="x", sem="al%d" % t, cnt=2 * half, after=[j])
-        cuts = ((0, 160, 256, 0), (160, NS, C, 2)) if OPT["sx"] else ((0, NS, C, 0),)
         side = ("qv", "sv") if last else ("qu2", "su2")
-        for (a, b, w, k) in cuts:
+        for (a, b, k) in ((0, 160, 0), (160, NS, 2)):
             for p in range(4):
-                mov(A("xi", 4 * a + p, 4 * b, 4), ind(A("e", C * p, C * (p + 1) + w), A("lqw", 16 + a // 16, 16 + b // 16)))
+                mov(A("xi", 4 * a + p, 4 * b, 4), ind(A("e", C * p, C * p + C), A("lqw", 30 + a // 16, 30 + b // 16)))
             quant(A("qx", a, b), A("sx", a, b), A("xi", 4 * a, 4 * b))
             mm(bank(k, 0, b - a), A(side[0]), A(side[1]), A("qx", a, b), A("sx", a, b))
             mov(A("yr" if last else "sr", a, b), bank(k, 0, b - a))
+            if not last:
+                again(a, b, 4 + k // 2)
         for p in range(4):
             mm(bank(4 + p, 0, 128), A("qe", 128 * p, 128 * p + 128), A("se", 128 * p, 128 * p + 128),
                A("lq", 224 * t, 224 * t + 128), A("ls", 512 * t + NS, 512 * t + NS + 128))
@@ -848,19 +678,12 @@ def rank_program(g, core, T, topo):
             dma("y", T.ot[:, 0:NS], T.otr[0:128:16, :], [A("otr")], [])
             dma("y", T.ot[:, NS:C], T.lrow[0:128:16, :], [A("lrow")], [])
         else:
-            mov(A("st", 0, 160), ind(A("sr", 0, NS), tw(t + 1, 0, 10)))
-            mov(A("st", 160, NS), ind(A("sr", 0, NS), tw(t + 1, 10, 18)))
-            for (a, b, w, k) in cuts:
-                tt(A("d", a, b), A("st", a, b), bank(k, 0, b - a), op.subtract)
-            if OPT["d1"]:
-                mm(bank(3, 0, 128), A("qu2"), A("su2"), A("qb"), A("sq"))
-                mov(A("st", NS, C), bank(3, 0, NL))
-                tt(A("d", NS, C), ind(A("sr"), tw(t + 1, 18, 24)), A("st", NS, C), op.subtract)
-            else:
-                mov(A("st", NS, C), ind(A("sr"), tw(t + 1, 18, 24)))
-                tt(A("d", NS, C), A("st", NS, C), bank(1, 0, NL), op.subtract)
-            for (a, b) in ((0, 160), (160, NS)) if OPT["su"] else ((0, NS),):
+            mm(bank(3, 0, 128), A("qu2"), A("su2"), A("qb"), A("sq"))
+            mov(A("st", NS, C), bank(3, 0, NL))
+            for (a, b) in ((0, 160), (160, NS)):
+                tt(A("d", a, b), ind(A("sr", 0, NS), tw(t + 1, a // 16, b // 16)), A("st", a, b), op.subtract)
                 tt(A("un", a, b), ind(A("tie", 0, 2), A("hw", 6 + a // 16, 6 + b // 16)), A("d", a, b), op.is_lt)
+            tt(A("d", NS, C), ind(A("sr"), tw(t + 1, 18, 24)), A("st", NS, C), op.subtract)
             tt(A("un", NS, C), ind(A("tie", 0, 2), tw(t + 1, 24, 30)), A("d", NS, C), op.is_lt)
 
     n = len(ops)

import math
import numpy as np
from concourse.bass import DstId, RemoteDMATransfer
from concourse.mybir import dt, AluOpType, ActivationFunctionType, AxisListType

C, M, NL, NS, R = 384, 192, 96, 288, 3
MS = NS // 2
STEP = [1, 2, 4]
PL = 208
DUP = 8
OFF = 16
TT = 320
BIG = 2.0 ** 80
EPS = 2.0 ** -110
LEV = 3072.0
OPT = {"cy": 0.83, "ga": 1.15, "dma": 1100.0, "rem": 1500.0, "rem0": 500.0, "issue": 800.0,
       "fine": [(1.0, 1.3, 210.0, 0.0, 200.0, 3.0, 20.0), (1.0, 1.0, 190.0, 100.0, -200.0, 3.0, 20.0), (1.35, 1.6, 270.0, 200.0, 300.0, 5.0, 25.0)],
       "seed": 4, "stages": [(1, 50000, 20.0), (3, 10000, 12.0), (3, 10000, 6.0)], "wide": 70, "some": 0.15, "shake": 500.0,
       "chain": 0.3, "pull": 800.0, "flips": 2, "free": 0.1, "since": 260.0, "lean": 1.0, "price": 0.07,
       "both": [7, 8, 11]}


def sb(n, d):
    return ("sbuf", [128, n], d)


F, B, I, U16, X4, U8 = "float32", "bfloat16", "int32", "uint16", "float8_e4m3fn_x4", "uint8"
SCRATCH = {
    "ps": ("psum", [128, 4096], F),
    "xi": sb(4 * C + 128, B), "ut": sb(512, B), "vt": sb(512, B), "twi": sb(24, I),
    "qx": sb(C, X4), "sx": sb(C, U8), "qb": sb(128, X4), "sq": sb(128, U8),
    "qu": sb(128, X4), "su": sb(128, U8), "qu2": sb(128, X4), "su2": sb(128, U8),
    "qv": sb(128, X4), "sv": sb(128, U8), "wq": sb(512, X4), "wp": sb(512, U8),
    "ones": sb(512, B), "et": sb(520, B), "qe": sb(512, X4), "se": sb(512, U8),
    "bo1": sb(512, B), "bo2": sb(512, B), "qo": sb(128, X4), "so": sb(128, U8), "zero": sb(512, B),
    "uli": sb(8, I), "ul": sb(8, U16), "pi": sb(1, I), "ri": sb(3, I), "rf": sb(3, F), "kb": sb(13, F),
    "i4": sb(M, B), "cm4": sb(M, B), "cm4n": sb(M, B), "keep4": sb(M, B), "orow": sb(M, B), "oh": sb(M, B),
    "iob": sb(C, B), "pos": sb(C, B), "i16": sb(C, B), "cm": sb(C, B), "cm1": sb(C, B), "keep": sb(C, B),
    "tie": sb(16, F), "iw": sb(24, F), "ths": sb(38, F), "hf": sb(38, F), "hw": sb(24, U16),
    "sr": sb(C, F), "st": sb(C, F), "d": sb(C, F), "un": sb(C, B), "cum": sb(C + 16, B),
    "cap2": sb(C, B), "uw": sb(24, F), "uc": sb(24, F), "cwu": sb(24, U16), "ud": sb(24, F), "cim": sb(C, B), "cih": sb(C, B),
    "twf": sb(64 * R, U16), "srow": sb(NL, F), "lrow": sb(NL, F),
    "junk": sb(5 * C, B), "acc": sb(12, F), "bw": sb(8, U16),
    "yo": sb(C + 8, B), "yg": sb(C + 8, B), "yq": sb(C + 8, B), "mo": sb(C, B), "mg": sb(C, B), "mq": sb(C, B),
    "po": sb(C, B), "pg": sb(C, B), "pq": sb(C, B),
    "cto": sb(M, B), "xa": sb(4 * (M + DUP), B), "nr": sb(C, B),
    "ow": sb(32, U16), "ow4": sb(48, U16), "lqw": sb(48, U16), "cap": sb(C, B), "cw": sb(24, U16),
    "dm": sb(M, F), "dh": sb(M, F), "dr": sb(M, F), "sg": sb(11 * M, B),
    "cmb": sb(M, B), "mr": sb(M, B), "r2": sb(M, B), "ra": sb(12, F), "thf": sb(12, F), "thw": sb(14, U16), "tb": sb(64, B), "thr": sb(M, B),
    "fl": sb(2048, B), "qf": sb(512, X4), "sf": sb(640, U8),
    "ct": sb(C, B), "ctm": sb(M, B), "cth": sb(M, B), "ctw": sb(48, U16),
    "xo": sb(4 * (M + DUP), B), "z": sb(4 * (M + DUP), B), "qz": sb(M + DUP, X4), "sz": sb(M + DUP, U8), "hx": sb(4 * PL, B),
    "lv": sb(M + 1, B), "gone": sb(C, B), "gn": sb(C, B), "ncs": sb(C, B), "e": sb(4 * C, B),
    "sl": sb(512, B), "qs": sb(128, X4), "lq": sb(R * 224, X4), "ls": sb(R * 512, U8),
    "tn": sb(2 * C, B), "nq": sb(NL, B), "nm": sb(NL, B), "nh": sb(NL, B),
    "yr": sb(C, F), "otr": sb(NS, F),
}
POOL = {"v": 56, "s": 36, "t": 10, "g": 10}
NDMA = 24
SEMAPHORES = (["%s%d" % (q, i) for q in POOL for i in range(POOL[q])] + ["m%d" % i for i in range(NDMA)]
              + ["ac%d" % t for t in range(R)] + ["al%d" % t for t in range(R)] + ["lc", "ll"])
QS = "vstgyx"


def graph(ops, par):
    f, ga, wake, local, far, fix, more = par
    cost = [{q: (f * (v[1] + (ga - OPT["ga"]) * o["gath"]) + fix + (more if q == "s" else 0.0) if o["kind"] == "c" else v[1])
             for q, v in o["alts"].items()} for o in ops]
    lat = [o["lat"] + {"d": local, "r": far}.get(o["kind"], 0.0) for o in ops]
    above, pre, suc = [], [], [[] for _ in ops]
    for i, o in enumerate(ops):
        known, mine = 0, []
        for j in sorted(o["deps"] | o["soft"], reverse=True):
            if not known >> j & 1 or ops[j]["lat"] > 100.0:
                mine.append((j, lat[j] if o["kind"] == "x" else 0.0 if j in o["soft"] else lat[j] + wake))
                suc[j].append((i, mine[-1][1]))
            known |= above[j] | 1 << j
        above.append(known)
        pre.append(mine)
    return cost, lat, pre, suc, above


def place(order, on, edges, base, low, choose, inside, cost):
    S, E, end, lean = {q: [-1.0] for q in QS}, {q: [low[q]] for q in QS}, {}, OPT["lean"]
    for i in order:
        ready = base[i]
        for (j, d) in edges[i]:
            if inside[j] and end[j] + d > ready:
                ready = end[j] + d
        best = None
        for q in (cost[i] if i in choose else on[i]):
            c, s, e = cost[i][q], S[q], E[q]
            k = m = len(e)
            at = ready
            if e[-1] > ready:
                while k > 1 and e[k - 1] > ready:
                    k -= 1
                if e[0] > at:
                    at = e[0]
                while k < m and at + c > s[k]:
                    at = e[k]
                    k += 1
            if best is None or at + c < best[0] + (lean * (best[0] - best[2]) if best[1] == "v" else 0.0):
                best = (at + c, q, at, k)
        end[i], on[i] = best[0], best[1]
        S[best[1]].insert(best[3], best[2])
        E[best[1]].insert(best[3], best[0])
    return end


def search(ops, sets, seq, on, moves, heat, rng):
    G = [graph(ops, par) for par in sets]
    n, ns, none = len(ops), len(sets), set()
    above = G[0][4]
    fin, rest = [[0.0] * n for _ in sets], [[0.0] * n for _ in sets]

    def survey(first, last):
        for s in range(ns):
            cost, lat, pre, suc = G[s][:4]
            for (f, e, low, near, part) in ((fin[s], pre, None, seq[:first][::-1], seq[first:]),
                                            (rest[s], suc, lat, seq[last + 1:], seq[:last + 1][::-1])):
                free = {}
                for i in near:
                    if on[i] not in free:
                        free[on[i]] = f[i]
                for i in part:
                    q = on[i]
                    at = free.get(q, 0.0)
                    if low and low[i] > at:
                        at = low[i]
                    for (j, d) in e[i]:
                        if f[j] + d > at:
                            at = f[j] + d
                    free[q] = f[i] = at + cost[i][q]
        return [max(r) for r in rest]

    span = survey(0, n - 1)
    norm = [span[0] / x / ns for x in span]
    best, keep = span[0], (list(seq), list(on), span)
    inside = [False] * n
    for it, u in enumerate(rng.random((moves, 12)).tolist()):
        w = int(OPT["wide"] * (0.3 + u[0]))
        first = max(0, int(u[1] * n) - w // 2)
        last = min(n - 1, first + w)
        W = seq[first:last + 1]
        for i in W:
            inside[i] = True
        before, after, edge, old = {}, {}, [], 0.0
        for i in seq[max(0, first - 150):first][::-1]:
            before.setdefault(on[i], i)
        for i in seq[last + 1:last + 150]:
            after.setdefault(on[i], i)
        for s in range(ns):
            cost, lat, pre, suc = G[s][:4]
            f, r, head, tail, top = fin[s], rest[s], {}, {}, 0.0
            for i in W:
                a = 0.0
                for (j, d) in pre[i]:
                    if not inside[j] and f[j] + d > a:
                        a = f[j] + d
                head[i], a = a, lat[i]
                for (j, d) in suc[i]:
                    if not inside[j] and r[j] + d > a:
                        a = r[j] + d
                tail[i], a = a, f[i] - cost[i][on[i]] + r[i]
                if a > top:
                    top = a
            lo = {q: (f[before[q]] if q in before else 0.0) for q in QS}
            hi = {q: (r[after[q]] if q in after else 0.0) for q in QS}
            edge.append((head, tail, lo, hi))
            old += max([top] + [lo[q] + hi[q] for q in QS]) * norm[s]
        s = int(u[2] * ns)
        cost, lat, pre, suc = G[s][:4]
        f, (head, tail, lo, hi) = fin[s], edge[s]
        noise = (rng.standard_normal(len(W)) * (rng.random(len(W)) < u[4] * OPT["some"]) * (2 * u[3] * OPT["shake"])).tolist()
        key = {i: f[i] - cost[i][on[i]] + x for i, x in zip(W, noise)}
        if u[8] < OPT["chain"]:
            x, far = W[int(u[9] * len(W))], -OPT["pull"] * math.log(u[10] + 1e-9)
            for i in W:
                if u[11] < 0.5 and (i == x or above[x] >> i & 1):
                    key[i] -= far
                if u[11] >= 0.5 and (i == x or above[i] >> x & 1):
                    key[i] += far
        for i in W:
            for (j, d) in pre[i]:
                if inside[j] and key[j] >= key[i]:
                    key[i] = key[j] + 1e-3
        on2, choose, open_ = list(on), none, [i for i in W if len(cost[i]) > 1]
        if open_:
            for x in rng.random((int(u[5] * (OPT["flips"] + 1)), 2)).tolist():
                i = open_[int(x[0] * len(open_))]
                other = [q for q in cost[i] if q != on[i]]
                on2[i] = other[int(x[1] * len(other))]
            if u[6] < OPT["free"]:
                choose = set(i for i, x in zip(open_, rng.random(len(open_)).tolist()) if x < 0.3)
        end = place(sorted(W, key=key.get), on2, pre, head, lo, choose, inside, cost)
        back = place(sorted(W, key=lambda i: -end[i] - 1e-6 * i), on2, suc, tail, hi, none, inside, cost)
        end = place(sorted(W, key=lambda i: 1e-6 * i - back[i]), on2, pre, head, lo, none, inside, cost)
        mid = sorted(W, key=lambda i: (end[i] - cost[i][on2[i]], end[i], i))
        new = 0.0
        for s in range(ns):
            cost, pre = G[s][0], G[s][2]
            head, tail, lo, hi = edge[s]
            free, e, top = dict(lo), {}, 0.0
            for i in mid:
                q = on2[i]
                at = free[q] if free[q] > head[i] else head[i]
                for (j, d) in pre[i]:
                    if inside[j] and e[j] + d > at:
                        at = e[j] + d
                free[q] = e[i] = at = at + cost[i][q]
                if at + tail[i] > top:
                    top = at + tail[i]
            new += max([top] + [free[q] + hi[q] for q in QS]) * norm[s]
        for i in W:
            inside[i] = False
        for i in open_:
            if on2[i] != on[i]:
                new += OPT["price"] * cost[i]["v"] * ((on2[i] == "v") - (on[i] == "v")) if "v" in cost[i] else 0.0
        if new <= old - heat * (1.0 - it / moves) * math.log(u[7] + 1e-12) and (mid != W or on2 != on):
            seq[first:last + 1] = mid
            on[:] = on2
            span = survey(first, last)
            start = [fin[0][i] - G[0][0][i][on[i]] for i in range(n)]
            seq.sort(key=lambda i: start[i])
            now = sum(a * b for a, b in zip(span, norm))
            if now < best:
                best, keep = now, (list(seq), list(on), span)
    return keep


def plan(ops):
    n, sets = len(ops), OPT["fine"]
    rng = np.random.default_rng(OPT["seed"])
    cost, lat, pre, suc = graph(ops, sets[0])[:4]
    tail = list(lat)
    for i in range(n - 1, -1, -1):
        tail[i] = min(cost[i].values()) + max([lat[i]] + [d + tail[j] for (j, d) in suc[i]])
    on = [list(x)[0] for x in cost]
    end = place(sorted(range(n), key=lambda i: 1e-6 * i - tail[i]), on, pre, [0.0] * n, {q: 0.0 for q in QS}, set(range(n)), [True] * n, cost)
    seq = sorted(range(n), key=lambda i: (end[i] - cost[i][on[i]], end[i], i))
    for (k, moves, heat) in OPT["stages"]:
        seq, on, span = search(ops, sets[:k], seq, on, moves, heat, rng)
    OPT["span"] = [int(x) for x in span]
    res = [None] * n
    for k, i in enumerate(seq):
        res[i] = (on[i], k)
    return res


def rank_program(g, core, T, topo):
    rank = T.rank_of(core)
    if rank is None:
        return
    n_ranks = len(T.cores)
    op = AluOpType
    fn = ActivationFunctionType
    queue = {"v": g.vector, "s": g.scalar, "t": g.tensor, "g": g, "y": g.sync}
    ops, hist = [], {}
    cy, ga = OPT["cy"], OPT["ga"]

    def A(name, a=0, b=None, st=1):
        return (name, a, SCRATCH[name][1][1] if b is None else b, st, None, None)

    def ind(w, off):
        return w[:4] + (off, w[5])

    def cast(w, d):
        return w[:5] + (d,)

    def real(x):
        if not isinstance(x, tuple):
            return x
        v = T[x[0]][:, x[1]:x[2]:x[3]] if x[3] != 1 else T[x[0]][:, x[1]:x[2]]
        if x[5] is not None:
            v = v.bitcast(x[5])
        if x[4] is not None:
            v = v.indirect(real(x[4]))
        return v

    def bits(x):
        if x[0] == "ps":
            return 1 << (x[1] // 512)
        if x[3] == 1:
            return ((1 << (x[2] - x[1])) - 1) << x[1]
        return sum(1 << i for i in range(x[1], x[2], x[3]))

    def size(x):
        return len(range(x[1], x[2], x[3]))

    def add(alts, rd, wr, kind="c", sem=None, cnt=1, chain=False, lat=0.0, after=()):
        me, deps, soft, use = len(ops), set(), set(after), []
        for x in rd:
            if isinstance(x, tuple):
                use.append((x[0], bits(x), x[0] == "ps"))
                if x[4] is not None:
                    use.append((x[4][0], bits(x[4]), False))
        for x in wr:
            use.append((x[0], bits(x), True))
        for name, m, w in use:
            for (j, m2, w2) in hist.get(name, []):
                if (w or w2) and m & m2:
                    (soft if chain and name == "ps" and "t" in ops[j]["alts"] else deps).add(j)
        for name, m, w in use:
            if w:
                hist[name] = [h for h in hist.get(name, []) if h[1] & ~m]
            hist.setdefault(name, []).append((me, m, w))
        ops.append({"alts": alts, "deps": deps, "soft": soft, "kind": kind, "sem": sem, "cnt": cnt, "lat": lat,
                    "key": str([x[:3] for x in wr + rd[:1] if isinstance(x, tuple)]),
                    "gath": size(wr[0]) if any(isinstance(x, tuple) and x[4] is not None for x in rd) else 0})
        return me

    def vcost(out, a, per, *more):
        if a[4] is not None:
            return 50 + ga * size(out)
        if per == 1 and all(SCRATCH[x[0]][2] in (B, U16) for x in (out, a) + more):
            per = 0.5
        return max(64, size(out) * per) * cy

    def tsv(out, a, s1, o0, s2=None, o1=None):
        if o1 is None:
            return (lambda: g.vector.tensor_scalar(real(out), real(a), real(s1), None, o0), vcost(out, a, 1))
        return (lambda: g.vector.tensor_scalar(real(out), real(a), real(s1), real(s2), o0, o1), vcost(out, a, 1))

    def acs(out, a, f, bias=0.0, scale=1.0, acc=None):
        return (lambda: g.scalar.activation(real(out), real(a), f, bias=real(bias), scale=scale, accum_out=real(acc)),
                (65 + ga * size(out) if a[4] is not None else max(64, size(out)) * cy) + (20 if acc else 0))

    def ts(out, a, s1, o0, s2=None, o1=None):
        add({"v": tsv(out, a, s1, o0, s2, o1)}, [a, s1, s2], [out])

    def tt(out, a, b, o):
        add({"v": (lambda: g.vector.tensor_tensor(real(out), real(a), real(b), o), vcost(out, a, 1 if b[0] == "ps" else 2, b))},
            [a, b], [out])

    def cp(out, a):
        add({"v": (lambda: g.vector.tensor_copy(real(out), real(a)), vcost(out, a, 1))}, [a], [out])

    def mov(out, a, scale=1.0, bias=0.0, pool=False):
        if scale == 1.0 and bias == 0.0:
            v = (lambda: g.vector.tensor_copy(real(out), real(a)), vcost(out, a, 1))
        elif bias == 0.0:
            v = tsv(out, a, scale, op.mult)
        else:
            v = tsv(out, a, scale, op.mult, bias, op.add)
        alts = {"v": v, "s": acs(out, a, fn.Copy if bias == 0.0 else fn.Identity, bias, scale)}
        if pool:
            alts["g"] = (lambda: g.affine_select(real(out), real(a), [[0, size(out)]], op.is_ge, 0.0, 0, 0), 210 + 2 * cy * size(out))
        add(alts, [a, bias], [out])

    def scan(out, a, b, o0, o1, init=0.0):
        add({"v": (lambda: g.vector.tensor_tensor_scan(real(out), real(a), real(b), real(init), o0, o1), vcost(out, a, 1, b))},
            [a, b, init], [out])

    def ms(out, val):
        add({"v": (lambda: g.vector.memset(real(out), val), vcost(out, out, 1))}, [], [out])

    def quant(q, s, a):
        add({"v": (lambda: g.vector.quantize_mx(real(q), real(s), real(a)), 12 + 0.22 * size(a))}, [a], [q, s])

    def act(out, a, f, bias=0.0, scale=1.0, acc=None):
        add({"s": acs(out, a, f, bias, scale, acc)}, [a, bias], [out] + ([acc] if acc else []))

    def mm(out, lq, lsc, rq, rsc, start=True, stop=True):
        add({"t": (lambda: g.tensor.matmul_mx(real(out), real(lq), real(lsc), real(rq), real(rsc), start, stop),
                   25 + 0.8 * (size(out) + 16))}, [lq, lsc, rq, rsc], [out], chain=not start, lat=60.0)

    def iota(out, pat, base=0, cmul=0):
        if SCRATCH[out[0]][2] == I:
            call = lambda: g.iota(real(out), pat, base, cmul)
        else:
            call = lambda: g.iota(real(out), pat, base, cmul, allow_small_or_imprecise_dtypes=True)
        add({"g": (call, 170 + 2 * cy * size(out))}, [], [out])

    def fill(out, val=0, early=False):
        alts = {"g": (lambda: g.iota(real(out), [[0, size(out)]], val, 0, allow_small_or_imprecise_dtypes=True), 170 + 2 * cy * size(out))}
        if early:
            alts["v"] = (lambda: g.vector.memset(real(out), float(val)), vcost(out, out, 1))
        add(alts, [], [out])

    def sel(out, a, pat, cmp, base, cmul):
        add({"g": (lambda: g.affine_select(real(out), real(a), pat, cmp, 0.0, base, cmul), 210 + 2 * cy * size(out))}, [a], [out])

    nd = [0]

    def dma(q, out, a, rd, wr, kb=0, after=()):
        nd[0] += 1
        return add({q: (lambda: queue[q].dma_start(out, a), 100.0)}, rd, wr, kind="d",
                   sem="m%d" % (nd[0] - 1), cnt=16, lat=OPT["dma"] + 3.5 * kb, after=after)

    def bank(b, a, n):
        return A("ps", 512 * b + a, 512 * b + a + n)

    def col(name, c):
        return A(name, c, c + 1)

    def tw(t, a=0, b=24):
        return A("twf", 64 * t + 22 + a, 64 * t + 22 + b)

    def steps(y, m, p, a, b, up=True):
        now, before = A(y, a + 1, b + 1), A(y, a, b)
        scan(A(m, a, b), now if up else before, before if up else now, op.max, op.subtract)
        scan(A(p, a, b), A(m, a, b), A("pos", a, b), op.add, op.min, (a - 191) / 32.0)

    def cum(a, b):
        return A("cum", 16 + a, 16 + b)

    def where(k, cnt, a, thr, scale, j):
        act(A("junk", C * j, C * j + size(cnt)), cnt, fn.Sign, col("kb", thr), scale, col("acc", k))
        ts(col("bw", k), col("acc", k), 0.5, op.mult, size(cnt) / 2 + a, op.add)

    def plane(c, lo, hi):
        at = (128, 0, TT)[(c - 1) // 4]
        return A("fl", 4 * (at + lo) + (c - 1) % 4, 4 * (at + hi), 4)

    def compare(c, by_s):
        w, piv = 16 * c, col("dh", 16 * c + 15)
        sg, out, acc = A("sg", M * (c - 1), M * (c - 1) + w), plane(c, 0, w), col("ra", c)
        if c in by_s:
            add({"s": acs(sg, A("dr", 0, w), fn.Sign, piv, -1.0), "v": tsv(sg, A("dr", 0, w), piv, op.is_gt, -1.0, op.mult)},
                [A("dr", 0, w), piv], [sg])
            act(out, sg, fn.Relu, 0.0, -1.0, acc)
        else:
            ts(out, A("dr", 0, w), piv, op.is_gt)
            add({"v": (lambda: g.vector.tensor_reduce(real(acc), real(out), AxisListType.X, op.add), max(64, w) * cy),
                 "s": acs(sg, out, fn.Copy, 0.0, 1.0, acc)}, [out], [sg, acc])

    def again(a, b, k):
        mm(bank(k, 0, b - a), A("qu2"), A("su2"), A("qx", a, b), A("sx", a, b))
        mov(A("st", a, b), bank(k, 0, b - a))

    dma("s", real(A("ut")), T.u[:], [], [A("ut")], 200)
    j = dma("y", real(A("xi", 0, 4 * M)), T.x[:, 0:4 * M], [], [A("xi", 0, 4 * M)], 332)
    j = dma("y", real(A("xi", 4 * M, 4 * C)), T.x[:, 4 * M:4 * C], [], [A("xi", 4 * M, 4 * C)], 520, [j])
    dma("y", real(A("twi")), T.tw[:], [], [A("twi")], 520, [j])
    dma("y", real(cast(A("wq"), dt.uint8)), T.wc[:], [col("xi", 4 * M)], [A("wq")], 256)
    dma("y", real(A("wp")), T.ws[:], [col("xi", 4 * M)], [A("wp")], 64)
    dma("y", real(A("vt")), T.v[:], [col("wq", 0)], [A("vt")], 128)

    iota(A("uli"), [[16, 8]])
    iota(A("pi"), [[0, 1]], 0, 1)
    iota(A("iob"), [[1, C]], -191)
    iota(A("i16"), [[0, 24], [1, 16]])
    iota(A("iw"), [[16, 24]])
    mov(A("pos"), A("iob"), 1.0 / 32)
    fill(A("zero"), early=True)
    fill(A("fl", 4 * 80, 4 * M), early=True)
    fill(A("fl", 4 * (TT + MS), 4 * (TT + M)), early=True)
    fill(A("xi", 4 * C, 4 * C + 128))
    fill(A("sl", 0, 128))
    ms(A("ones"), 1.0)
    sel(A("bo1"), A("ones"), [[-16, 8], [0, 64]], op.is_ge, 0, 1)
    sel(A("bo2"), A("bo1"), [[16, 8], [0, 64]], op.is_ge, 15, -1)
    fill(A("et", 0, 4))
    fill(A("et", 516, 520))
    sel(A("et", 4, 516), A("ones"), [[-1, 512]], op.is_equal, 0, 4)
    fill(col("lv", 0))
    fill(cum(-1, 0))
    for p in range(4):
        fill(A("hx", PL * p, PL * p + OFF - DUP))
    ms(col("tie", 0), EPS)
    ms(col("tie", 1), -EPS)
    for name in ("yo", "yg", "yq"):
        fill(col(name, 0), int(LEV))
    cp(A("ul"), A("uli"))
    ts(col("ri", 0), A("pi"), 15, op.bitwise_and)
    ts(col("ri", 1), A("pi"), 15, op.bitwise_and, 2, op.logical_shift_right)
    ts(col("ri", 2), A("pi"), 3, op.bitwise_and)
    cp(A("rf"), A("ri"))
    rf = col("rf", 0)
    for k, c, a, b in ((0, 0, 16.0, 15.5), (1, 0, 2.0, 32.0), (2, 0, 16.0, -352.5), (3, 0, 16.0, -96.5), (4, 0, -1.0, LEV + 7.5),
                       (5, 0, 16.0, 15.5 - 160), (6, 0, 1.0, LEV - 7.5), (7, 0, 1.0, MS + 0.5), (8, 0, 1.0, MS + 16.5), (9, 0, 1.0, MS + 32.5),
                       (10, 2, 1.0, 4.0 * 191), (11, 2, 1.0, 4.0 * (191 - NS)), (12, 2, 1.0, 4.0 * (DUP - 1))):
        mov(col("kb", k), col("rf", c), a, b)
    ts(A("cm"), A("i16"), rf, op.is_equal, BIG, op.mult)
    ms(A("cm", 0, C, 16), BIG)
    ts(A("cmb"), A("i16", 0, M), rf, op.not_equal, BIG, op.mult)
    iota(A("tb"), [[1, 64]])
    fill(A("mr"), 256, early=True)
    fill(col("ra", 0))
    ts(A("keep"), A("cm"), 0.0, op.is_equal)
    ts(A("cm1"), A("i16"), rf, op.is_equal)
    iota(A("i4"), [[0, M // 4], [1, 4]])
    ts(A("cm4"), A("i4"), col("rf", 1), op.is_equal, BIG, op.mult)
    ts(A("keep4"), A("i4"), col("rf", 1), op.not_equal)
    mov(A("cm4n"), A("cm4"), 2.0, -BIG)
    mov(A("iw"), A("iw"), 1.0, rf)
    mov(A("mr", 0, M, 16), A("iw", 0, 12), -1.0, col("kb", 1))
    mov(A("ths", 0, 6), A("iw", 0, 6), -1.0, -145.0)
    fill(A("ths", 6, 20))
    mov(A("ths", 20, 38), A("iw", 0, 18), -16.0, 16 * 143.0)
    for t in range(R):
        quant(A("lq", 224 * t + NL, 224 * t + 224), A("ls", 512 * t + C, 512 * t + 512), A("zero"))
    quant(A("qf", M, TT), A("sf", M, TT), A("zero"))
    quant(A("qo"), A("so"), A("bo2"))
    for k in range(4):
        quant(A("qe", 128 * k, 128 * k + 128), A("se", 128 * k, 128 * k + 128), A("et", 4 - k, 516 - k))
    quant(A("qv"), A("sv"), A("vt"))
    quant(A("qu"), A("su"), A("ut"))
    cp(tw(0), A("twi"))
    cp(cast(A("qu2"), dt.uint32), ind(cast(A("qu"), dt.uint32), A("ul")))
    cp(A("su2"), ind(A("su"), A("ul")))

    tt(A("hf", 0, 24), A("twi"), A("iw"), op.is_lt)
    cp(A("hw"), A("hf", 0, 24))
    for (a, b, k) in ((0, M, 0), (M, C, 1)):
        quant(A("qx", a, b), A("sx", a, b), A("xi", 4 * a, 4 * b))
        mm(bank(k, 0, M), A("qu2"), A("su2"), A("qx", a, b), A("sx", a, b))
        mov(A("sr", a, b), bank(k, 0, M))
        again(a, b, 2 + k)
    for (a, b) in ((0, M), (M, C)):
        tt(A("d", a, b), ind(A("sr"), tw(0, a // 16, b // 16)), A("st", a, b), op.subtract)
        tt(A("un", a, b), ind(A("tie", 0, 2), A("hw", a // 16, b // 16)), A("d", a, b), op.is_lt)

    for t in range(R):
        last = t == R - 1
        parts = [(0, C, 0, M)] if t == 0 else [(0, NS, 0, MS), (NS, C, MS, M)]
        for s, (a, b, ka, kb) in enumerate(parts):
            un, n = A("un", a, b), (kb - ka) // 16
            scan(cum(a, b), un, un, op.add, op.max, float(ka))
            ow = A("ow", 16 * s, 16 * s + n)
            if s:
                for c in range(n):
                    act(A("junk", C + NL * c, C + NL * c + NL), cum(a, b), fn.Sign, col("kb", 7 + c), -1.0, col("acc", 8 + c))
                ts(ow, A("acc", 8, 8 + n), 0.5, op.mult, NL / 2, op.add)
            else:
                scan(A("yo", a + 1, b + 1), un, un, op.add, op.max, col("kb", 4))
                steps("yo", "mo", "po", a, b)
                where(0, cum(a, b - 1), a, 0, -1.0, 0)
                ts(A("ow", 0, 16), ind(A("po", a, b), col("bw", 0)), 32.0, op.mult, 191.0, op.add)
            mov(A("orow", ka, kb), ind(A("pos", a, b), ow))
            scan(A("oh", ka, kb), A("cm4n", ka, kb), A("orow", ka, kb), op.max, op.min, -8.0)
            ts(A("ow4", ka // 4, kb // 4), A("oh", ka + 3, kb, 4), 128.0, op.mult, col("kb", 10 + s), op.add)
            mov(A("dr", ka, kb), ind(A("d", a, b), ow))
            tt(A("dm", ka, kb), ind(A("d", a, b), ow), A("cmb", ka, kb), op.max)
            scan(A("dh", ka, kb), A("cm", ka, kb), A("dm", ka, kb), op.max, op.min)
            mov(A("ct", a, b), ind(cum(0, b), tw(t, a // 16, b // 16)))
            mov(A("cto", ka, kb), ind(A("ct", a, b), ow))
            w = (kb - ka) // (1 if s else 2)
            for lo in range(ka, kb, w):
                src, at = ind(A("xi", 4 * a, 4 * b), A("ow4", lo // 4, (lo + w) // 4)), 4 * (DUP + lo)
                mov(A("xo", at, at + 4 * w), src, 0.5)
                if s:
                    mov(A("xa", at, at + 4 * w), src, 0.5)
                else:
                    mov(A("xa", at, at + 4 * w), A("xo", at, at + 4 * w), pool=True)
            scan(A("cap", a, b), A("cm", a, b), cum(a, b), op.max, op.min)
            scan(A("cap2", a, b), A("cm", a, b), cum(a - 1, b - 1), op.max, op.min)
        for name in ("xo", "xa"):
            mov(A(name, 0, 4 * DUP), ind(A("xi", 4 * a, 4 * b), A("ow4", (M - DUP) // 4, M // 4)), 0.5)
        scan(A("ctm"), A("cto"), A("cm4"), op.max, op.min)
        scan(A("cth"), A("keep4"), A("ctm"), op.mult, op.add)
        ts(A("ctw"), A("cth", 3, M, 4), 4.0, op.mult, col("kb", 12), op.add)
        ts(A("cw"), A("cap", 15, C, 16), OFF - 1.0, op.add)
        scan(A("cim"), A("ct"), A("cm1"), op.add, op.mult)
        scan(A("cih"), A("keep"), A("cim"), op.mult, op.add)
        tt(A("uw"), A("cap", 15, C, 16), A("cap2", 15, C, 16), op.subtract)
        tt(A("ud"), A("cap", 15, C, 16), A("cih", 15, C, 16), op.subtract)
        tt(A("uc"), A("uw"), A("ud"), op.mult)
        tt(A("uw"), A("uc"), A("cih", 15, C, 16), op.add)
        cp(A("cwu"), A("uw"))
        for c in range(1, 12):
            compare(c, OPT["both"])
        for s, (a, b, ka, kb) in enumerate(parts):
            lo, hi = ka // 16, kb // 16
            tt(plane(12, ka, kb), A("dh", ka, kb), A("dr", ka, kb), op.is_le)
            scan(A("r2", ka, kb), A("mr", ka, kb), plane(12, ka, kb), op.min, op.add, 256.0)
            if s:
                for c in range(lo, hi):
                    ts(col("thw", c + s), col("ra", c), col("r2", 16 * c + 15), op.add)
            else:
                tt(A("thf", lo, hi), A("ra", lo, hi), A("r2", ka + 15, kb, 16), op.add)
                cp(A("thw", lo, hi), A("thf", lo, hi))
            mov(A("thr", ka, kb), ind(A("tb"), A("thw", lo + s, hi + s)))
        for (lo, tiles) in ((0, ((128, M), (0, 128))), (TT, ((TT, M),))):
            quant(A("qf", lo, lo + M), A("sf", lo, lo + M), A("fl", 4 * lo, 4 * (lo + M)))
            for (at, wide) in tiles:
                mm(bank(2, 0, wide), A("qo"), A("so"), A("qf", at, at + wide), A("sf", at, at + wide), at == 128, at == TT)
        tt(A("lv", 1, M + 1), A("thr"), bank(2, 0, M), op.is_ge)
        for (at, lo, hi) in ((DUP, 0, NL), (DUP + NL, NL, M), (0, M - DUP, M)):
            tt(A("z", 4 * at, 4 * (at + hi - lo)), ind(A("xo"), A("ctw", lo // 4, hi // 4)), A("xa", 4 * (DUP - 1 + lo), 4 * (DUP - 1 + hi)), op.add)
        quant(A("qz"), A("sz"), A("z"))
        for p in range(4):
            mm(bank(4 + p, 0, M + DUP), A("wq", 128 * p, 128 * p + 128), A("wp", 128 * p, 128 * p + 128), A("qz"), A("sz"))
            mov(A("hx", PL * p + OFF - DUP, PL * p + PL), bank(4 + p, 0, M + DUP), 0.03125)
        for p in range(4):
            tt(A("e", C * p, C * p + C), ind(A("hx", PL * p, PL * p + PL), A("cw")), A("xi", p, 4 * C, 4), op.add)
        for lo in (0, M):
            mov(A("gone", lo, lo + M), ind(A("lv"), A("cwu", lo // 16, (lo + M) // 16)))
        scan(A("gn"), A("gone"), A("zero", 0, C), op.add, op.add)
        scan(A("yg", 1, C + 1), A("gone"), A("zero", 0, C), op.add, op.add, col("kb", 4))
        steps("yg", "mg", "pg", 0, C)
        where(4, A("gn", 0, C - 1), 0, 5, -1.0, 2)
        ts(A("lqw", 0, 16), ind(A("pg"), col("bw", 4)), 32.0, op.mult, 191.0, op.add)
        scan(A("ncs"), A("gone"), A("ones", 0, C), op.add, op.subtract, float(MS))
        scan(A("yq", 1, C + 1), A("gone"), A("ones", 0, C), op.add, op.subtract, col("kb", 6))
        steps("yq", "mq", "pq", 0, C, False)
        where(6, A("ncs", 0, 128), 0, 2, 1.0, 3)
        where(7, A("ncs", 47, C - 1), 47, 3, 1.0, 4)
        ts(A("lqw", 16, 48), ind(A("pq"), A("bw", 6, 8)), 32.0, op.mult, 191.0, op.add)
        lw, qw = A("lqw", 10, 16), A("lqw", 30, 48)
        for p in range(4):
            mov(A("sl", 128 + p, 512, 4), ind(A("e", C * p, C * p + C), lw))
        quant(A("qs"), A("sf", 512, 640), A("sl"))
        dst = T.cores[(rank + STEP[t]) % n_ranks]
        rid, pid = topo.addr(dst)[:2]
        eng = topo.engines(core, dst)
        half = len(eng) // 2
        m0, m1 = sum(1 << k for k in eng[:half]), sum(1 << k for k in eng[half:])
        scales = A("sf", 640 - C, 640)

        def send_codes(t=t, rid=rid, pid=pid, m0=m0, m1=m1, scales=scales):
            to = [DstId(rid=rid, pnc=pid)]
            return g.remote_dma_fused([
                RemoteDMATransfer(dst_ids=to, dma_engine_mask=m0, remote_sem=T.sem["ac%d" % t],
                                  src=real(cast(A("qs", 32, 128), dt.uint8)), dst=real(cast(A("lq", 224 * t, 224 * t + NL), dt.uint8))),
                RemoteDMATransfer(dst_ids=to, dma_engine_mask=m1, remote_sem=T.sem["ac%d" % t],
                                  src=real(scales), dst=real(A("ls", 512 * t, 512 * t + C)))], local_sem=T.sem.lc)

        j = add({"g": (send_codes, OPT["issue"])}, [A("qs", 32, 128), scales], [], kind="r", sem="lc", cnt=2 * half,
                lat=OPT["rem"] + (OPT["rem0"] if t == 0 else 0.0))
        add({"x": (None, 0.0)}, [], [A("lq", 224 * t, 224 * t + NL), A("ls", 512 * t, 512 * t + C)], kind="x",
            sem="ac%d" % t, cnt=2 * half, after=[j])
        mov(A("tn", 0, C), ind(A("gn"), tw(t)), -1.0, -float(MS))
        mov(A("tn", C, 2 * C), ind(A("ncs"), tw(t)))
        if last:
            mov(A("srow"), ind(A("tn", 0, C), lw), -1.0, 143.0)
            mov(A("otr"), ind(A("tn", C, 2 * C), qw), -1.0, 143.0)
            pairs = [(A("srow"), A("lrow"), m0 | m1)]
        else:
            mov(A("nq"), ind(A("tn", 0, C), lw))
            scan(A("nm"), A("nq"), A("cm1", 0, NL), op.add, op.mult)
            scan(A("nh"), A("keep", 0, NL), A("nm"), op.mult, op.add)
            ts(tw(t + 1, -22, -16), A("nh", 15, NL, 16), -1.0, op.mult, 143.0, op.add)
            tt(A("hf", 0, 6), A("nh", 15, NL, 16), A("ths", 0, 6), op.is_gt)
            cp(A("hw", 0, 6), A("hf", 0, 6))
            ts(A("po"), A("mq"), 0.0, op.is_equal)
            scan(A("nr"), A("tn", C, 2 * C), A("mq"), op.add, op.mult)
            scan(A("mo"), A("po"), A("nr"), op.mult, op.add)
            ts(tw(t + 1, -14, 18), ind(A("mo"), A("bw", 6, 8)), -1.0 / 16, op.mult, 143.0, op.add)
            tt(A("hf", 6, 38), ind(A("mo"), A("bw", 6, 8)), A("ths", 6, 38), op.is_gt)
            cp(A("hw", 6, 24), A("hf", 20, 38))
            pairs = [(tw(t + 1, -22, -16), tw(t + 1, 18, 24), m0), (A("hw", 0, 6), tw(t + 1, 24, 30), m1)]

        def send_list(t=t, rid=rid, pid=pid, pairs=pairs):
            return g.remote_dma_fused([
                RemoteDMATransfer(dst_ids=[DstId(rid=rid, pnc=pid)], dma_engine_mask=m, remote_sem=T.sem["al%d" % t], src=real(a), dst=real(b))
                for (a, b, m) in pairs], local_sem=T.sem.ll)

        j = add({"g": (send_list, OPT["issue"])}, [a for (a, b, m) in pairs], [], kind="r", sem="ll", cnt=2 * half,
                lat=OPT["rem"] + (OPT["rem0"] / 2 if t == 0 else 0.0))
        add({"x": (None, 0.0)}, [], [b for (a, b, m) in pairs], kind="x", sem="al%d" % t, cnt=2 * half, after=[j])
        side = ("qv", "sv") if last else ("qu2", "su2")
        for (a, b, k) in ((0, 160, 0), (160, NS, 2)):
            for p in range(4):
                mov(A("xi", 4 * a + p, 4 * b, 4), ind(A("e", C * p, C * p + C), A("lqw", 30 + a // 16, 30 + b // 16)))
            quant(A("qx", a, b), A("sx", a, b), A("xi", 4 * a, 4 * b))
            mm(bank(k, 0, b - a), A(side[0]), A(side[1]), A("qx", a, b), A("sx", a, b))
            mov(A("yr" if last else "sr", a, b), bank(k, 0, b - a))
            if not last:
                again(a, b, 4 + k // 2)
        for p in range(4):
            mm(bank(4 + p, 0, 128), A("qe", 128 * p, 128 * p + 128), A("se", 128 * p, 128 * p + 128),
               A("lq", 224 * t, 224 * t + 128), A("ls", 512 * t + NS, 512 * t + NS + 128))
            mov(A("xi", 4 * NS + p, 4 * C, 4), bank(4 + p, 0, NL))
        quant(A("qb"), A("sq"), A("xi", 4 * NS, 4 * NS + 512))
        mm(bank(1, 0, 128), A(side[0]), A(side[1]), A("qb"), A("sq"))
        mov(A("yr" if last else "sr", NS, C), bank(1, 0, NL))
        if last:
            dma("y", T.oc[:, 0:4 * NS], real(cast(A("qx", 0, NS), dt.uint8)), [A("qx", 0, NS)], [], 144)
            for k in range(4):
                dma("y", T.osc[4 * k:4 * k + 4, 0:NS], T.sx[32 * k:32 * k + 4, 0:NS], [A("sx", 0, NS)], [])
            dma("y", T.y[:, 0:NS], real(A("yr", 0, NS)), [A("yr", 0, NS)], [], 144)
            dma("y", T.oc[:, 4 * NS:4 * C], real(cast(A("qb", 0, NL), dt.uint8)), [A("qb")], [], 48)
            for k in range(4):
                dma("y" if k < 2 else "s", T.osc[4 * k:4 * k + 4, NS:C], T.sq[32 * k:32 * k + 4, 0:NL], [A("sq")], [])
            dma("s", T.y[:, NS:C], real(A("yr", NS, C)), [A("yr", NS, C)], [], 48)
            dma("y", T.ot[:, 0:NS], T.otr[0:128:16, :], [A("otr")], [])
            dma("y", T.ot[:, NS:C], T.lrow[0:128:16, :], [A("lrow")], [])
        else:
            mm(bank(3, 0, 128), A("qu2"), A("su2"), A("qb"), A("sq"))
            mov(A("st", NS, C), bank(3, 0, NL))
            for (a, b) in ((0, 160), (160, NS)):
                tt(A("d", a, b), ind(A("sr", 0, NS), tw(t + 1, a // 16, b // 16)), A("st", a, b), op.subtract)
                tt(A("un", a, b), ind(A("tie", 0, 2), A("hw", 6 + a // 16, 6 + b // 16)), A("d", a, b), op.is_lt)
            tt(A("d", NS, C), ind(A("sr"), tw(t + 1, 18, 24)), A("st", NS, C), op.subtract)
            tt(A("un", NS, C), ind(A("tie", 0, 2), tw(t + 1, 24, 30)), A("d", NS, C), op.is_lt)

    n = len(ops)
    if "plan" not in OPT:
        OPT["plan"] = plan(ops)
    for i in range(n):
        ops[i]["q"], ops[i]["start"] = OPT["plan"][i][:2]
    order = sorted(range(n), key=lambda k: (ops[k]["start"], k))

    ops.append({"q": "g", "alts": {"g": (None, 0.0)}, "deps": set(j for j in range(n) if ops[j]["kind"] != "c"), "kind": "e"})
    order.append(n)
    pos = {order[k]: k for k in range(n + 1)}
    know, seen, line = {q: 0 for q in queue}, {}, {q: [] for q in queue}
    for i in order:
        o = ops[i]
        o["waits"], o["sig"], o["know"], o["before"] = [], o["kind"] != "c", 0, 0
        if o["q"] == "x":
            continue
        if o["kind"] == "c":
            o["before"] = seen.get(o["q"], 0)
            seen[o["q"]] = o["before"] | 1 << i
        for j in sorted(o["deps"], key=lambda k: -pos[k]):
            if not know[o["q"]] >> j & 1:
                if ops[j]["q"] == o["q"] and ops[j]["kind"] == "c":
                    since = 0.0
                    for x in reversed(line[o["q"]]):
                        if x == j or since >= OPT["since"]:
                            j = x
                            break
                        since += ops[x]["alts"][o["q"]][1]
                o["waits"].append(j)
                ops[j]["sig"] = True
                know[o["q"]] |= ops[j]["know"] | 1 << j | ops[j]["before"]
        o["know"] = know[o["q"]]
        if o["kind"] == "c":
            line[o["q"]].append(i)
    turn, prev, total = {q: 0 for q in POOL}, {}, {}
    for i in order:
        o = ops[i]
        if not o["sig"] or o["kind"] == "e":
            continue
        if o["kind"] == "c":
            o["sem"] = "%s%d" % (o["q"], turn[o["q"]] % POOL[o["q"]])
            turn[o["q"]] += 1
        j = prev.get(o["sem"])
        if j is not None and not o["know"] >> j & 1:
            o["waits"].append(j)
        prev[o["sem"]] = i
        total[o["sem"]] = total.get(o["sem"], 0) + o["cnt"]
        o["val"] = total[o["sem"]]
    for i in order:
        o = ops[i]
        if o["q"] == "x":
            continue
        for j in o["waits"]:
            queue[o["q"]].wait_ge(T.sem[ops[j]["sem"]], ops[j]["val"])
        call = o["alts"][o["q"]][0]
        if call is not None:
            ins = call()
            if o["sig"] and o["kind"] != "r":
                ins.then_inc(T.sem[o["sem"]], o["cnt"])
